import numpy as np
import ml_dtypes


def mxq(x, axis, fmt="e4m3"):
    dtype, down = {"e4m3": (ml_dtypes.float8_e4m3fn, 7), "e5m2": (ml_dtypes.float8_e5m2, 14)}[fmt]
    v = np.moveaxis(np.asarray(x, np.float32).astype(ml_dtypes.bfloat16).astype(np.float64), axis, -1)
    blocks = v.reshape(v.shape[:-1] + (-1, 32))
    amax = np.abs(blocks).max(-1, keepdims=True)
    byte = np.maximum(np.where(amax > 0, np.frexp(amax)[1] - 1 + 127, 0) - down, 1)
    scale = np.exp2(byte - 127.0)
    codes = (blocks / scale).astype(np.float32).astype(dtype).astype(np.float64)
    return np.moveaxis((codes * scale).reshape(v.shape), -1, axis)


WIDE = False


def mx_kscale(k):
    if not WIDE:
        return np.ones(k)
    levels = np.array([10, -10, 5, -5, 0])
    if k % 512:
        return np.exp2(np.random.permutation(np.resize(levels, k // 32))).repeat(32)
    a = np.empty((k // 512, 16))
    for p in range(k // 512):
        a[p, :8] = np.random.permutation(np.resize(levels, 8))
        for g in range(8):
            far = levels[np.abs(levels - a[p, g]) >= 10]
            a[p, g + 8] = far[np.random.randint(len(far))]
    return np.exp2(a.ravel()).repeat(32)


def f64(x):
    return np.asarray(x).astype(np.float64)


def striped(idx):
    return np.tile(idx.reshape(-1, 16).T, (8, 1)).astype(np.uint16)


def unstriped(offs):
    return offs[:16].T.reshape(-1).astype(np.int64)


E2M1 = np.array([0.0, 0.5, 1.0, 1.5, 2.0, 3.0, 4.0, 6.0, -0.0, -0.5, -1.0, -1.5, -2.0, -3.0, -4.0, -6.0])


def pack_weight(w, fmt):
    k, n = w.shape
    w = f64(np.asarray(w, np.float32).astype(ml_dtypes.bfloat16)).reshape(k // 32, 32, n)
    amax = np.abs(w).max(1)
    if fmt == "e4m3":
        byte = np.frexp(amax)[1] - 1 + 127 - 7
    else:
        mant, ex = np.frexp(amax / 6.0)
        byte = np.where(mant > 0.5, ex, ex - 1) + 127
    byte = np.clip(np.where(amax > 0, byte, 1), 1, 254)
    scaled = (w * np.exp2(127.0 - byte)[:, None, :]).reshape(k, n).astype(np.float32)
    by_word = np.ascontiguousarray(scaled.reshape(k // 512, 128, 4, n).transpose(0, 1, 3, 2))
    if fmt == "e4m3":
        words = by_word.astype(ml_dtypes.float8_e4m3fn).view(np.uint8)
    else:
        c = by_word.astype(ml_dtypes.float4_e2m1fn).view(np.uint8) & 0xF
        words = (c[..., 0::2] | (c[..., 1::2] << 4)).reshape(k // 512, 128, 2 * n)
    return np.ascontiguousarray(words), np.ascontiguousarray(byte.astype(np.uint8).reshape(k // 512, 16, n))


def unpack_weight(words, scales, fmt):
    g, _, n = scales.shape
    words = np.ascontiguousarray(words).reshape(g, 128, n, -1)
    if fmt == "e4m3":
        vals = words.view(ml_dtypes.float8_e4m3fn).astype(np.float64)
    else:
        nib = np.empty((g, 128, n, 4), np.uint8)
        nib[..., 0::2] = words & 0xF
        nib[..., 1::2] = words >> 4
        vals = E2M1[nib]
    vals = vals * np.repeat(np.exp2(scales.astype(np.float64) - 127.0), 8, axis=1)[..., None]
    return vals.transpose(0, 1, 3, 2).reshape(g * 512, n)


def gelu(v):
    return 0.5 * v * (1.0 + np.tanh(np.sqrt(2.0 / np.pi) * (v + 0.044715 * v**3)))


K, M, H, N, T, S, T2, P = 1024, 512, 1024, 512, 2048, 1024, 2048, 1024

def setup_inputs():
    n = np.random.standard_normal
    s = mx_kscale(K)[:, None]
    d = mx_kscale(M)[:, None]
    u = mx_kscale(H)[:, None]
    tab_words, tab_scales = pack_weight(n((K, T)) * s, "e4m3")
    w1_words, w1_scales = pack_weight(n((K, M)) / np.sqrt(K) / s, "e2m1")
    w3_words, w3_scales = pack_weight(n((H, N)) / np.sqrt(H) / u, "e4m3")
    return {
        "tab_words": tab_words, "tab_scales": tab_scales,
        "offs": striped(np.random.permutation(T)[:S]),
        "w1_words": w1_words, "w1_scales": w1_scales,
        "b1": (0.5 * n(M)).astype(np.float32),
        "gain": (np.exp(0.3 * n(M)) * d[:, 0]).astype(np.float32),
        "w2": (1.5 * n((M, H)) / np.sqrt(M) / d * u.T).astype(np.float32),
        "wgs": np.exp(0.3 * n((128, S))).astype(np.float32),
        "offs2": striped(np.random.permutation(T2)[:S]),
        "offs3": striped(np.random.permutation(T2)[:P]),
        "cap": ((0.3 + n((H, P))) * u).astype(np.float32),
        "w3_words": w3_words, "w3_scales": w3_scales,
    }

def reference(tab_words, tab_scales, offs, w1_words, w1_scales, b1, gain, w2, wgs, offs2, offs3, cap, w3_words, w3_scales):
    v = unpack_weight(tab_words, tab_scales, "e4m3")[:, unstriped(offs)]
    w1 = unpack_weight(w1_words, w1_scales, "e2m1")
    w3 = unpack_weight(w3_words, w3_scales, "e4m3")
    e = np.tanh((w1.T @ v) + f64(b1)[:, None]) * f64(gain)[:, None]
    h = mxq(f64(w2), 0, "e4m3").T @ mxq(e, 0, "e4m3")
    page = np.zeros((H, T2))
    page[:, unstriped(offs2)] = np.tile(f64(wgs), (H // 128, 1)) * h
    x = page[:, unstriped(offs3)]
    z = np.minimum(x, f64(cap))
    return w3.T @ mxq(z, 0, "e4m3")

@@ -1,0 +1,307 @@
+from contextlib import ExitStack
+
+import concourse.mybir as mybir
+
+K, M, H, N, T, S, T2, PICKS = 1024, 512, 1024, 512, 2048, 1024, 2048, 1024
+FLOPS = 2 * (K * M * S + M * H * S + H * N * PICKS)
+
+F32 = mybir.dt.float32
+BF16 = mybir.dt.bfloat16
+I32 = mybir.dt.int32
+U32 = mybir.dt.uint32
+U16 = mybir.dt.uint16
+U8 = mybir.dt.uint8
+FP8X4 = mybir.dt.float8_e4m3fn_x4
+FP4X4 = mybir.dt.float4_e2m1fn_x4
+ACT = mybir.ActivationFunctionType
+ALU = mybir.AluOpType
+
+P = 128
+PACK = 4
+PIECE = 256
+PIECES = S // PIECE
+LIST_COLS = PIECE // 16
+
+
+def tile_list_spill_slot_advisor_kernel(
+    tc, tab_words, tab_scales, offs, w1_words, w1_scales, b1, gain, w2, wgs, offs2, offs3, cap, w3_words, w3_scales, out
+):
+    nc = tc.nc
+    with ExitStack() as ctx:
+        lists = ctx.enter_context(tc.tile_pool(name="lists", bufs=1))
+        sb = ctx.enter_context(tc.tile_pool(name="sb", bufs=1))
+        ring = ctx.enter_context(tc.tile_pool(name="ring", bufs=2))
+        psum = ctx.enter_context(tc.psum_pool(name="psum", bufs=4))
+
+        def held(name, shape, dtype, tag=None):
+            return sb.tile(shape, dtype, name=name, tag=tag or name, align_bytes=64)
+
+        def ringed(name, shape, dtype):
+            return ring.tile(shape, dtype, name=name, tag=name, align_bytes=64)
+
+        def cols(j):
+            return slice(j * PIECE, (j + 1) * PIECE)
+
+        def entries(j):
+            return slice(j * LIST_COLS, (j + 1) * LIST_COLS)
+
+        def interleave(engine_copy, dst, src):
+            engine_copy(
+                dst.rearrange("p (c i) t -> p c t i", i=4),
+                src.rearrange("p t (c i) -> p c t i", i=4),
+            )
+
+        tab_plane = held("tab_plane", [P, T], U8)
+        w1_plane_raw = held("w1_plane_raw", [P, 2, M], U8)
+        v_plane = [held(f"v_plane{a}", [P, S], U8) for a in range(2)]
+        nc.vector.memset(w1_plane_raw[:].rearrange("p a c -> p (a c)").bitcast(I32), 0)
+        for q in range(4):
+            nc.vector.memset(tab_plane[32 * q : 32 * q + 24, :].bitcast(I32), 0)
+        for a in range(2):
+            nc.vector.memset(v_plane[a][96:128, :].bitcast(I32), 0)
+
+        idx = lists.tile([P, S // 16], U16, name="idx")
+        idx2 = lists.tile([P, S // 16], U16, name="idx2")
+        idx3 = lists.tile([P, PICKS // 16], U16, name="idx3")
+        b1_sb = held("b1_sb", [P, PACK], F32)
+        gain_sb = held("gain_sb", [P, PACK], F32)
+        nc.sync.dma_start(idx[:], offs)
+        for q in range(4):
+            nc.sync.dma_start(
+                tab_plane[32 * q + 24 : 32 * q + 32, :].bitcast(I32), tab_scales[:, 4 * q : 4 * q + 4, :].bitcast(I32)
+            )
+        w1_raw = held("w1_raw", [P, 2, M // 2], I32)
+        nc.sync.dma_start(w1_raw[:], w1_words.rearrange("a p b -> p a b").bitcast(I32))
+        tab = [held(f"tab{a}", [P, T], I32) for a in range(2)]
+        for a in range(2):
+            nc.sync.dma_start(tab[a][:], tab_words[a].rearrange("p t i -> p (t i)").bitcast(I32))
+        nc.gpsimd.dma_start(b1_sb[:], b1.rearrange("(p t) -> p t", t=PACK))
+        nc.gpsimd.dma_start(gain_sb[:], gain.rearrange("(p t) -> p t", t=PACK))
+        for q in range(4):
+            nc.scalar.dma_start(
+                w1_plane_raw[32 * q : 32 * q + 4, :, :].bitcast(I32),
+                w1_scales[:, 4 * q : 4 * q + 4, :].rearrange("a r c -> r a c").bitcast(I32),
+            )
+        nc.sync.dma_start(idx2[:], offs2)
+        nc.sync.dma_start(idx3[:], offs3)
+        pages = [held(f"page{t}", [P, T2], F32) for t in range(PACK)]
+        for t in range(PACK):
+            for c0 in range(0, T2, 512):
+                nc.gpsimd.memset(pages[t][:, c0 : c0 + 512], 0.0)
+
+        w1_codes = held("w1_codes", [P, 2, M // 2], I32)
+        nc.vector.tensor_copy(
+            w1_codes[:].bitcast(U16).rearrange("p a (t m) -> p a m t", t=PACK),
+            w1_raw[:].bitcast(U16).rearrange("p a (m t) -> p a m t", t=PACK),
+        )
+        w2_rows = w2.rearrange("(p j) r -> p j r", j=PACK)
+        w2_raw = [held("w2_raw0", [P, PACK, 512], F32, tag="w1_raw")]
+        nc.sync.dma_start(w2_raw[0][:], w2_rows[:, :, 0:512])
+
+        v_codes = [held(f"v_codes{a}", [P, S], U32) for a in range(2)]
+
+        def gather_scales(first, last):
+            span = slice(first * PIECE, last * PIECE)
+            picked_scales = held("picked_scales", [P, (last - first) * PIECE], U8)
+            nc.vector.tensor_copy(
+                picked_scales[:], tab_plane[:].indirect(idx[:, first * LIST_COLS : last * LIST_COLS])
+            )
+            for a in range(2):
+                shift = 24 + 4 * a
+                nc.scalar.dma_start(
+                    v_plane[a][0 : P - shift, span].bitcast(I32), picked_scales[shift:P, :].bitcast(I32)
+                )
+
+        def gather_words(first, last):
+            for a in range(2):
+                nc.vector.tensor_copy(
+                    v_codes[a][:, first * PIECE : last * PIECE],
+                    tab[a][:].bitcast(U32).indirect(idx[:, first * LIST_COLS : last * LIST_COLS]),
+                )
+
+        gather_scales(0, 2)
+        w1_plane = held("w1_plane", [P, 2, M], U8)
+        nc.vector.tensor_copy(
+            w1_plane[:].rearrange("p a (t m) -> p a m t", t=PACK),
+            w1_plane_raw[:].rearrange("p a (m t) -> p a m t", t=PACK),
+        )
+        gather_words(0, 1)
+        gather_words(1, 2)
+        gather_scales(2, 4)
+        gather_words(2, 4)
+
+        wgs_sb = held("wgs_sb", [P, PACK, S], F32, tag="w1_plane_raw")
+        wgs_rows = wgs.rearrange("(p t) s -> p t s", t=PACK)
+        for span in (slice(0, PIECE), slice(PIECE, S)):
+            for q in range(4):
+                nc.sync.dma_start(wgs_sb[32 * q : 32 * q + 32, :, span], wgs_rows[:, :, span])
+        w2_raw.append(held("w2_raw1", [P, PACK, 512], F32, tag="tab1"))
+        nc.sync.dma_start(w2_raw[1][:], w2_rows[:, :, 512:1024])
+        cap_rows = cap.rearrange("(a p t) m -> a p t m", a=2, t=PACK)
+        cap0 = held("cap0", [P, PACK, PICKS], F32, tag="tab0")
+        nc.sync.dma_start(cap0[:], cap_rows[0])
+
+        w2_codes = [held(f"w2_codes{a}", [P, 512], U32) for a in range(2)]
+        w2_plane = [held(f"w2_plane{a}", [P, 512], U8) for a in range(2)]
+
+        def round_w2(a, engine_copy, tag):
+            grouped = held(f"w2_grouped{a}", [P, PACK, 128, PACK], BF16, tag=tag)
+            engine_copy(
+                grouped[:].rearrange("p t m j -> p m j t"), w2_raw[a][:].rearrange("p j (m t) -> p m j t", t=PACK)
+            )
+            return grouped
+
+        def quantize(codes, plane, grouped):
+            nc.vector.quantize_mx(out=codes.bitcast(FP8X4), scales=plane, in_=grouped)
+
+        def quantize_w2(a, grouped):
+            quantize(w2_codes[a][:], w2_plane[a][:], grouped[:].rearrange("p t m j -> p (t m j)"))
+
+        quantize_w2(0, round_w2(0, nc.vector.tensor_copy, "w2_grouped0"))
+
+        w3_codes = held("w3_codes", [P, 2, N], I32, tag="w2_grouped0")
+        nc.sync.dma_start(w3_codes[:], w3_words.rearrange("a p c i -> p a (c i)").bitcast(I32))
+
+        e_codes = held("e_codes", [P, S], U32)
+        e_plane = held("e_plane", [P, S], U8)
+
+        def features(j):
+            th = ringed("th", [P, PACK, PIECE], F32)
+            for pair in range(2):
+                bank = psum.tile([P, 2, PIECE], F32, name="bank_a", tag="bank_a")
+                for u in range(2):
+                    t = 2 * pair + u
+                    for half in range(2):
+                        c0 = j * PIECE + half * 128
+                        for a in range(2):
+                            nc.tensor.matmul_mx(
+                                out=bank[:, u, half * 128 : half * 128 + 128],
+                                lhsT=w1_codes[:, a, 64 * t : 64 * t + 64].bitcast(FP4X4),
+                                lhsT_scale=w1_plane[:, a, 128 * t : 128 * t + 128],
+                                rhs=v_codes[a][:, c0 : c0 + 128].bitcast(FP8X4),
+                                rhs_scale=v_plane[a][:, c0 : c0 + 128],
+                                start=(a == 0),
+                                stop=(a == 1),
+                            )
+                for u in range(2):
+                    t = 2 * pair + u
+                    nc.scalar.activation(th[:, t, :], bank[:, u, :], ACT.Tanh, bias=b1_sb[:, t : t + 1])
+            e_rows = held(f"e_rows{j}", [P, PACK, PIECE], BF16)
+            for t in range(PACK):
+                nc.scalar.activation(e_rows[:, t, :], th[:, t, :], ACT.Copy, scale=gain_sb[:, t : t + 1])
+            if j == PIECES - 1:
+                e_grouped = held("e_grouped_last", [P, PIECE, PACK], BF16, tag="late")
+            else:
+                e_grouped = ringed("e_grouped", [P, PIECE, PACK], BF16)
+            interleave(nc.scalar.copy, e_grouped[:], e_rows[:])
+            return e_grouped
+
+        def quantize_e(j, e_grouped):
+            quantize(e_codes[:, cols(j)], e_plane[:, cols(j)], e_grouped[:].rearrange("p n t -> p (n t)"))
+
+        def costs(a, t, span, dst):
+            width = span.stop - span.start
+            bank = psum.tile([P, 512], F32, name="bank_b", tag="bank_b")
+            nc.tensor.matmul_mx(
+                out=bank[:, 0:width],
+                lhsT=w2_codes[a][:, 128 * t : 128 * t + 128].bitcast(FP8X4),
+                lhsT_scale=w2_plane[a][:, 128 * t : 128 * t + 128],
+                rhs=e_codes[:, span].bitcast(FP8X4),
+                rhs_scale=e_plane[:, span],
+                start=True,
+                stop=True,
+            )
+            nc.scalar.copy(dst, bank[:, 0:width])
+
+        def put(t, offsets, values, span):
+            nc.vector.tensor_tensor(pages[t][:].indirect(offsets), values, wgs_sb[:, t, span], ALU.mult)
+
+        h0 = [held(f"h0{t}", [P, S], F32) for t in range(PACK - 1)]
+        quantize_e(0, features(0))
+        for j in range(PIECES):
+            for t in range(PACK - 1):
+                costs(0, t, cols(j), h0[t][:, cols(j)])
+            for t in range(PACK - 1):
+                put(t, idx2[:, entries(j)], h0[t][:, cols(j)], cols(j))
+            if j + 1 < PIECES:
+                quantize_e(j + 1, features(j + 1))
+                h03 = held(f"h03_{j}", [P, PIECE], F32, tag=f"e_rows{j + 1}")
+            else:
+                quantize_w2(1, round_w2(1, nc.scalar.copy, "late"))
+                h03 = held(f"h03_{j}", [P, PIECE], F32)
+            costs(0, PACK - 1, cols(j), h03[:])
+            put(PACK - 1, idx2[:, entries(j)], h03[:], cols(j))
+
+        h1 = [held(f"h1{t}", [P, S], F32) for t in range(PACK)]
+        for t in range(PACK):
+            for half in range(2):
+                span = slice(512 * half, 512 * half + 512)
+                costs(1, t, span, h1[t][:, span])
+
+        w3_plane = held("w3_plane", [P, 2, N], U8, tag="e_rows0")
+        nc.vector.memset(w3_plane[:].rearrange("p a c -> p (a c)").bitcast(I32), 0)
+        for q in range(4):
+            nc.sync.dma_start(
+                w3_plane[32 * q : 32 * q + 4, :, :].bitcast(I32),
+                w3_scales[:, 4 * q : 4 * q + 4, :].rearrange("a r c -> r a c").bitcast(I32),
+            )
+
+        x = held("x", [P, PACK, PICKS], F32)
+        z_rows0 = held("z_rows0", [P, PACK, PICKS], BF16, tag="w1_raw")
+        for t in range(PACK):
+            nc.vector.tensor_copy(x[:, t, :], pages[t][:].indirect(idx3[:]))
+        for t in range(PACK):
+            nc.vector.tensor_tensor(z_rows0[:, t, :], x[:, t, :], cap0[:, t, :], ALU.min)
+        z_grouped0 = held("z_grouped0", [P, PICKS, PACK], BF16, tag="tab1")
+        interleave(nc.scalar.copy, z_grouped0[:], z_rows0[:])
+        cap1 = held("cap1", [P, PACK, PICKS], F32, tag="tab0")
+        nc.sync.dma_start(cap1[:], cap_rows[1])
+
+        z_plane = [held(f"z_plane{a}", [P, PICKS], U8) for a in range(2)]
+        for t in range(PACK - 1):
+            put(t, idx2[:], h1[t][:], slice(0, S))
+        z_codes0 = held("z_codes0", [P, PICKS], U32, tag="h12")
+        quantize(z_codes0[:], z_plane[0][:], z_grouped0[:].rearrange("p n t -> p (n t)"))
+        put(PACK - 1, idx2[:], h1[PACK - 1][:], slice(0, S))
+        for t in range(PACK - 1):
+            nc.vector.tensor_copy(x[:, t, :], pages[t][:].indirect(idx3[:]))
+        z_codes = [z_codes0, held("z_codes1", [P, PICKS], U32, tag="h00")]
+
+        out_rows = out.rearrange("(c p) m -> p c m", p=P)
+        staging_tags = ["h01", "h02", "h10", "h11"]
+
+        def limit(j):
+            nc.vector.tensor_copy(x[:, PACK - 1, cols(j)], pages[PACK - 1][:].indirect(idx3[:, entries(j)]))
+            z_rows = ringed("z_rows", [P, PACK, PIECE], BF16)
+            nc.vector.tensor_tensor(z_rows[:], x[:, :, cols(j)], cap1[:, :, cols(j)], ALU.min)
+            z_grouped = held(f"z_grouped_p{j}", [P, PIECE, PACK], BF16)
+            interleave(nc.vector.tensor_copy if j == PIECES - 1 else nc.scalar.copy, z_grouped[:], z_rows[:])
+            return z_grouped
+
+        def scores(j, z_grouped):
+            quantize(z_codes[1][:, cols(j)], z_plane[1][:, cols(j)], z_grouped[:].rearrange("p n t -> p (n t)"))
+            tag = "bank_a" if j % 2 == 0 else "bank_b"
+            banks = [psum.tile([P, 512], F32, name=f"acc{c}", tag=tag) for c in range(4)]
+            for a in range(2):
+                for c in range(4):
+                    nc.tensor.matmul_mx(
+                        out=banks[c][:, 0:PIECE],
+                        lhsT=w3_codes[:, a, 128 * c : 128 * c + 128].bitcast(FP8X4),
+                        lhsT_scale=w3_plane[:, a, 128 * c : 128 * c + 128],
+                        rhs=z_codes[a][:, cols(j)].bitcast(FP8X4),
+                        rhs_scale=z_plane[a][:, cols(j)],
+                        start=(a == 0),
+                        stop=(a == 1),
+                    )
+            staged = held(f"staged{j}", [P, 4, PIECE], F32, tag=staging_tags[j])
+            for c in range(4):
+                copy = nc.vector.tensor_copy if (j == PIECES - 1 and c % 2 == 1) else nc.scalar.copy
+                copy(staged[:, c, :], banks[c][:, 0:PIECE])
+            for pair in range(2):
+                nc.sync.dma_start(out_rows[:, 2 * pair : 2 * pair + 2, cols(j)], staged[:, 2 * pair : 2 * pair + 2, :])
+
+        grouped = limit(0)
+        for j in range(PIECES):
+            ahead = limit(j + 1) if j + 1 < PIECES else None
+            scores(j, grouped)
+            grouped = ahead

@@ -54,11 +54,15 @@ def tile_list_spill_slot_advisor_kernel(
         tab_plane = held("tab_plane", [P, T], U8)
         w1_plane_raw = held("w1_plane_raw", [P, 2, M], U8)
         v_plane = [held(f"v_plane{a}", [P, S], U8) for a in range(2)]
-        nc.vector.memset(w1_plane_raw[:].rearrange("p a c -> p (a c)").bitcast(I32), 0)
+        nc.gpsimd.memset(w1_plane_raw[:].rearrange("p a c -> p (a c)").bitcast(I32), 0)
         for q in range(4):
             nc.vector.memset(tab_plane[32 * q : 32 * q + 24, :].bitcast(I32), 0)
         for a in range(2):
             nc.vector.memset(v_plane[a][96:128, :].bitcast(I32), 0)
+
+        warm = held("warm", [P, 8], F32)
+        nc.vector.memset(warm[:, 0:1], 0.0)
+        nc.scalar.activation(warm[:, 1:2], warm[:, 0:1], ACT.Tanh)
 
         idx = lists.tile([P, S // 16], U16, name="idx")
         idx2 = lists.tile([P, S // 16], U16, name="idx2")
@@ -72,13 +76,16 @@ def tile_list_spill_slot_advisor_kernel(
             )
         w1_raw = held("w1_raw", [P, 2, M // 2], I32)
         nc.sync.dma_start(w1_raw[:], w1_words.rearrange("a p b -> p a b").bitcast(I32))
+        w2_rows = w2.rearrange("(p j) r -> p j r", j=PACK)
+        w2_raw = [held("w2_raw0", [P, PACK, 512], F32)]
+        nc.sync.dma_start(w2_raw[0][:], w2_rows[:, :, 0:512])
         tab = [held(f"tab{a}", [P, T], I32) for a in range(2)]
         for a in range(2):
             nc.sync.dma_start(tab[a][:], tab_words[a].rearrange("p t i -> p (t i)").bitcast(I32))
-        nc.gpsimd.dma_start(b1_sb[:], b1.rearrange("(p t) -> p t", t=PACK))
-        nc.gpsimd.dma_start(gain_sb[:], gain.rearrange("(p t) -> p t", t=PACK))
+        nc.sync.dma_start(b1_sb[:], b1.rearrange("(p t) -> p t", t=PACK))
+        nc.sync.dma_start(gain_sb[:], gain.rearrange("(p t) -> p t", t=PACK))
         for q in range(4):
-            nc.scalar.dma_start(
+            nc.gpsimd.dma_start(
                 w1_plane_raw[32 * q : 32 * q + 4, :, :].bitcast(I32),
                 w1_scales[:, 4 * q : 4 * q + 4, :].rearrange("a r c -> r a c").bitcast(I32),
             )
@@ -94,52 +101,37 @@ def tile_list_spill_slot_advisor_kernel(
             w1_codes[:].bitcast(U16).rearrange("p a (t m) -> p a m t", t=PACK),
             w1_raw[:].bitcast(U16).rearrange("p a (m t) -> p a m t", t=PACK),
         )
-        w2_rows = w2.rearrange("(p j) r -> p j r", j=PACK)
-        w2_raw = [held("w2_raw0", [P, PACK, 512], F32, tag="w1_raw")]
-        nc.sync.dma_start(w2_raw[0][:], w2_rows[:, :, 0:512])
 
-        v_codes = [held(f"v_codes{a}", [P, S], U32) for a in range(2)]
-
-        def gather_scales(first, last):
-            span = slice(first * PIECE, last * PIECE)
-            picked_scales = held("picked_scales", [P, (last - first) * PIECE], U8)
-            nc.vector.tensor_copy(
-                picked_scales[:], tab_plane[:].indirect(idx[:, first * LIST_COLS : last * LIST_COLS])
-            )
-            for a in range(2):
-                shift = 24 + 4 * a
-                nc.scalar.dma_start(
-                    v_plane[a][0 : P - shift, span].bitcast(I32), picked_scales[shift:P, :].bitcast(I32)
-                )
-
-        def gather_words(first, last):
-            for a in range(2):
-                nc.vector.tensor_copy(
-                    v_codes[a][:, first * PIECE : last * PIECE],
-                    tab[a][:].bitcast(U32).indirect(idx[:, first * LIST_COLS : last * LIST_COLS]),
-                )
-
-        gather_scales(0, 2)
+        picked_scales = held("picked_scales", [P, S], U8)
+        nc.vector.tensor_copy(picked_scales[:], tab_plane[:].indirect(idx[:]))
+        for a in range(2):
+            shift = 24 + 4 * a
+            nc.scalar.dma_start(v_plane[a][0 : P - shift, :].bitcast(I32), picked_scales[shift:P, :].bitcast(I32))
         w1_plane = held("w1_plane", [P, 2, M], U8)
         nc.vector.tensor_copy(
             w1_plane[:].rearrange("p a (t m) -> p a m t", t=PACK),
             w1_plane_raw[:].rearrange("p a (m t) -> p a m t", t=PACK),
         )
-        gather_words(0, 1)
-        gather_words(1, 2)
-        gather_scales(2, 4)
-        gather_words(2, 4)
+        v_codes0 = held("v_codes0", [P, S], U32)
+        nc.vector.tensor_copy(v_codes0[:], tab[0][:].bitcast(U32).indirect(idx[:]))
+        v_codes1_first = held("v_codes1_first", [P, PIECE], U32)
+        nc.vector.tensor_copy(v_codes1_first[:], tab[1][:].bitcast(U32).indirect(idx[:, entries(0)]))
+        v_codes1_rest = held("v_codes1_rest", [P, S - PIECE], U32, tag="w1_plane_raw")
+        nc.vector.tensor_copy(v_codes1_rest[:], tab[1][:].bitcast(U32).indirect(idx[:, LIST_COLS : S // 16]))
 
-        wgs_sb = held("wgs_sb", [P, PACK, S], F32, tag="w1_plane_raw")
+        def v_codes(a, c0):
+            if a == 0:
+                return v_codes0[:, c0 : c0 + 128]
+            if c0 < PIECE:
+                return v_codes1_first[:, c0 : c0 + 128]
+            return v_codes1_rest[:, c0 - PIECE : c0 - PIECE + 128]
+
+        wgs_sb = held("wgs_sb", [P, PACK, S], F32, tag="picked_scales")
         wgs_rows = wgs.rearrange("(p t) s -> p t s", t=PACK)
         for span in (slice(0, PIECE), slice(PIECE, S)):
             for q in range(4):
                 nc.sync.dma_start(wgs_sb[32 * q : 32 * q + 32, :, span], wgs_rows[:, :, span])
-        w2_raw.append(held("w2_raw1", [P, PACK, 512], F32, tag="tab1"))
-        nc.sync.dma_start(w2_raw[1][:], w2_rows[:, :, 512:1024])
         cap_rows = cap.rearrange("(a p t) m -> a p t m", a=2, t=PACK)
-        cap0 = held("cap0", [P, PACK, PICKS], F32, tag="tab0")
-        nc.sync.dma_start(cap0[:], cap_rows[0])
 
         w2_codes = [held(f"w2_codes{a}", [P, 512], U32) for a in range(2)]
         w2_plane = [held(f"w2_plane{a}", [P, 512], U8) for a in range(2)]
@@ -157,11 +149,6 @@ def tile_list_spill_slot_advisor_kernel(
         def quantize_w2(a, grouped):
             quantize(w2_codes[a][:], w2_plane[a][:], grouped[:].rearrange("p t m j -> p (t m j)"))
 
-        quantize_w2(0, round_w2(0, nc.vector.tensor_copy, "w2_grouped0"))
-
-        w3_codes = held("w3_codes", [P, 2, N], I32, tag="w2_grouped0")
-        nc.sync.dma_start(w3_codes[:], w3_words.rearrange("a p c i -> p a (c i)").bitcast(I32))
-
         e_codes = held("e_codes", [P, S], U32)
         e_plane = held("e_plane", [P, S], U8)
 
@@ -178,7 +165,7 @@ def tile_list_spill_slot_advisor_kernel(
                                 out=bank[:, u, half * 128 : half * 128 + 128],
                                 lhsT=w1_codes[:, a, 64 * t : 64 * t + 64].bitcast(FP4X4),
                                 lhsT_scale=w1_plane[:, a, 128 * t : 128 * t + 128],
-                                rhs=v_codes[a][:, c0 : c0 + 128].bitcast(FP8X4),
+                                rhs=v_codes(a, c0).bitcast(FP8X4),
                                 rhs_scale=v_plane[a][:, c0 : c0 + 128],
                                 start=(a == 0),
                                 stop=(a == 1),
@@ -188,55 +175,63 @@ def tile_list_spill_slot_advisor_kernel(
                     nc.scalar.activation(th[:, t, :], bank[:, u, :], ACT.Tanh, bias=b1_sb[:, t : t + 1])
             e_rows = held(f"e_rows{j}", [P, PACK, PIECE], BF16)
             for t in range(PACK):
-                nc.scalar.activation(e_rows[:, t, :], th[:, t, :], ACT.Copy, scale=gain_sb[:, t : t + 1])
-            if j == PIECES - 1:
-                e_grouped = held("e_grouped_last", [P, PIECE, PACK], BF16, tag="late")
-            else:
-                e_grouped = ringed("e_grouped", [P, PIECE, PACK], BF16)
-            interleave(nc.scalar.copy, e_grouped[:], e_rows[:])
+                if j == 0:
+                    nc.vector.tensor_scalar(e_rows[:, t, :], th[:, t, :], gain_sb[:, t : t + 1], None, ALU.mult)
+                else:
+                    nc.scalar.activation(e_rows[:, t, :], th[:, t, :], ACT.Copy, scale=gain_sb[:, t : t + 1])
+            e_grouped = ringed("e_grouped", [P, PIECE, PACK], BF16)
+            interleave(nc.vector.tensor_copy if j == 0 else nc.scalar.copy, e_grouped[:], e_rows[:])
             return e_grouped
 
         def quantize_e(j, e_grouped):
             quantize(e_codes[:, cols(j)], e_plane[:, cols(j)], e_grouped[:].rearrange("p n t -> p (n t)"))
 
-        def costs(a, t, span, dst):
+        def costs(a, slots, span, dst):
             width = span.stop - span.start
-            bank = psum.tile([P, 512], F32, name="bank_b", tag="bank_b")
-            nc.tensor.matmul_mx(
-                out=bank[:, 0:width],
-                lhsT=w2_codes[a][:, 128 * t : 128 * t + 128].bitcast(FP8X4),
-                lhsT_scale=w2_plane[a][:, 128 * t : 128 * t + 128],
-                rhs=e_codes[:, span].bitcast(FP8X4),
-                rhs_scale=e_plane[:, span],
-                start=True,
-                stop=True,
-            )
-            nc.scalar.copy(dst, bank[:, 0:width])
+            bank = psum.tile([P, len(slots), width], F32, name="bank_b", tag="bank_b")
+            for u, t in enumerate(slots):
+                nc.tensor.matmul_mx(
+                    out=bank[:, u, :],
+                    lhsT=w2_codes[a][:, 128 * t : 128 * t + 128].bitcast(FP8X4),
+                    lhsT_scale=w2_plane[a][:, 128 * t : 128 * t + 128],
+                    rhs=e_codes[:, span].bitcast(FP8X4),
+                    rhs_scale=e_plane[:, span],
+                    start=True,
+                    stop=True,
+                )
+            nc.scalar.copy(dst, bank[:])
 
         def put(t, offsets, values, span):
             nc.vector.tensor_tensor(pages[t][:].indirect(offsets), values, wgs_sb[:, t, span], ALU.mult)
 
-        h0 = [held(f"h0{t}", [P, S], F32) for t in range(PACK - 1)]
+        quantize_w2(0, round_w2(0, nc.scalar.copy, "w2_grouped0"))
         quantize_e(0, features(0))
+        w2_raw.append(held("w2_raw1", [P, PACK, 512], F32, tag="v_codes1_first"))
+        nc.sync.dma_start(w2_raw[1][:], w2_rows[:, :, 512:1024])
         for j in range(PIECES):
+            h0 = held(f"h0_{j}", [P, PACK - 1, PIECE], F32)
+            costs(0, (0,), cols(j), h0[:, 0:1, :])
+            costs(0, (1, 2), cols(j), h0[:, 1:3, :])
             for t in range(PACK - 1):
-                costs(0, t, cols(j), h0[t][:, cols(j)])
-            for t in range(PACK - 1):
-                put(t, idx2[:, entries(j)], h0[t][:, cols(j)], cols(j))
+                put(t, idx2[:, entries(j)], h0[:, t, :], cols(j))
             if j + 1 < PIECES:
                 quantize_e(j + 1, features(j + 1))
-                h03 = held(f"h03_{j}", [P, PIECE], F32, tag=f"e_rows{j + 1}")
+                h03 = held(f"h03_{j}", [P, 1, PIECE], F32, tag=f"e_rows{j + 1}")
             else:
-                quantize_w2(1, round_w2(1, nc.scalar.copy, "late"))
-                h03 = held(f"h03_{j}", [P, PIECE], F32)
-            costs(0, PACK - 1, cols(j), h03[:])
-            put(PACK - 1, idx2[:, entries(j)], h03[:], cols(j))
+                h03 = held(f"h03_{j}", [P, 1, PIECE], F32)
+            costs(0, (PACK - 1,), cols(j), h03[:])
+            put(PACK - 1, idx2[:, entries(j)], h03[:, 0, :], cols(j))
+        cap0 = held("cap0", [P, PACK, PICKS], F32, tag="v_codes0")
+        nc.sync.dma_start(cap0[:], cap_rows[0])
+        w3_codes = held("w3_codes", [P, 2, N], I32, tag="v_plane0")
+        nc.sync.dma_start(w3_codes[:], w3_words.rearrange("a p c i -> p a (c i)").bitcast(I32))
+        quantize_w2(1, round_w2(1, nc.scalar.copy, f"e_rows{PIECES - 1}"))
 
-        h1 = [held(f"h1{t}", [P, S], F32) for t in range(PACK)]
+        h1 = [held(f"h1{t}", [P, 1, S], F32) for t in range(PACK)]
         for t in range(PACK):
             for half in range(2):
                 span = slice(512 * half, 512 * half + 512)
-                costs(1, t, span, h1[t][:, span])
+                costs(1, (t,), span, h1[t][:, :, span])
 
         w3_plane = held("w3_plane", [P, 2, N], U8, tag="e_rows0")
         nc.vector.memset(w3_plane[:].rearrange("p a c -> p (a c)").bitcast(I32), 0)
@@ -247,32 +242,32 @@ def tile_list_spill_slot_advisor_kernel(
             )
 
         x = held("x", [P, PACK, PICKS], F32)
-        z_rows0 = held("z_rows0", [P, PACK, PICKS], BF16, tag="w1_raw")
+        z_rows0 = held("z_rows0", [P, PACK, PICKS], BF16, tag="w2_raw0")
         for t in range(PACK):
             nc.vector.tensor_copy(x[:, t, :], pages[t][:].indirect(idx3[:]))
         for t in range(PACK):
             nc.vector.tensor_tensor(z_rows0[:, t, :], x[:, t, :], cap0[:, t, :], ALU.min)
         z_grouped0 = held("z_grouped0", [P, PICKS, PACK], BF16, tag="tab1")
         interleave(nc.scalar.copy, z_grouped0[:], z_rows0[:])
-        cap1 = held("cap1", [P, PACK, PICKS], F32, tag="tab0")
+        cap1 = held("cap1", [P, PACK, PICKS], F32, tag="v_codes0")
         nc.sync.dma_start(cap1[:], cap_rows[1])
 
         z_plane = [held(f"z_plane{a}", [P, PICKS], U8) for a in range(2)]
         for t in range(PACK - 1):
-            put(t, idx2[:], h1[t][:], slice(0, S))
+            put(t, idx2[:], h1[t][:, 0, :], slice(0, S))
         z_codes0 = held("z_codes0", [P, PICKS], U32, tag="h12")
         quantize(z_codes0[:], z_plane[0][:], z_grouped0[:].rearrange("p n t -> p (n t)"))
-        put(PACK - 1, idx2[:], h1[PACK - 1][:], slice(0, S))
+        put(PACK - 1, idx2[:], h1[PACK - 1][:, 0, :], slice(0, S))
         for t in range(PACK - 1):
             nc.vector.tensor_copy(x[:, t, :], pages[t][:].indirect(idx3[:]))
-        z_codes = [z_codes0, held("z_codes1", [P, PICKS], U32, tag="h00")]
+        z_codes = [z_codes0, held("z_codes1", [P, PICKS], U32, tag="h0_0")]
 
         out_rows = out.rearrange("(c p) m -> p c m", p=P)
-        staging_tags = ["h01", "h02", "h10", "h11"]
+        staging_tags = ["h0_1", "h0_2", "h0_3", "h10"]
 
         def limit(j):
             nc.vector.tensor_copy(x[:, PACK - 1, cols(j)], pages[PACK - 1][:].indirect(idx3[:, entries(j)]))
-            z_rows = ringed("z_rows", [P, PACK, PIECE], BF16)
+            z_rows = held(f"z_rows_p{j}", [P, PACK, PIECE], BF16, tag=f"z_grouped_p{j - 2}" if j >= 2 else None)
             nc.vector.tensor_tensor(z_rows[:], x[:, :, cols(j)], cap1[:, :, cols(j)], ALU.min)
             z_grouped = held(f"z_grouped_p{j}", [P, PIECE, PACK], BF16)
             interleave(nc.vector.tensor_copy if j == PIECES - 1 else nc.scalar.copy, z_grouped[:], z_rows[:])
@@ -295,7 +290,7 @@ def tile_list_spill_slot_advisor_kernel(
                     )
             staged = held(f"staged{j}", [P, 4, PIECE], F32, tag=staging_tags[j])
             for c in range(4):
-                copy = nc.vector.tensor_copy if (j == PIECES - 1 and c % 2 == 1) else nc.scalar.copy
+                copy = nc.vector.tensor_copy if j == PIECES - 1 else nc.scalar.copy
                 copy(staged[:, c, :], banks[c][:, 0:PIECE])
             for pair in range(2):
                 nc.sync.dma_start(out_rows[:, 2 * pair : 2 * pair + 2, cols(j)], staged[:, 2 * pair : 2 * pair + 2, :])

@@ -51,12 +51,10 @@ def tile_list_spill_slot_advisor_kernel(
                 src.rearrange("p t (c i) -> p c t i", i=4),
             )
 
-        tab_plane = held("tab_plane", [P, T], U8)
+        tab_plane = held("tab_plane", [P, T], U8, tag="v_codes0")
         w1_plane_raw = held("w1_plane_raw", [P, 2, M], U8)
         v_plane = [held(f"v_plane{a}", [P, S], U8) for a in range(2)]
         nc.gpsimd.memset(w1_plane_raw[:].rearrange("p a c -> p (a c)").bitcast(I32), 0)
-        for q in range(4):
-            nc.vector.memset(tab_plane[32 * q : 32 * q + 24, :].bitcast(I32), 0)
         for a in range(2):
             nc.vector.memset(v_plane[a][96:128, :].bitcast(I32), 0)
 
@@ -74,6 +72,8 @@ def tile_list_spill_slot_advisor_kernel(
             nc.sync.dma_start(
                 tab_plane[32 * q + 24 : 32 * q + 32, :].bitcast(I32), tab_scales[:, 4 * q : 4 * q + 4, :].bitcast(I32)
             )
+        for q in range(4):
+            nc.vector.memset(tab_plane[32 * q : 32 * q + 24, :].bitcast(I32), 0)
         w1_raw = held("w1_raw", [P, 2, M // 2], I32)
         nc.sync.dma_start(w1_raw[:], w1_words.rearrange("a p b -> p a b").bitcast(I32))
         w2_rows = w2.rearrange("(p j) r -> p j r", j=PACK)

@@ -116,20 +116,20 @@ def tile_list_spill_slot_advisor_kernel(
         nc.vector.tensor_copy(v_codes0[:], tab[0][:].bitcast(U32).indirect(idx[:]))
         v_codes1_first = held("v_codes1_first", [P, PIECE], U32)
         nc.vector.tensor_copy(v_codes1_first[:], tab[1][:].bitcast(U32).indirect(idx[:, entries(0)]))
-        v_codes1_rest = held("v_codes1_rest", [P, S - PIECE], U32, tag="w1_plane_raw")
-        nc.vector.tensor_copy(v_codes1_rest[:], tab[1][:].bitcast(U32).indirect(idx[:, LIST_COLS : S // 16]))
+        v_codes1_second = held("v_codes1_second", [P, PIECE], U32, tag="w1_plane_raw")
+        nc.vector.tensor_copy(v_codes1_second[:], tab[1][:].bitcast(U32).indirect(idx[:, entries(1)]))
+        v_codes1 = [v_codes1_first, v_codes1_second]
 
         def v_codes(a, c0):
             if a == 0:
                 return v_codes0[:, c0 : c0 + 128]
-            if c0 < PIECE:
-                return v_codes1_first[:, c0 : c0 + 128]
-            return v_codes1_rest[:, c0 - PIECE : c0 - PIECE + 128]
+            part = min(c0 // PIECE, 2)
+            return v_codes1[part][:, c0 - part * PIECE : c0 - part * PIECE + 128]
 
         wgs_sb = held("wgs_sb", [P, PACK, S], F32, tag="picked_scales")
         wgs_rows = wgs.rearrange("(p t) s -> p t s", t=PACK)
-        for span in (slice(0, PIECE), slice(PIECE, S)):
-            for q in range(4):
+        for span in (cols(0), cols(1), slice(2 * PIECE, S)):
+            for q in (0, 2, 1, 3):
                 nc.sync.dma_start(wgs_sb[32 * q : 32 * q + 32, :, span], wgs_rows[:, :, span])
         cap_rows = cap.rearrange("(a p t) m -> a p t m", a=2, t=PACK)
 
@@ -179,7 +179,7 @@ def tile_list_spill_slot_advisor_kernel(
                     nc.vector.tensor_scalar(e_rows[:, t, :], th[:, t, :], gain_sb[:, t : t + 1], None, ALU.mult)
                 else:
                     nc.scalar.activation(e_rows[:, t, :], th[:, t, :], ACT.Copy, scale=gain_sb[:, t : t + 1])
-            e_grouped = ringed("e_grouped", [P, PIECE, PACK], BF16)
+            e_grouped = held(f"e_grouped{j}", [P, PIECE, PACK], BF16)
             interleave(nc.vector.tensor_copy if j == 0 else nc.scalar.copy, e_grouped[:], e_rows[:])
             return e_grouped
 
@@ -206,6 +206,8 @@ def tile_list_spill_slot_advisor_kernel(
 
         quantize_w2(0, round_w2(0, nc.scalar.copy, "w2_grouped0"))
         quantize_e(0, features(0))
+        v_codes1.append(held("v_codes1_rest", [P, S - 2 * PIECE], U32, tag="e_grouped0"))
+        nc.vector.tensor_copy(v_codes1[2][:], tab[1][:].bitcast(U32).indirect(idx[:, 2 * LIST_COLS : S // 16]))
         w2_raw.append(held("w2_raw1", [P, PACK, 512], F32, tag="v_codes1_first"))
         nc.sync.dma_start(w2_raw[1][:], w2_rows[:, :, 512:1024])
         for j in range(PIECES):
@@ -234,7 +236,7 @@ def tile_list_spill_slot_advisor_kernel(
                 costs(1, (t,), span, h1[t][:, :, span])
 
         w3_plane = held("w3_plane", [P, 2, N], U8, tag="e_rows0")
-        nc.vector.memset(w3_plane[:].rearrange("p a c -> p (a c)").bitcast(I32), 0)
+        nc.gpsimd.memset(w3_plane[:].rearrange("p a c -> p (a c)").bitcast(I32), 0)
         for q in range(4):
             nc.sync.dma_start(
                 w3_plane[32 * q : 32 * q + 4, :, :].bitcast(I32),
@@ -290,7 +292,7 @@ def tile_list_spill_slot_advisor_kernel(
                     )
             staged = held(f"staged{j}", [P, 4, PIECE], F32, tag=staging_tags[j])
             for c in range(4):
-                copy = nc.vector.tensor_copy if j == PIECES - 1 else nc.scalar.copy
+                copy = nc.vector.tensor_copy if (j == PIECES - 1 and c < 3) else nc.scalar.copy
                 copy(staged[:, c, :], banks[c][:, 0:PIECE])
             for pair in range(2):
                 nc.sync.dma_start(out_rows[:, 2 * pair : 2 * pair + 2, cols(j)], staged[:, 2 * pair : 2 * pair + 2, :])

@@ -51,16 +51,20 @@ def tile_list_spill_slot_advisor_kernel(
                 src.rearrange("p t (c i) -> p c t i", i=4),
             )
 
-        tab_plane = held("tab_plane", [P, T], U8, tag="v_codes0")
+        tab_plane = held("tab_plane", [P, T], U8)
         w1_plane_raw = held("w1_plane_raw", [P, 2, M], U8)
         v_plane = [held(f"v_plane{a}", [P, S], U8) for a in range(2)]
+        pages = [held(f"page{t}", [P, T2], F32) for t in range(PACK)]
         nc.gpsimd.memset(w1_plane_raw[:].rearrange("p a c -> p (a c)").bitcast(I32), 0)
+        for q in range(4):
+            nc.vector.memset(tab_plane[32 * q : 32 * q + 24, :].bitcast(I32), 0)
         for a in range(2):
             nc.vector.memset(v_plane[a][96:128, :].bitcast(I32), 0)
 
         warm = held("warm", [P, 8], F32)
         nc.vector.memset(warm[:, 0:1], 0.0)
         nc.scalar.activation(warm[:, 1:2], warm[:, 0:1], ACT.Tanh)
+        nc.vector.memset(pages[0][:], 0.0)
 
         idx = lists.tile([P, S // 16], U16, name="idx")
         idx2 = lists.tile([P, S // 16], U16, name="idx2")
@@ -72,18 +76,14 @@ def tile_list_spill_slot_advisor_kernel(
             nc.sync.dma_start(
                 tab_plane[32 * q + 24 : 32 * q + 32, :].bitcast(I32), tab_scales[:, 4 * q : 4 * q + 4, :].bitcast(I32)
             )
-        for q in range(4):
-            nc.vector.memset(tab_plane[32 * q : 32 * q + 24, :].bitcast(I32), 0)
-        w1_raw = held("w1_raw", [P, 2, M // 2], I32)
-        nc.sync.dma_start(w1_raw[:], w1_words.rearrange("a p b -> p a b").bitcast(I32))
-        w2_rows = w2.rearrange("(p j) r -> p j r", j=PACK)
-        w2_raw = [held("w2_raw0", [P, PACK, 512], F32)]
-        nc.sync.dma_start(w2_raw[0][:], w2_rows[:, :, 0:512])
         tab = [held(f"tab{a}", [P, T], I32) for a in range(2)]
-        for a in range(2):
-            nc.sync.dma_start(tab[a][:], tab_words[a].rearrange("p t i -> p (t i)").bitcast(I32))
+        w1_raw = held("w1_raw", [P, 2, M // 2], I32)
+        nc.sync.dma_start(tab[0][:], tab_words[0].rearrange("p t i -> p (t i)").bitcast(I32))
+        nc.sync.dma_start(w1_raw[:], w1_words.rearrange("a p b -> p a b").bitcast(I32))
+        nc.sync.dma_start(tab[1][:], tab_words[1].rearrange("p t i -> p (t i)").bitcast(I32))
         nc.sync.dma_start(b1_sb[:], b1.rearrange("(p t) -> p t", t=PACK))
         nc.sync.dma_start(gain_sb[:], gain.rearrange("(p t) -> p t", t=PACK))
+        w2_rows = w2.rearrange("(p j) r -> p j r", j=PACK)
         for q in range(4):
             nc.gpsimd.dma_start(
                 w1_plane_raw[32 * q : 32 * q + 4, :, :].bitcast(I32),
@@ -91,42 +91,39 @@ def tile_list_spill_slot_advisor_kernel(
             )
         nc.sync.dma_start(idx2[:], offs2)
         nc.sync.dma_start(idx3[:], offs3)
-        pages = [held(f"page{t}", [P, T2], F32) for t in range(PACK)]
-        for t in range(PACK):
+        for t in range(1, PACK):
             for c0 in range(0, T2, 512):
                 nc.gpsimd.memset(pages[t][:, c0 : c0 + 512], 0.0)
-
-        w1_codes = held("w1_codes", [P, 2, M // 2], I32)
-        nc.vector.tensor_copy(
-            w1_codes[:].bitcast(U16).rearrange("p a (t m) -> p a m t", t=PACK),
-            w1_raw[:].bitcast(U16).rearrange("p a (m t) -> p a m t", t=PACK),
-        )
 
         picked_scales = held("picked_scales", [P, S], U8)
         nc.vector.tensor_copy(picked_scales[:], tab_plane[:].indirect(idx[:]))
         for a in range(2):
             shift = 24 + 4 * a
             nc.scalar.dma_start(v_plane[a][0 : P - shift, :].bitcast(I32), picked_scales[shift:P, :].bitcast(I32))
+
+        def pick_words(a, name, first, last, tag=None):
+            codes = held(name, [P, (last - first) * PIECE], U32, tag=tag)
+            offsets = idx[:, first * LIST_COLS : last * LIST_COLS]
+            nc.vector.tensor_copy(codes[:], tab[a][:].bitcast(U32).indirect(offsets))
+            return [codes[:, (j - first) * PIECE : (j - first + 1) * PIECE] for j in range(first, last)]
+
+        v_codes = [pick_words(0, "v0_front", 0, 2)]
+
+        w1_codes = held("w1_codes", [P, 2, M // 2], I32)
+        nc.vector.tensor_copy(
+            w1_codes[:].bitcast(U16).rearrange("p a (t m) -> p a m t", t=PACK),
+            w1_raw[:].bitcast(U16).rearrange("p a (m t) -> p a m t", t=PACK),
+        )
+        w2_raw = [held("w2_raw0", [P, PACK, 512], F32, tag="w1_raw")]
+        nc.sync.dma_start(w2_raw[0][:], w2_rows[:, :, 0:512])
         w1_plane = held("w1_plane", [P, 2, M], U8)
         nc.vector.tensor_copy(
             w1_plane[:].rearrange("p a (t m) -> p a m t", t=PACK),
             w1_plane_raw[:].rearrange("p a (m t) -> p a m t", t=PACK),
         )
-        v_codes0 = held("v_codes0", [P, S], U32)
-        nc.vector.tensor_copy(v_codes0[:], tab[0][:].bitcast(U32).indirect(idx[:]))
-        v_codes1_first = held("v_codes1_first", [P, PIECE], U32)
-        nc.vector.tensor_copy(v_codes1_first[:], tab[1][:].bitcast(U32).indirect(idx[:, entries(0)]))
-        v_codes1_second = held("v_codes1_second", [P, PIECE], U32, tag="w1_plane_raw")
-        nc.vector.tensor_copy(v_codes1_second[:], tab[1][:].bitcast(U32).indirect(idx[:, entries(1)]))
-        v_codes1 = [v_codes1_first, v_codes1_second]
+        v_codes.append(pick_words(1, "v1_first", 0, 1) + pick_words(1, "v1_second", 1, 2))
 
-        def v_codes(a, c0):
-            if a == 0:
-                return v_codes0[:, c0 : c0 + 128]
-            part = min(c0 // PIECE, 2)
-            return v_codes1[part][:, c0 - part * PIECE : c0 - part * PIECE + 128]
-
-        wgs_sb = held("wgs_sb", [P, PACK, S], F32, tag="picked_scales")
+        wgs_sb = held("wgs_sb", [P, PACK, S], F32, tag="w1_plane_raw")
         wgs_rows = wgs.rearrange("(p t) s -> p t s", t=PACK)
         for span in (cols(0), cols(1), slice(2 * PIECE, S)):
             for q in (0, 2, 1, 3):
@@ -136,54 +133,52 @@ def tile_list_spill_slot_advisor_kernel(
         w2_codes = [held(f"w2_codes{a}", [P, 512], U32) for a in range(2)]
         w2_plane = [held(f"w2_plane{a}", [P, 512], U8) for a in range(2)]
 
-        def round_w2(a, engine_copy, tag):
-            grouped = held(f"w2_grouped{a}", [P, PACK, 128, PACK], BF16, tag=tag)
-            engine_copy(
-                grouped[:].rearrange("p t m j -> p m j t"), w2_raw[a][:].rearrange("p j (m t) -> p m j t", t=PACK)
-            )
-            return grouped
-
         def quantize(codes, plane, grouped):
             nc.vector.quantize_mx(out=codes.bitcast(FP8X4), scales=plane, in_=grouped)
 
-        def quantize_w2(a, grouped):
-            quantize(w2_codes[a][:], w2_plane[a][:], grouped[:].rearrange("p t m j -> p (t m j)"))
+        def quantize_w2(a, t0, t1, tag=None):
+            grouped = held(f"w2_grouped{a}{t0}", [P, t1 - t0, 128, PACK], BF16, tag=tag)
+            nc.scalar.copy(
+                grouped[:].rearrange("p t m j -> p m j t"),
+                w2_raw[a][:].rearrange("p j (m t) -> p m j t", t=PACK)[:, :, :, t0:t1],
+            )
+            span = slice(128 * t0, 128 * t1)
+            quantize(w2_codes[a][:, span], w2_plane[a][:, span], grouped[:].rearrange("p t m j -> p (t m j)"))
 
         e_codes = held("e_codes", [P, S], U32)
         e_plane = held("e_plane", [P, S], U8)
 
         def features(j):
             th = ringed("th", [P, PACK, PIECE], F32)
-            for pair in range(2):
-                bank = psum.tile([P, 2, PIECE], F32, name="bank_a", tag="bank_a")
-                for u in range(2):
-                    t = 2 * pair + u
+            banks = [psum.tile([P, PIECE], F32, name=f"pre{t}", tag="bank_a") for t in range(PACK)]
+            for a in range(2):
+                for t in range(PACK):
                     for half in range(2):
-                        c0 = j * PIECE + half * 128
-                        for a in range(2):
-                            nc.tensor.matmul_mx(
-                                out=bank[:, u, half * 128 : half * 128 + 128],
-                                lhsT=w1_codes[:, a, 64 * t : 64 * t + 64].bitcast(FP4X4),
-                                lhsT_scale=w1_plane[:, a, 128 * t : 128 * t + 128],
-                                rhs=v_codes(a, c0).bitcast(FP8X4),
-                                rhs_scale=v_plane[a][:, c0 : c0 + 128],
-                                start=(a == 0),
-                                stop=(a == 1),
-                            )
-                for u in range(2):
-                    t = 2 * pair + u
-                    nc.scalar.activation(th[:, t, :], bank[:, u, :], ACT.Tanh, bias=b1_sb[:, t : t + 1])
-            e_rows = held(f"e_rows{j}", [P, PACK, PIECE], BF16)
+                        c0 = half * 128
+                        nc.tensor.matmul_mx(
+                            out=banks[t][:, c0 : c0 + 128],
+                            lhsT=w1_codes[:, a, 64 * t : 64 * t + 64].bitcast(FP4X4),
+                            lhsT_scale=w1_plane[:, a, 128 * t : 128 * t + 128],
+                            rhs=v_codes[a][j][:, c0 : c0 + 128].bitcast(FP8X4),
+                            rhs_scale=v_plane[a][:, j * PIECE + c0 : j * PIECE + c0 + 128],
+                            start=(a == 0 and half == 0),
+                            stop=(a == 1 and half == 1),
+                        )
             for t in range(PACK):
-                if j == 0:
-                    nc.vector.tensor_scalar(e_rows[:, t, :], th[:, t, :], gain_sb[:, t : t + 1], None, ALU.mult)
-                else:
-                    nc.scalar.activation(e_rows[:, t, :], th[:, t, :], ACT.Copy, scale=gain_sb[:, t : t + 1])
+                nc.scalar.activation(th[:, t, :], banks[t][:], ACT.Tanh, bias=b1_sb[:, t : t + 1])
             e_grouped = held(f"e_grouped{j}", [P, PIECE, PACK], BF16)
-            interleave(nc.vector.tensor_copy if j == 0 else nc.scalar.copy, e_grouped[:], e_rows[:])
-            return e_grouped
-
-        def quantize_e(j, e_grouped):
+            if j == 0:
+                nc.vector.tensor_tensor(
+                    e_grouped[:].rearrange("p (c i) t -> p c t i", i=4),
+                    th[:].rearrange("p t (c i) -> p c t i", i=4),
+                    gain_sb[:].unsqueeze(1).unsqueeze(3).to_broadcast([P, PIECE // 4, PACK, 4]),
+                    ALU.mult,
+                )
+            else:
+                e_rows = held(f"e_rows{j}", [P, PACK, PIECE], BF16)
+                for t in range(PACK):
+                    nc.scalar.activation(e_rows[:, t, :], th[:, t, :], ACT.Copy, scale=gain_sb[:, t : t + 1])
+                interleave(nc.scalar.copy, e_grouped[:], e_rows[:])
             quantize(e_codes[:, cols(j)], e_plane[:, cols(j)], e_grouped[:].rearrange("p n t -> p (n t)"))
 
         def costs(a, slots, span, dst):
@@ -204,30 +199,32 @@ def tile_list_spill_slot_advisor_kernel(
         def put(t, offsets, values, span):
             nc.vector.tensor_tensor(pages[t][:].indirect(offsets), values, wgs_sb[:, t, span], ALU.mult)
 
-        quantize_w2(0, round_w2(0, nc.scalar.copy, "w2_grouped0"))
-        quantize_e(0, features(0))
-        v_codes1.append(held("v_codes1_rest", [P, S - 2 * PIECE], U32, tag="e_grouped0"))
-        nc.vector.tensor_copy(v_codes1[2][:], tab[1][:].bitcast(U32).indirect(idx[:, 2 * LIST_COLS : S // 16]))
-        w2_raw.append(held("w2_raw1", [P, PACK, 512], F32, tag="v_codes1_first"))
-        nc.sync.dma_start(w2_raw[1][:], w2_rows[:, :, 512:1024])
+        quantize_w2(0, 0, 2)
+        features(0)
+        v_codes[0].extend(pick_words(0, "v0_back", 2, PIECES, tag="v1_first"))
+        v_codes[1].extend(pick_words(1, "v1_back", 2, PIECES, tag="e_grouped0"))
+        quantize_w2(0, 2, PACK)
+        w2_raw.append(held("w2_raw1", [P, PACK, 512], F32, tag="v1_second"))
         for j in range(PIECES):
-            h0 = held(f"h0_{j}", [P, PACK - 1, PIECE], F32)
+            h0 = held(f"h0_{j}", [P, PACK, PIECE], F32)
             costs(0, (0,), cols(j), h0[:, 0:1, :])
             costs(0, (1, 2), cols(j), h0[:, 1:3, :])
             for t in range(PACK - 1):
                 put(t, idx2[:, entries(j)], h0[:, t, :], cols(j))
             if j + 1 < PIECES:
-                quantize_e(j + 1, features(j + 1))
-                h03 = held(f"h03_{j}", [P, 1, PIECE], F32, tag=f"e_rows{j + 1}")
+                features(j + 1)
+                h03 = held(f"h03_{j}", [P, 1, PIECE], F32, tag=f"e_rows{j + 1}")[:]
             else:
-                h03 = held(f"h03_{j}", [P, 1, PIECE], F32)
-            costs(0, (PACK - 1,), cols(j), h03[:])
+                h03 = h0[:, 3:4, :]
+            if j == 0:
+                nc.sync.dma_start(w2_raw[1][:], w2_rows[:, :, 512:1024])
+            costs(0, (PACK - 1,), cols(j), h03)
             put(PACK - 1, idx2[:, entries(j)], h03[:, 0, :], cols(j))
-        cap0 = held("cap0", [P, PACK, PICKS], F32, tag="v_codes0")
+        cap0 = held("cap0", [P, PACK, PICKS], F32, tag="tab0")
         nc.sync.dma_start(cap0[:], cap_rows[0])
-        w3_codes = held("w3_codes", [P, 2, N], I32, tag="v_plane0")
+        w3_codes = held("w3_codes", [P, 2, N], I32, tag="v_plane1")
         nc.sync.dma_start(w3_codes[:], w3_words.rearrange("a p c i -> p a (c i)").bitcast(I32))
-        quantize_w2(1, round_w2(1, nc.scalar.copy, f"e_rows{PIECES - 1}"))
+        quantize_w2(1, 0, PACK, tag=f"e_rows{PIECES - 1}")
 
         h1 = [held(f"h1{t}", [P, 1, S], F32) for t in range(PACK)]
         for t in range(PACK):
@@ -235,7 +232,7 @@ def tile_list_spill_slot_advisor_kernel(
                 span = slice(512 * half, 512 * half + 512)
                 costs(1, (t,), span, h1[t][:, :, span])
 
-        w3_plane = held("w3_plane", [P, 2, N], U8, tag="e_rows0")
+        w3_plane = held("w3_plane", [P, 2, N], U8, tag="e_rows1")
         nc.gpsimd.memset(w3_plane[:].rearrange("p a c -> p (a c)").bitcast(I32), 0)
         for q in range(4):
             nc.sync.dma_start(
@@ -244,61 +241,67 @@ def tile_list_spill_slot_advisor_kernel(
             )
 
         x = held("x", [P, PACK, PICKS], F32)
-        z_rows0 = held("z_rows0", [P, PACK, PICKS], BF16, tag="w2_raw0")
+        z_rows0 = held("z_rows0", [P, PACK, PICKS], BF16, tag="w1_raw")
         for t in range(PACK):
             nc.vector.tensor_copy(x[:, t, :], pages[t][:].indirect(idx3[:]))
-        for t in range(PACK):
-            nc.vector.tensor_tensor(z_rows0[:, t, :], x[:, t, :], cap0[:, t, :], ALU.min)
+        for t in range(0, PACK, 2):
+            nc.vector.tensor_tensor(z_rows0[:, t : t + 2, :], x[:, t : t + 2, :], cap0[:, t : t + 2, :], ALU.min)
         z_grouped0 = held("z_grouped0", [P, PICKS, PACK], BF16, tag="tab1")
         interleave(nc.scalar.copy, z_grouped0[:], z_rows0[:])
-        cap1 = held("cap1", [P, PACK, PICKS], F32, tag="v_codes0")
+        cap1 = held("cap1", [P, PACK, PICKS], F32, tag="tab0")
         nc.sync.dma_start(cap1[:], cap_rows[1])
 
         z_plane = [held(f"z_plane{a}", [P, PICKS], U8) for a in range(2)]
         for t in range(PACK - 1):
             put(t, idx2[:], h1[t][:, 0, :], slice(0, S))
-        z_codes0 = held("z_codes0", [P, PICKS], U32, tag="h12")
-        quantize(z_codes0[:], z_plane[0][:], z_grouped0[:].rearrange("p n t -> p (n t)"))
+        z_codes = [held("z_codes0", [P, PICKS], U32, tag="h12"), held("z_codes1", [P, PICKS], U32)]
+        quantize(z_codes[0][:], z_plane[0][:], z_grouped0[:].rearrange("p n t -> p (n t)"))
         put(PACK - 1, idx2[:], h1[PACK - 1][:, 0, :], slice(0, S))
-        for t in range(PACK - 1):
-            nc.vector.tensor_copy(x[:, t, :], pages[t][:].indirect(idx3[:]))
-        z_codes = [z_codes0, held("z_codes1", [P, PICKS], U32, tag="h0_0")]
 
         out_rows = out.rearrange("(c p) m -> p c m", p=P)
-        staging_tags = ["h0_1", "h0_2", "h0_3", "h10"]
+        spans = [cols(j) for j in range(PIECES - 1)] + [slice(768, 896), slice(896, 1024)]
 
-        def limit(j):
-            nc.vector.tensor_copy(x[:, PACK - 1, cols(j)], pages[PACK - 1][:].indirect(idx3[:, entries(j)]))
-            z_rows = held(f"z_rows_p{j}", [P, PACK, PIECE], BF16, tag=f"z_grouped_p{j - 2}" if j >= 2 else None)
-            nc.vector.tensor_tensor(z_rows[:], x[:, :, cols(j)], cap1[:, :, cols(j)], ALU.min)
-            z_grouped = held(f"z_grouped_p{j}", [P, PIECE, PACK], BF16)
-            interleave(nc.vector.tensor_copy if j == PIECES - 1 else nc.scalar.copy, z_grouped[:], z_rows[:])
-            return z_grouped
-
-        def scores(j, z_grouped):
-            quantize(z_codes[1][:, cols(j)], z_plane[1][:, cols(j)], z_grouped[:].rearrange("p n t -> p (n t)"))
-            tag = "bank_a" if j % 2 == 0 else "bank_b"
-            banks = [psum.tile([P, 512], F32, name=f"acc{c}", tag=tag) for c in range(4)]
-            for a in range(2):
-                for c in range(4):
-                    nc.tensor.matmul_mx(
-                        out=banks[c][:, 0:PIECE],
-                        lhsT=w3_codes[:, a, 128 * c : 128 * c + 128].bitcast(FP8X4),
-                        lhsT_scale=w3_plane[:, a, 128 * c : 128 * c + 128],
-                        rhs=z_codes[a][:, cols(j)].bitcast(FP8X4),
-                        rhs_scale=z_plane[a][:, cols(j)],
-                        start=(a == 0),
-                        stop=(a == 1),
-                    )
-            staged = held(f"staged{j}", [P, 4, PIECE], F32, tag=staging_tags[j])
+        def score_pass(a, banks, span):
             for c in range(4):
-                copy = nc.vector.tensor_copy if (j == PIECES - 1 and c < 3) else nc.scalar.copy
-                copy(staged[:, c, :], banks[c][:, 0:PIECE])
-            for pair in range(2):
-                nc.sync.dma_start(out_rows[:, 2 * pair : 2 * pair + 2, cols(j)], staged[:, 2 * pair : 2 * pair + 2, :])
+                nc.tensor.matmul_mx(
+                    out=banks[c][:],
+                    lhsT=w3_codes[:, a, 128 * c : 128 * c + 128].bitcast(FP8X4),
+                    lhsT_scale=w3_plane[:, a, 128 * c : 128 * c + 128],
+                    rhs=z_codes[a][:, span].bitcast(FP8X4),
+                    rhs_scale=z_plane[a][:, span],
+                    start=(a == 0),
+                    stop=(a == 1),
+                )
 
-        grouped = limit(0)
-        for j in range(PIECES):
-            ahead = limit(j + 1) if j + 1 < PIECES else None
-            scores(j, grouped)
-            grouped = ahead
+        def open_scores(n):
+            span = spans[n]
+            tag = "bank_a" if n % 2 == 0 else "bank_b"
+            banks = [psum.tile([P, span.stop - span.start], F32, name=f"acc{c}", tag=tag) for c in range(4)]
+            score_pass(0, banks, span)
+            return banks
+
+        opened = [open_scores(0), open_scores(1)]
+        for t in range(2):
+            nc.vector.tensor_copy(x[:, t, :], pages[t][:].indirect(idx3[:]))
+        for n, span in enumerate(spans):
+            width = span.stop - span.start
+            if n < PIECES:
+                for t in range(2, PACK):
+                    nc.vector.tensor_copy(x[:, t, cols(n)], pages[t][:].indirect(idx3[:, entries(n)]))
+            z_grouped = held(f"z_grouped_p{n}", [P, width, PACK], BF16)
+            nc.vector.tensor_tensor(
+                z_grouped[:].rearrange("p (c i) t -> p c t i", i=4),
+                x[:, :, span].rearrange("p t (c i) -> p c t i", i=4),
+                cap1[:, :, span].rearrange("p t (c i) -> p c t i", i=4),
+                ALU.min,
+            )
+            quantize(z_codes[1][:, span], z_plane[1][:, span], z_grouped[:].rearrange("p n t -> p (n t)"))
+            score_pass(1, opened[n], span)
+            staged = held(f"staged{n}", [P, 4, width], F32, tag=f"h0_{n}" if n < PIECES else "h10")
+            for c in range(4):
+                copy = nc.vector.tensor_copy if (n >= PIECES - 1 and c < 2) else nc.scalar.copy
+                copy(staged[:, c, :], opened[n][c][:])
+            for pair in range(2):
+                nc.sync.dma_start(out_rows[:, 2 * pair : 2 * pair + 2, span], staged[:, 2 * pair : 2 * pair + 2, :])
+            if n + 2 < len(spans):
+                opened.append(open_scores(n + 2))

@@ -51,20 +51,15 @@ def tile_list_spill_slot_advisor_kernel(
                 src.rearrange("p t (c i) -> p c t i", i=4),
             )
 
-        tab_plane = held("tab_plane", [P, T], U8)
+        tab_plane = held("tab_plane", [P, 2, T], U8)
         w1_plane_raw = held("w1_plane_raw", [P, 2, M], U8)
-        v_plane = [held(f"v_plane{a}", [P, S], U8) for a in range(2)]
-        pages = [held(f"page{t}", [P, T2], F32) for t in range(PACK)]
+        pages = [held(f"page{t}", [P, T2], F32) for t in range(2)]
         nc.gpsimd.memset(w1_plane_raw[:].rearrange("p a c -> p (a c)").bitcast(I32), 0)
-        for q in range(4):
-            nc.vector.memset(tab_plane[32 * q : 32 * q + 24, :].bitcast(I32), 0)
-        for a in range(2):
-            nc.vector.memset(v_plane[a][96:128, :].bitcast(I32), 0)
-
+        nc.vector.memset(tab_plane[:].rearrange("p a c -> p (a c)").bitcast(I32), 0)
         warm = held("warm", [P, 8], F32)
         nc.vector.memset(warm[:, 0:1], 0.0)
-        nc.scalar.activation(warm[:, 1:2], warm[:, 0:1], ACT.Tanh)
-        nc.vector.memset(pages[0][:], 0.0)
+        for t in range(2):
+            nc.vector.memset(pages[t][:], 0.0)
 
         idx = lists.tile([P, S // 16], U16, name="idx")
         idx2 = lists.tile([P, S // 16], U16, name="idx2")
@@ -72,42 +67,41 @@ def tile_list_spill_slot_advisor_kernel(
         b1_sb = held("b1_sb", [P, PACK], F32)
         gain_sb = held("gain_sb", [P, PACK], F32)
         nc.sync.dma_start(idx[:], offs)
-        for q in range(4):
-            nc.sync.dma_start(
-                tab_plane[32 * q + 24 : 32 * q + 32, :].bitcast(I32), tab_scales[:, 4 * q : 4 * q + 4, :].bitcast(I32)
-            )
-        tab = [held(f"tab{a}", [P, T], I32) for a in range(2)]
-        w1_raw = held("w1_raw", [P, 2, M // 2], I32)
-        nc.sync.dma_start(tab[0][:], tab_words[0].rearrange("p t i -> p (t i)").bitcast(I32))
-        nc.sync.dma_start(w1_raw[:], w1_words.rearrange("a p b -> p a b").bitcast(I32))
-        nc.sync.dma_start(tab[1][:], tab_words[1].rearrange("p t i -> p (t i)").bitcast(I32))
-        nc.sync.dma_start(b1_sb[:], b1.rearrange("(p t) -> p t", t=PACK))
-        nc.sync.dma_start(gain_sb[:], gain.rearrange("(p t) -> p t", t=PACK))
-        w2_rows = w2.rearrange("(p j) r -> p j r", j=PACK)
-        for q in range(4):
-            nc.gpsimd.dma_start(
-                w1_plane_raw[32 * q : 32 * q + 4, :, :].bitcast(I32),
-                w1_scales[:, 4 * q : 4 * q + 4, :].rearrange("a r c -> r a c").bitcast(I32),
-            )
         nc.sync.dma_start(idx2[:], offs2)
         nc.sync.dma_start(idx3[:], offs3)
-        for t in range(1, PACK):
-            for c0 in range(0, T2, 512):
-                nc.gpsimd.memset(pages[t][:, c0 : c0 + 512], 0.0)
+        nc.sync.dma_start(b1_sb[:], b1.rearrange("(p t) -> p t", t=PACK))
+        nc.sync.dma_start(gain_sb[:], gain.rearrange("(p t) -> p t", t=PACK))
+        tab = [held("tab0", [P, T], I32)]
+        w1_raw = held("w1_raw", [P, 2, M // 2], I32)
+        nc.sync.dma_start(w1_raw[:], w1_words.rearrange("a p b -> p a b").bitcast(I32))
+        nc.sync.dma_start(tab[0][:], tab_words[0].rearrange("p t i -> p (t i)").bitcast(I32))
+        w2_rows = w2.rearrange("(p j) r -> p j r", j=PACK)
 
-        picked_scales = held("picked_scales", [P, S], U8)
-        nc.vector.tensor_copy(picked_scales[:], tab_plane[:].indirect(idx[:]))
-        for a in range(2):
-            shift = 24 + 4 * a
-            nc.scalar.dma_start(v_plane[a][0 : P - shift, :].bitcast(I32), picked_scales[shift:P, :].bitcast(I32))
+        def load_scale_rows(queue, plane, scales, q):
+            queue.dma_start(
+                plane[32 * q : 32 * q + 4, :, :].bitcast(I32),
+                scales[:, 4 * q : 4 * q + 4, :].rearrange("a r c -> r a c").bitcast(I32),
+            )
+
+        for q in range(4):
+            load_scale_rows(nc.sync, tab_plane, tab_scales, q)
+        for q in range(4):
+            load_scale_rows(nc.gpsimd if q < 2 else nc.sync, w1_plane_raw, w1_scales, q)
+        nc.scalar.activation(warm[:, 1:2], warm[:, 0:1], ACT.Tanh)
+        tab.append(held("tab1", [P, T], I32, tag="warm"))
+        nc.sync.dma_start(tab[1][:], tab_words[1].rearrange("p t i -> p (t i)").bitcast(I32))
+
+        def pick(window, dtype, name, first, last, tag=None):
+            picked = held(name, [P, (last - first) * PIECE], dtype, tag=tag)
+            offsets = idx[:, first * LIST_COLS : last * LIST_COLS]
+            nc.vector.tensor_copy(picked[:], window.indirect(offsets))
+            return [picked[:, (j - first) * PIECE : (j - first + 1) * PIECE] for j in range(first, last)]
 
         def pick_words(a, name, first, last, tag=None):
-            codes = held(name, [P, (last - first) * PIECE], U32, tag=tag)
-            offsets = idx[:, first * LIST_COLS : last * LIST_COLS]
-            nc.vector.tensor_copy(codes[:], tab[a][:].bitcast(U32).indirect(offsets))
-            return [codes[:, (j - first) * PIECE : (j - first + 1) * PIECE] for j in range(first, last)]
+            return pick(tab[a][:].bitcast(U32), U32, name, first, last, tag)
 
-        v_codes = [pick_words(0, "v0_front", 0, 2)]
+        def pick_scales(a, name, first, last, tag=None):
+            return pick(tab_plane[:, a, :], U8, name, first, last, tag)
 
         w1_codes = held("w1_codes", [P, 2, M // 2], I32)
         nc.vector.tensor_copy(
@@ -116,14 +110,15 @@ def tile_list_spill_slot_advisor_kernel(
         )
         w2_raw = [held("w2_raw0", [P, PACK, 512], F32, tag="w1_raw")]
         nc.sync.dma_start(w2_raw[0][:], w2_rows[:, :, 0:512])
+        v_plane = [pick_scales(a, f"s{a}_first", 0, 1) for a in range(2)]
         w1_plane = held("w1_plane", [P, 2, M], U8)
         nc.vector.tensor_copy(
             w1_plane[:].rearrange("p a (t m) -> p a m t", t=PACK),
             w1_plane_raw[:].rearrange("p a (m t) -> p a m t", t=PACK),
         )
-        v_codes.append(pick_words(1, "v1_first", 0, 1) + pick_words(1, "v1_second", 1, 2))
+        v_codes = [pick_words(a, f"v{a}_first", 0, 1) for a in range(2)]
 
-        wgs_sb = held("wgs_sb", [P, PACK, S], F32, tag="w1_plane_raw")
+        wgs_sb = held("wgs_sb", [P, PACK, S], F32, tag="s0_first")
         wgs_rows = wgs.rearrange("(p t) s -> p t s", t=PACK)
         for span in (cols(0), cols(1), slice(2 * PIECE, S)):
             for q in (0, 2, 1, 3):
@@ -136,61 +131,52 @@ def tile_list_spill_slot_advisor_kernel(
         def quantize(codes, plane, grouped):
             nc.vector.quantize_mx(out=codes.bitcast(FP8X4), scales=plane, in_=grouped)
 
-        def quantize_w2(a, t0, t1, tag=None):
+        def quantize_w2(a, t0, t1, copy=nc.scalar.copy, tag=None):
             grouped = held(f"w2_grouped{a}{t0}", [P, t1 - t0, 128, PACK], BF16, tag=tag)
-            nc.scalar.copy(
+            copy(
                 grouped[:].rearrange("p t m j -> p m j t"),
                 w2_raw[a][:].rearrange("p j (m t) -> p m j t", t=PACK)[:, :, :, t0:t1],
             )
             span = slice(128 * t0, 128 * t1)
             quantize(w2_codes[a][:, span], w2_plane[a][:, span], grouped[:].rearrange("p t m j -> p (t m j)"))
 
-        e_codes = held("e_codes", [P, S], U32)
+        e_codes = []
         e_plane = held("e_plane", [P, S], U8)
 
-        def features(j):
-            th = ringed("th", [P, PACK, PIECE], F32)
-            banks = [psum.tile([P, PIECE], F32, name=f"pre{t}", tag="bank_a") for t in range(PACK)]
-            for a in range(2):
-                for t in range(PACK):
+        def features(j, codes_tag=None):
+            th = held(f"th{j}", [P, PACK, PIECE], F32, tag=f"th{j}")
+            e_rows = held(f"e_rows{j}", [P, PACK, PIECE], BF16)
+            for t in range(PACK):
+                bank = psum.tile([P, PIECE], F32, name=f"pre{t}", tag="bank_a")
+                for a in range(2):
                     for half in range(2):
                         c0 = half * 128
                         nc.tensor.matmul_mx(
-                            out=banks[t][:, c0 : c0 + 128],
+                            out=bank[:, c0 : c0 + 128],
                             lhsT=w1_codes[:, a, 64 * t : 64 * t + 64].bitcast(FP4X4),
                             lhsT_scale=w1_plane[:, a, 128 * t : 128 * t + 128],
                             rhs=v_codes[a][j][:, c0 : c0 + 128].bitcast(FP8X4),
-                            rhs_scale=v_plane[a][:, j * PIECE + c0 : j * PIECE + c0 + 128],
+                            rhs_scale=v_plane[a][j][:, c0 : c0 + 128],
                             start=(a == 0 and half == 0),
                             stop=(a == 1 and half == 1),
                         )
+                nc.scalar.activation(th[:, t, :], bank[:], ACT.Tanh, bias=b1_sb[:, t : t + 1])
             for t in range(PACK):
-                nc.scalar.activation(th[:, t, :], banks[t][:], ACT.Tanh, bias=b1_sb[:, t : t + 1])
+                nc.scalar.activation(e_rows[:, t, :], th[:, t, :], ACT.Copy, scale=gain_sb[:, t : t + 1])
             e_grouped = held(f"e_grouped{j}", [P, PIECE, PACK], BF16)
-            if j == 0:
-                nc.vector.tensor_tensor(
-                    e_grouped[:].rearrange("p (c i) t -> p c t i", i=4),
-                    th[:].rearrange("p t (c i) -> p c t i", i=4),
-                    gain_sb[:].unsqueeze(1).unsqueeze(3).to_broadcast([P, PIECE // 4, PACK, 4]),
-                    ALU.mult,
-                )
-            else:
-                e_rows = held(f"e_rows{j}", [P, PACK, PIECE], BF16)
-                for t in range(PACK):
-                    nc.scalar.activation(e_rows[:, t, :], th[:, t, :], ACT.Copy, scale=gain_sb[:, t : t + 1])
-                interleave(nc.scalar.copy, e_grouped[:], e_rows[:])
-            quantize(e_codes[:, cols(j)], e_plane[:, cols(j)], e_grouped[:].rearrange("p n t -> p (n t)"))
+            interleave(nc.scalar.copy, e_grouped[:], e_rows[:])
+            e_codes.append(held(f"e_codes{j}", [P, PIECE], U32, tag=codes_tag))
+            quantize(e_codes[j][:], e_plane[:, cols(j)], e_grouped[:].rearrange("p n t -> p (n t)"))
 
-        def costs(a, slots, span, dst):
-            width = span.stop - span.start
-            bank = psum.tile([P, len(slots), width], F32, name="bank_b", tag="bank_b")
-            for u, t in enumerate(slots):
+        def costs(a, parts, dst):
+            bank = psum.tile([P, len(parts), PIECE], F32, name="bank_b", tag="bank_b")
+            for u, (t, j) in enumerate(parts):
                 nc.tensor.matmul_mx(
                     out=bank[:, u, :],
                     lhsT=w2_codes[a][:, 128 * t : 128 * t + 128].bitcast(FP8X4),
                     lhsT_scale=w2_plane[a][:, 128 * t : 128 * t + 128],
-                    rhs=e_codes[:, span].bitcast(FP8X4),
-                    rhs_scale=e_plane[:, span],
+                    rhs=e_codes[j][:].bitcast(FP8X4),
+                    rhs_scale=e_plane[:, cols(j)],
                     start=True,
                     stop=True,
                 )
@@ -199,46 +185,56 @@ def tile_list_spill_slot_advisor_kernel(
         def put(t, offsets, values, span):
             nc.vector.tensor_tensor(pages[t][:].indirect(offsets), values, wgs_sb[:, t, span], ALU.mult)
 
-        quantize_w2(0, 0, 2)
         features(0)
-        v_codes[0].extend(pick_words(0, "v0_back", 2, PIECES, tag="v1_first"))
-        v_codes[1].extend(pick_words(1, "v1_back", 2, PIECES, tag="e_grouped0"))
-        quantize_w2(0, 2, PACK)
+        quantize_w2(0, 0, 1, nc.vector.tensor_copy, tag="th0")
+        quantize_w2(0, 1, 3, tag="e_rows0")
+        for a in range(2):
+            v_codes[a].extend(pick_words(a, f"v{a}_second", 1, 2))
+        v_codes[1].extend(pick_words(1, "v1_back", 2, PIECES))
+        s_second = held("s_second", [P, 2, PIECE], U8, tag="v1_first")
+        for a in range(2):
+            nc.vector.tensor_copy(s_second[:, a, :], tab_plane[:, a, :].indirect(idx[:, entries(1)]))
+            v_plane[a].append(s_second[:, a, :])
+        v_codes[0].extend(pick_words(0, "v0_back", 2, PIECES, tag="s1_first"))
+        v_plane[0].extend(pick_scales(0, "s0_back", 2, PIECES, tag="e_grouped0"))
+        for t, tag in ((2, "th0"), (3, "e_rows0")):
+            pages.append(held(f"page{t}", [P, T2], F32, tag=tag))
+            for c0 in range(0, T2, 512):
+                nc.gpsimd.memset(pages[t][:, c0 : c0 + 512], 0.0)
         w2_raw.append(held("w2_raw1", [P, PACK, 512], F32, tag="v1_second"))
         for j in range(PIECES):
-            h0 = held(f"h0_{j}", [P, PACK, PIECE], F32)
-            costs(0, (0,), cols(j), h0[:, 0:1, :])
-            costs(0, (1, 2), cols(j), h0[:, 1:3, :])
+            h0 = [held(f"h0_{j}{t}", [P, 1, PIECE], F32) for t in range(PACK)]
             for t in range(PACK - 1):
-                put(t, idx2[:, entries(j)], h0[:, t, :], cols(j))
-            if j + 1 < PIECES:
-                features(j + 1)
-                h03 = held(f"h03_{j}", [P, 1, PIECE], F32, tag=f"e_rows{j + 1}")[:]
-            else:
-                h03 = h0[:, 3:4, :]
+                costs(0, [(t, j)], h0[t][:])
+            put(0, idx2[:, entries(j)], h0[0][:, 0, :], cols(j))
             if j == 0:
+                quantize_w2(0, 3, PACK, tag="h0_00")
+            costs(0, [(PACK - 1, j)], h0[PACK - 1][:])
+            put(1, idx2[:, entries(j)], h0[1][:, 0, :], cols(j))
+            if 0 < j < PIECES - 1:
+                features(j + 1, f"h0_{j}0")
+            put(2, idx2[:, entries(j)], h0[2][:, 0, :], cols(j))
+            if j == 0:
+                v_plane[1].extend(pick_scales(1, "s1_back", 2, PIECES, tag="h0_00"))
+                features(1, "h0_01")
                 nc.sync.dma_start(w2_raw[1][:], w2_rows[:, :, 512:1024])
-            costs(0, (PACK - 1,), cols(j), h03)
-            put(PACK - 1, idx2[:, entries(j)], h03[:, 0, :], cols(j))
+            put(PACK - 1, idx2[:, entries(j)], h0[PACK - 1][:, 0, :], cols(j))
         cap0 = held("cap0", [P, PACK, PICKS], F32, tag="tab0")
         nc.sync.dma_start(cap0[:], cap_rows[0])
-        w3_codes = held("w3_codes", [P, 2, N], I32, tag="v_plane1")
+        w3_codes = held("w3_codes", [P, 2, N], I32, tag="tab_plane")
         nc.sync.dma_start(w3_codes[:], w3_words.rearrange("a p c i -> p a (c i)").bitcast(I32))
-        quantize_w2(1, 0, PACK, tag=f"e_rows{PIECES - 1}")
+        for t in (0, 2):
+            quantize_w2(1, t, t + 2, tag=f"h0_{PIECES - 1}{PACK - 1}")
 
-        h1 = [held(f"h1{t}", [P, 1, S], F32) for t in range(PACK)]
+        h1 = [held(f"h1{t}", [P, PIECES, PIECE], F32) for t in range(PACK)]
         for t in range(PACK):
             for half in range(2):
-                span = slice(512 * half, 512 * half + 512)
-                costs(1, (t,), span, h1[t][:, :, span])
+                costs(1, [(t, 2 * half), (t, 2 * half + 1)], h1[t][:, 2 * half : 2 * half + 2, :])
 
-        w3_plane = held("w3_plane", [P, 2, N], U8, tag="e_rows1")
+        w3_plane = held("w3_plane", [P, 2, N], U8, tag="h0_03")
         nc.gpsimd.memset(w3_plane[:].rearrange("p a c -> p (a c)").bitcast(I32), 0)
         for q in range(4):
-            nc.sync.dma_start(
-                w3_plane[32 * q : 32 * q + 4, :, :].bitcast(I32),
-                w3_scales[:, 4 * q : 4 * q + 4, :].rearrange("a r c -> r a c").bitcast(I32),
-            )
+            load_scale_rows(nc.sync, w3_plane, w3_scales, q)
 
         x = held("x", [P, PACK, PICKS], F32)
         z_rows0 = held("z_rows0", [P, PACK, PICKS], BF16, tag="w1_raw")
@@ -246,62 +242,94 @@ def tile_list_spill_slot_advisor_kernel(
             nc.vector.tensor_copy(x[:, t, :], pages[t][:].indirect(idx3[:]))
         for t in range(0, PACK, 2):
             nc.vector.tensor_tensor(z_rows0[:, t : t + 2, :], x[:, t : t + 2, :], cap0[:, t : t + 2, :], ALU.min)
-        z_grouped0 = held("z_grouped0", [P, PICKS, PACK], BF16, tag="tab1")
+        z_grouped0 = held("z_grouped0", [P, PICKS, PACK], BF16)
         interleave(nc.scalar.copy, z_grouped0[:], z_rows0[:])
         cap1 = held("cap1", [P, PACK, PICKS], F32, tag="tab0")
         nc.sync.dma_start(cap1[:], cap_rows[1])
 
         z_plane = [held(f"z_plane{a}", [P, PICKS], U8) for a in range(2)]
         for t in range(PACK - 1):
-            put(t, idx2[:], h1[t][:, 0, :], slice(0, S))
+            put(t, idx2[:], h1[t][:].rearrange("p j c -> p (j c)"), slice(0, S))
         z_codes = [held("z_codes0", [P, PICKS], U32, tag="h12"), held("z_codes1", [P, PICKS], U32)]
         quantize(z_codes[0][:], z_plane[0][:], z_grouped0[:].rearrange("p n t -> p (n t)"))
-        put(PACK - 1, idx2[:], h1[PACK - 1][:, 0, :], slice(0, S))
+        put(PACK - 1, idx2[:], h1[PACK - 1][:].rearrange("p j c -> p (j c)"), slice(0, S))
 
         out_rows = out.rearrange("(c p) m -> p c m", p=P)
-        spans = [cols(j) for j in range(PIECES - 1)] + [slice(768, 896), slice(896, 1024)]
+        last = PIECES - 1
+        spans = [cols(j) for j in range(last)] + [slice(768, 896), slice(896, 1024)]
 
         def score_pass(a, banks, span):
             for c in range(4):
                 nc.tensor.matmul_mx(
-                    out=banks[c][:],
+                    out=banks[c // 2][:, c % 2, :],
                     lhsT=w3_codes[:, a, 128 * c : 128 * c + 128].bitcast(FP8X4),
                     lhsT_scale=w3_plane[:, a, 128 * c : 128 * c + 128],
                     rhs=z_codes[a][:, span].bitcast(FP8X4),
                     rhs_scale=z_plane[a][:, span],
-                    start=(a == 0),
-                    stop=(a == 1),
+                    start=(a == 0 and c % 2 == 0),
+                    stop=(a == 1 and c % 2 == 1),
                 )
 
         def open_scores(n):
             span = spans[n]
             tag = "bank_a" if n % 2 == 0 else "bank_b"
-            banks = [psum.tile([P, span.stop - span.start], F32, name=f"acc{c}", tag=tag) for c in range(4)]
+            banks = [psum.tile([P, 2, span.stop - span.start], F32, name=f"acc{c}", tag=tag) for c in range(2)]
             score_pass(0, banks, span)
             return banks
 
-        opened = [open_scores(0), open_scores(1)]
-        for t in range(2):
-            nc.vector.tensor_copy(x[:, t, :], pages[t][:].indirect(idx3[:]))
-        for n, span in enumerate(spans):
-            width = span.stop - span.start
-            if n < PIECES:
-                for t in range(2, PACK):
-                    nc.vector.tensor_copy(x[:, t, cols(n)], pages[t][:].indirect(idx3[:, entries(n)]))
-            z_grouped = held(f"z_grouped_p{n}", [P, width, PACK], BF16)
+        def fetch(j, slots, tag):
+            picked = held(f"x{j}{slots[0]}", [P, len(slots), PIECE], F32, tag=tag)
+            for u, t in enumerate(slots):
+                nc.vector.tensor_copy(picked[:, u, :], pages[t][:].indirect(idx3[:, entries(j)]))
+            return picked
+
+        def fetch_pairs(j):
+            return [fetch(j, (0, 1), "x_low"), fetch(j, (2, 3), "x_high")]
+
+        def limit(j, pairs):
+            z_rows = held(f"z_rows_p{j}", [P, PACK, PIECE], BF16, tag="z_rows_p")
+            for u in range(2):
+                slots = slice(2 * u, 2 * u + 2)
+                nc.vector.tensor_tensor(z_rows[:, slots, :], pairs[u][:], cap1[:, slots, cols(j)], ALU.min)
+            z_grouped = held(f"z_grouped_p{j}", [P, PIECE, PACK], BF16)
+            interleave(nc.scalar.copy, z_grouped[:], z_rows[:])
+            return z_grouped
+
+        def limit_last(picked, half, tag):
+            span = spans[last + half]
+            z_grouped = held(f"z_grouped_last{half}", [P, 128, PACK], BF16, tag=tag)
             nc.vector.tensor_tensor(
                 z_grouped[:].rearrange("p (c i) t -> p c t i", i=4),
-                x[:, :, span].rearrange("p t (c i) -> p c t i", i=4),
+                picked[:, :, 128 * half : 128 * half + 128].rearrange("p t (c i) -> p c t i", i=4),
                 cap1[:, :, span].rearrange("p t (c i) -> p c t i", i=4),
                 ALU.min,
             )
+            return z_grouped
+
+        def scores(n, z_grouped):
+            span = spans[n]
             quantize(z_codes[1][:, span], z_plane[1][:, span], z_grouped[:].rearrange("p n t -> p (n t)"))
             score_pass(1, opened[n], span)
-            staged = held(f"staged{n}", [P, 4, width], F32, tag=f"h0_{n}" if n < PIECES else "h10")
-            for c in range(4):
-                copy = nc.vector.tensor_copy if (n >= PIECES - 1 and c < 2) else nc.scalar.copy
-                copy(staged[:, c, :], opened[n][c][:])
+
+        def store(n):
+            span = spans[n]
             for pair in range(2):
-                nc.sync.dma_start(out_rows[:, 2 * pair : 2 * pair + 2, span], staged[:, 2 * pair : 2 * pair + 2, :])
-            if n + 2 < len(spans):
-                opened.append(open_scores(n + 2))
+                staged = held(f"staged{n}{pair}", [P, 2, span.stop - span.start], F32)
+                copy = nc.vector.tensor_copy if (n >= last and pair == 0) else nc.scalar.copy
+                copy(staged[:], opened[n][pair][:])
+                nc.sync.dma_start(out_rows[:, 2 * pair : 2 * pair + 2, span], staged[:])
+
+        opened = [open_scores(n) for n in range(PIECES)]
+        picked = fetch_pairs(0)
+        for n in range(last):
+            z_grouped = limit(n, picked)
+            picked = fetch_pairs(n + 1) if n + 1 < last else fetch(last, (0, 1, 2, 3), "x_low")
+            scores(n, z_grouped)
+            store(n)
+            if n == 0:
+                opened.append(open_scores(PIECES))
+        halves = [limit_last(picked, 0, "z_rows_p"), limit_last(picked, 1, None)]
+        for n in range(2):
+            scores(last + n, halves[n])
+        for n in range(2):
+            store(last + n)

@@ -51,15 +51,26 @@ def tile_list_spill_slot_advisor_kernel(
                 src.rearrange("p t (c i) -> p c t i", i=4),
             )
 
-        tab_plane = held("tab_plane", [P, 2, T], U8)
+        tab_plane = held("tab_plane", [P, T], U8)
         w1_plane_raw = held("w1_plane_raw", [P, 2, M], U8)
-        pages = [held(f"page{t}", [P, T2], F32) for t in range(2)]
+        v_plane = [held(f"v_plane{a}", [P, S], U8) for a in range(2)]
+        pages = []
+
+        def zeroed_page(tag):
+            page = held(f"page{len(pages)}", [P, T2], F32, tag=tag)
+            for c0 in range(0, T2, 512):
+                nc.gpsimd.memset(page[:, c0 : c0 + 512], 0.0)
+            pages.append(page)
+
         nc.gpsimd.memset(w1_plane_raw[:].rearrange("p a c -> p (a c)").bitcast(I32), 0)
-        nc.vector.memset(tab_plane[:].rearrange("p a c -> p (a c)").bitcast(I32), 0)
+        for q in range(4):
+            nc.vector.memset(tab_plane[32 * q : 32 * q + 24, :].bitcast(I32), 0)
+        for a in range(2):
+            nc.vector.memset(v_plane[a][96:128, :].bitcast(I32), 0)
+
         warm = held("warm", [P, 8], F32)
         nc.vector.memset(warm[:, 0:1], 0.0)
-        for t in range(2):
-            nc.vector.memset(pages[t][:], 0.0)
+        nc.scalar.activation(warm[:, 1:2], warm[:, 0:1], ACT.Tanh)
 
         idx = lists.tile([P, S // 16], U16, name="idx")
         idx2 = lists.tile([P, S // 16], U16, name="idx2")
@@ -67,15 +78,16 @@ def tile_list_spill_slot_advisor_kernel(
         b1_sb = held("b1_sb", [P, PACK], F32)
         gain_sb = held("gain_sb", [P, PACK], F32)
         nc.sync.dma_start(idx[:], offs)
+        for q in range(4):
+            nc.sync.dma_start(
+                tab_plane[32 * q + 24 : 32 * q + 32, :].bitcast(I32), tab_scales[:, 4 * q : 4 * q + 4, :].bitcast(I32)
+            )
         nc.sync.dma_start(idx2[:], offs2)
         nc.sync.dma_start(idx3[:], offs3)
-        nc.sync.dma_start(b1_sb[:], b1.rearrange("(p t) -> p t", t=PACK))
-        nc.sync.dma_start(gain_sb[:], gain.rearrange("(p t) -> p t", t=PACK))
-        tab = [held("tab0", [P, T], I32)]
+        tab = [held(f"tab{a}", [P, T], I32) for a in range(2)]
         w1_raw = held("w1_raw", [P, 2, M // 2], I32)
-        nc.sync.dma_start(w1_raw[:], w1_words.rearrange("a p b -> p a b").bitcast(I32))
         nc.sync.dma_start(tab[0][:], tab_words[0].rearrange("p t i -> p (t i)").bitcast(I32))
-        w2_rows = w2.rearrange("(p j) r -> p j r", j=PACK)
+        nc.sync.dma_start(w1_raw[:], w1_words.rearrange("a p b -> p a b").bitcast(I32))
 
         def load_scale_rows(queue, plane, scales, q):
             queue.dma_start(
@@ -84,41 +96,44 @@ def tile_list_spill_slot_advisor_kernel(
             )
 
         for q in range(4):
-            load_scale_rows(nc.sync, tab_plane, tab_scales, q)
-        for q in range(4):
-            load_scale_rows(nc.gpsimd if q < 2 else nc.sync, w1_plane_raw, w1_scales, q)
-        nc.scalar.activation(warm[:, 1:2], warm[:, 0:1], ACT.Tanh)
-        tab.append(held("tab1", [P, T], I32, tag="warm"))
+            load_scale_rows(nc.sync, w1_plane_raw, w1_scales, q)
         nc.sync.dma_start(tab[1][:], tab_words[1].rearrange("p t i -> p (t i)").bitcast(I32))
+        nc.sync.dma_start(b1_sb[:], b1.rearrange("(p t) -> p t", t=PACK))
+        nc.sync.dma_start(gain_sb[:], gain.rearrange("(p t) -> p t", t=PACK))
+        w2_rows = w2.rearrange("(p j) r -> p j r", j=PACK)
+        zeroed_page("warm")
 
-        def pick(window, dtype, name, first, last, tag=None):
-            picked = held(name, [P, (last - first) * PIECE], dtype, tag=tag)
-            offsets = idx[:, first * LIST_COLS : last * LIST_COLS]
-            nc.vector.tensor_copy(picked[:], window.indirect(offsets))
-            return [picked[:, (j - first) * PIECE : (j - first + 1) * PIECE] for j in range(first, last)]
+        picked_scales = held("picked_scales", [P, S], U8)
+        nc.vector.tensor_copy(picked_scales[:], tab_plane[:].indirect(idx[:]))
+        for a in range(2):
+            shift = 24 + 4 * a
+            nc.sync.dma_start(v_plane[a][0 : P - shift, :].bitcast(I32), picked_scales[shift:P, :].bitcast(I32))
 
         def pick_words(a, name, first, last, tag=None):
-            return pick(tab[a][:].bitcast(U32), U32, name, first, last, tag)
+            codes = held(name, [P, (last - first) * PIECE], U32, tag=tag)
+            offsets = idx[:, first * LIST_COLS : last * LIST_COLS]
+            nc.vector.tensor_copy(codes[:], tab[a][:].bitcast(U32).indirect(offsets))
+            return [codes[:, (j - first) * PIECE : (j - first + 1) * PIECE] for j in range(first, last)]
 
-        def pick_scales(a, name, first, last, tag=None):
-            return pick(tab_plane[:, a, :], U8, name, first, last, tag)
 
         w1_codes = held("w1_codes", [P, 2, M // 2], I32)
         nc.vector.tensor_copy(
             w1_codes[:].bitcast(U16).rearrange("p a (t m) -> p a m t", t=PACK),
             w1_raw[:].bitcast(U16).rearrange("p a (m t) -> p a m t", t=PACK),
         )
-        w2_raw = [held("w2_raw0", [P, PACK, 512], F32, tag="w1_raw")]
+        w2_raw = [held("w2_raw0", [P, PACK, 512], F32, tag="tab_plane")]
         nc.sync.dma_start(w2_raw[0][:], w2_rows[:, :, 0:512])
-        v_plane = [pick_scales(a, f"s{a}_first", 0, 1) for a in range(2)]
+        v_codes = [pick_words(0, "v0_front", 0, 2)]
         w1_plane = held("w1_plane", [P, 2, M], U8)
         nc.vector.tensor_copy(
             w1_plane[:].rearrange("p a (t m) -> p a m t", t=PACK),
             w1_plane_raw[:].rearrange("p a (m t) -> p a m t", t=PACK),
         )
-        v_codes = [pick_words(a, f"v{a}_first", 0, 1) for a in range(2)]
+        v_codes.append(pick_words(1, "v1_first", 0, 1))
 
-        wgs_sb = held("wgs_sb", [P, PACK, S], F32, tag="s0_first")
+        zeroed_page("w1_raw")
+        zeroed_page("w1_plane_raw")
+        wgs_sb = held("wgs_sb", [P, PACK, S], F32, tag="picked_scales")
         wgs_rows = wgs.rearrange("(p t) s -> p t s", t=PACK)
         for span in (cols(0), cols(1), slice(2 * PIECE, S)):
             for q in (0, 2, 1, 3):
@@ -145,7 +160,6 @@ def tile_list_spill_slot_advisor_kernel(
 
         def features(j, codes_tag=None):
             th = held(f"th{j}", [P, PACK, PIECE], F32, tag=f"th{j}")
-            e_rows = held(f"e_rows{j}", [P, PACK, PIECE], BF16)
             for t in range(PACK):
                 bank = psum.tile([P, PIECE], F32, name=f"pre{t}", tag="bank_a")
                 for a in range(2):
@@ -156,15 +170,24 @@ def tile_list_spill_slot_advisor_kernel(
                             lhsT=w1_codes[:, a, 64 * t : 64 * t + 64].bitcast(FP4X4),
                             lhsT_scale=w1_plane[:, a, 128 * t : 128 * t + 128],
                             rhs=v_codes[a][j][:, c0 : c0 + 128].bitcast(FP8X4),
-                            rhs_scale=v_plane[a][j][:, c0 : c0 + 128],
+                            rhs_scale=v_plane[a][:, j * PIECE + c0 : j * PIECE + c0 + 128],
                             start=(a == 0 and half == 0),
                             stop=(a == 1 and half == 1),
                         )
                 nc.scalar.activation(th[:, t, :], bank[:], ACT.Tanh, bias=b1_sb[:, t : t + 1])
-            for t in range(PACK):
-                nc.scalar.activation(e_rows[:, t, :], th[:, t, :], ACT.Copy, scale=gain_sb[:, t : t + 1])
             e_grouped = held(f"e_grouped{j}", [P, PIECE, PACK], BF16)
-            interleave(nc.scalar.copy, e_grouped[:], e_rows[:])
+            if j == 0:
+                nc.vector.tensor_tensor(
+                    e_grouped[:].rearrange("p (c i) t -> p c t i", i=4),
+                    th[:].rearrange("p t (c i) -> p c t i", i=4),
+                    gain_sb[:].unsqueeze(1).unsqueeze(3).to_broadcast([P, PIECE // 4, PACK, 4]),
+                    ALU.mult,
+                )
+            else:
+                e_rows = held(f"e_rows{j}", [P, PACK, PIECE], BF16)
+                for t in range(PACK):
+                    nc.scalar.activation(e_rows[:, t, :], th[:, t, :], ACT.Copy, scale=gain_sb[:, t : t + 1])
+                interleave(nc.scalar.copy, e_grouped[:], e_rows[:])
             e_codes.append(held(f"e_codes{j}", [P, PIECE], U32, tag=codes_tag))
             quantize(e_codes[j][:], e_plane[:, cols(j)], e_grouped[:].rearrange("p n t -> p (n t)"))
 
@@ -186,42 +209,31 @@ def tile_list_spill_slot_advisor_kernel(
             nc.vector.tensor_tensor(pages[t][:].indirect(offsets), values, wgs_sb[:, t, span], ALU.mult)
 
         features(0)
-        quantize_w2(0, 0, 1, nc.vector.tensor_copy, tag="th0")
-        quantize_w2(0, 1, 3, tag="e_rows0")
-        for a in range(2):
-            v_codes[a].extend(pick_words(a, f"v{a}_second", 1, 2))
-        v_codes[1].extend(pick_words(1, "v1_back", 2, PIECES))
-        s_second = held("s_second", [P, 2, PIECE], U8, tag="v1_first")
-        for a in range(2):
-            nc.vector.tensor_copy(s_second[:, a, :], tab_plane[:, a, :].indirect(idx[:, entries(1)]))
-            v_plane[a].append(s_second[:, a, :])
-        v_codes[0].extend(pick_words(0, "v0_back", 2, PIECES, tag="s1_first"))
-        v_plane[0].extend(pick_scales(0, "s0_back", 2, PIECES, tag="e_grouped0"))
-        for t, tag in ((2, "th0"), (3, "e_rows0")):
-            pages.append(held(f"page{t}", [P, T2], F32, tag=tag))
-            for c0 in range(0, T2, 512):
-                nc.gpsimd.memset(pages[t][:, c0 : c0 + 512], 0.0)
+        quantize_w2(0, 0, 2, tag="v1_first")
+        v_codes[1].extend(pick_words(1, "v1_second", 1, 2))
+        v_codes[0].extend(pick_words(0, "v0_back", 2, PIECES))
+        v_codes[1].extend(pick_words(1, "v1_back", 2, PIECES, tag="e_grouped0"))
+        zeroed_page("v1_first")
         w2_raw.append(held("w2_raw1", [P, PACK, 512], F32, tag="v1_second"))
         for j in range(PIECES):
             h0 = [held(f"h0_{j}{t}", [P, 1, PIECE], F32) for t in range(PACK)]
-            for t in range(PACK - 1):
+            for t in range(2):
                 costs(0, [(t, j)], h0[t][:])
+            if j == 0:
+                quantize_w2(0, 2, PACK, tag="th0")
             put(0, idx2[:, entries(j)], h0[0][:, 0, :], cols(j))
-            if j == 0:
-                quantize_w2(0, 3, PACK, tag="h0_00")
-            costs(0, [(PACK - 1, j)], h0[PACK - 1][:])
+            for t in range(2, PACK):
+                costs(0, [(t, j)], h0[t][:])
             put(1, idx2[:, entries(j)], h0[1][:, 0, :], cols(j))
-            if 0 < j < PIECES - 1:
-                features(j + 1, f"h0_{j}0")
             put(2, idx2[:, entries(j)], h0[2][:, 0, :], cols(j))
+            if j + 1 < PIECES:
+                features(j + 1, f"h0_{j}1")
             if j == 0:
-                v_plane[1].extend(pick_scales(1, "s1_back", 2, PIECES, tag="h0_00"))
-                features(1, "h0_01")
                 nc.sync.dma_start(w2_raw[1][:], w2_rows[:, :, 512:1024])
             put(PACK - 1, idx2[:, entries(j)], h0[PACK - 1][:, 0, :], cols(j))
         cap0 = held("cap0", [P, PACK, PICKS], F32, tag="tab0")
         nc.sync.dma_start(cap0[:], cap_rows[0])
-        w3_codes = held("w3_codes", [P, 2, N], I32, tag="tab_plane")
+        w3_codes = held("w3_codes", [P, 2, N], I32, tag="v_plane1")
         nc.sync.dma_start(w3_codes[:], w3_words.rearrange("a p c i -> p a (c i)").bitcast(I32))
         for t in (0, 2):
             quantize_w2(1, t, t + 2, tag=f"h0_{PIECES - 1}{PACK - 1}")
@@ -237,7 +249,7 @@ def tile_list_spill_slot_advisor_kernel(
             load_scale_rows(nc.sync, w3_plane, w3_scales, q)
 
         x = held("x", [P, PACK, PICKS], F32)
-        z_rows0 = held("z_rows0", [P, PACK, PICKS], BF16, tag="w1_raw")
+        z_rows0 = held("z_rows0", [P, PACK, PICKS], BF16, tag="tab_plane")
         for t in range(PACK):
             nc.vector.tensor_copy(x[:, t, :], pages[t][:].indirect(idx3[:]))
         for t in range(0, PACK, 2):

@@ -132,12 +132,6 @@ def tile_list_spill_slot_advisor_kernel(
         v_codes.append(pick_words(1, "v1_first", 0, 1))
 
         zeroed_page("w1_raw")
-        zeroed_page("w1_plane_raw")
-        wgs_sb = held("wgs_sb", [P, PACK, S], F32, tag="picked_scales")
-        wgs_rows = wgs.rearrange("(p t) s -> p t s", t=PACK)
-        for span in (cols(0), cols(1), slice(2 * PIECE, S)):
-            for q in (0, 2, 1, 3):
-                nc.sync.dma_start(wgs_sb[32 * q : 32 * q + 32, :, span], wgs_rows[:, :, span])
         cap_rows = cap.rearrange("(a p t) m -> a p t m", a=2, t=PACK)
 
         w2_codes = [held(f"w2_codes{a}", [P, 512], U32) for a in range(2)]
@@ -158,38 +152,57 @@ def tile_list_spill_slot_advisor_kernel(
         e_codes = []
         e_plane = held("e_plane", [P, S], U8)
 
-        def features(j, codes_tag=None):
-            th = held(f"th{j}", [P, PACK, PIECE], F32, tag=f"th{j}")
+        def first_product(j, bank_cols, t, halves):
+            for a in range(2):
+                for n, half in enumerate(halves):
+                    c0 = half * 128
+                    nc.tensor.matmul_mx(
+                        out=bank_cols[:, 128 * n : 128 * n + 128],
+                        lhsT=w1_codes[:, a, 64 * t : 64 * t + 64].bitcast(FP4X4),
+                        lhsT_scale=w1_plane[:, a, 128 * t : 128 * t + 128],
+                        rhs=v_codes[a][j][:, c0 : c0 + 128].bitcast(FP8X4),
+                        rhs_scale=v_plane[a][:, j * PIECE + c0 : j * PIECE + c0 + 128],
+                        start=(a == 0 and n == 0),
+                        stop=(a == 1 and n == len(halves) - 1),
+                    )
+
+        def squash(j):
+            th = held(f"th{j}", [P, PACK, PIECE], F32)
             for t in range(PACK):
                 bank = psum.tile([P, PIECE], F32, name=f"pre{t}", tag="bank_a")
-                for a in range(2):
-                    for half in range(2):
-                        c0 = half * 128
-                        nc.tensor.matmul_mx(
-                            out=bank[:, c0 : c0 + 128],
-                            lhsT=w1_codes[:, a, 64 * t : 64 * t + 64].bitcast(FP4X4),
-                            lhsT_scale=w1_plane[:, a, 128 * t : 128 * t + 128],
-                            rhs=v_codes[a][j][:, c0 : c0 + 128].bitcast(FP8X4),
-                            rhs_scale=v_plane[a][:, j * PIECE + c0 : j * PIECE + c0 + 128],
-                            start=(a == 0 and half == 0),
-                            stop=(a == 1 and half == 1),
-                        )
+                first_product(j, bank[:], t, (0, 1))
                 nc.scalar.activation(th[:, t, :], bank[:], ACT.Tanh, bias=b1_sb[:, t : t + 1])
+            return th
+
+        def features(j, th, codes_tag):
+            e_rows = held(f"e_rows{j}", [P, PACK, PIECE], BF16)
+            for t in range(PACK):
+                nc.scalar.activation(e_rows[:, t, :], th[:, t, :], ACT.Copy, scale=gain_sb[:, t : t + 1])
             e_grouped = held(f"e_grouped{j}", [P, PIECE, PACK], BF16)
-            if j == 0:
+            interleave(nc.scalar.copy, e_grouped[:], e_rows[:])
+            e_codes.append(held(f"e_codes{j}", [P, PIECE], U32, tag=codes_tag))
+            quantize(e_codes[j][:], e_plane[:, cols(j)], e_grouped[:].rearrange("p n t -> p (n t)"))
+
+        def first_features():
+            e_codes.append(held("e_codes0", [P, PIECE], U32))
+            for half in range(2):
+                th = held(f"th0{half}", [P, PACK, 128], F32)
+                for pair in range(2):
+                    bank = psum.tile([P, 2, 128], F32, name=f"pre{pair}", tag="bank_a")
+                    for u in range(2):
+                        first_product(0, bank[:, u, :], 2 * pair + u, (half,))
+                    for u in range(2):
+                        t = 2 * pair + u
+                        nc.scalar.activation(th[:, t, :], bank[:, u, :], ACT.Tanh, bias=b1_sb[:, t : t + 1])
+                e_grouped = held(f"e_grouped0{half}", [P, 128, PACK], BF16)
                 nc.vector.tensor_tensor(
                     e_grouped[:].rearrange("p (c i) t -> p c t i", i=4),
                     th[:].rearrange("p t (c i) -> p c t i", i=4),
-                    gain_sb[:].unsqueeze(1).unsqueeze(3).to_broadcast([P, PIECE // 4, PACK, 4]),
+                    gain_sb[:].unsqueeze(1).unsqueeze(3).to_broadcast([P, 128 // 4, PACK, 4]),
                     ALU.mult,
                 )
-            else:
-                e_rows = held(f"e_rows{j}", [P, PACK, PIECE], BF16)
-                for t in range(PACK):
-                    nc.scalar.activation(e_rows[:, t, :], th[:, t, :], ACT.Copy, scale=gain_sb[:, t : t + 1])
-                interleave(nc.scalar.copy, e_grouped[:], e_rows[:])
-            e_codes.append(held(f"e_codes{j}", [P, PIECE], U32, tag=codes_tag))
-            quantize(e_codes[j][:], e_plane[:, cols(j)], e_grouped[:].rearrange("p n t -> p (n t)"))
+                span = slice(128 * half, 128 * half + 128)
+                quantize(e_codes[0][:, span], e_plane[:, span], e_grouped[:].rearrange("p n t -> p (n t)"))
 
         def costs(a, parts, dst):
             bank = psum.tile([P, len(parts), PIECE], F32, name="bank_b", tag="bank_b")
@@ -208,26 +221,36 @@ def tile_list_spill_slot_advisor_kernel(
         def put(t, offsets, values, span):
             nc.vector.tensor_tensor(pages[t][:].indirect(offsets), values, wgs_sb[:, t, span], ALU.mult)
 
-        features(0)
-        quantize_w2(0, 0, 2, tag="v1_first")
+        first_features()
+        wgs_sb = held("wgs_sb", [P, PACK, S], F32, tag="w1_plane_raw")
+        wgs_rows = wgs.rearrange("(p t) s -> p t s", t=PACK)
+        for span in (cols(0), cols(1), slice(2 * PIECE, S)):
+            for q in (0, 2, 1, 3):
+                nc.sync.dma_start(wgs_sb[32 * q : 32 * q + 32, :, span], wgs_rows[:, :, span])
+        quantize_w2(0, 0, 1, nc.vector.tensor_copy, tag="th00")
+        quantize_w2(0, 1, 2, tag="e_grouped00")
         v_codes[1].extend(pick_words(1, "v1_second", 1, 2))
-        v_codes[0].extend(pick_words(0, "v0_back", 2, PIECES))
-        v_codes[1].extend(pick_words(1, "v1_back", 2, PIECES, tag="e_grouped0"))
+        v_codes[0].extend(pick_words(0, "v0_back", 2, PIECES, tag="picked_scales"))
+        v_codes[1].extend(pick_words(1, "v1_back", 2, PIECES, tag="e_grouped01"))
         zeroed_page("v1_first")
+        zeroed_page("e_grouped00")
         w2_raw.append(held("w2_raw1", [P, PACK, 512], F32, tag="v1_second"))
+        squashed = []
         for j in range(PIECES):
             h0 = [held(f"h0_{j}{t}", [P, 1, PIECE], F32) for t in range(PACK)]
             for t in range(2):
                 costs(0, [(t, j)], h0[t][:])
             if j == 0:
-                quantize_w2(0, 2, PACK, tag="th0")
+                quantize_w2(0, 2, PACK, tag="th01")
             put(0, idx2[:, entries(j)], h0[0][:, 0, :], cols(j))
             for t in range(2, PACK):
                 costs(0, [(t, j)], h0[t][:])
             put(1, idx2[:, entries(j)], h0[1][:, 0, :], cols(j))
             put(2, idx2[:, entries(j)], h0[2][:, 0, :], cols(j))
             if j + 1 < PIECES:
-                features(j + 1, f"h0_{j}1")
+                features(j + 1, squashed.pop() if j > 0 else squash(1), f"h0_{j}1")
+            if j + 2 < PIECES:
+                squashed.append(squash(j + 2))
             if j == 0:
                 nc.sync.dma_start(w2_raw[1][:], w2_rows[:, :, 512:1024])
             put(PACK - 1, idx2[:, entries(j)], h0[PACK - 1][:, 0, :], cols(j))

@@ -68,9 +68,10 @@ def tile_list_spill_slot_advisor_kernel(
         for a in range(2):
             nc.vector.memset(v_plane[a][96:128, :].bitcast(I32), 0)
 
-        warm = held("warm", [P, 8], F32)
-        nc.vector.memset(warm[:, 0:1], 0.0)
-        nc.scalar.activation(warm[:, 1:2], warm[:, 0:1], ACT.Tanh)
+        warm_in = held("warm_in", [P, 1], F32)
+        warm_out = held("warm_out", [P, 1], F32)
+        nc.vector.memset(warm_in[:], 0.0)
+        nc.scalar.activation(warm_out[:], warm_in[:], ACT.Tanh)
 
         idx = lists.tile([P, S // 16], U16, name="idx")
         idx2 = lists.tile([P, S // 16], U16, name="idx2")
@@ -101,7 +102,8 @@ def tile_list_spill_slot_advisor_kernel(
         nc.sync.dma_start(b1_sb[:], b1.rearrange("(p t) -> p t", t=PACK))
         nc.sync.dma_start(gain_sb[:], gain.rearrange("(p t) -> p t", t=PACK))
         w2_rows = w2.rearrange("(p j) r -> p j r", j=PACK)
-        zeroed_page("warm")
+        zeroed_page("warm_in")
+        zeroed_page("warm_out")
 
         picked_scales = held("picked_scales", [P, S], U8)
         nc.vector.tensor_copy(picked_scales[:], tab_plane[:].indirect(idx[:]))
@@ -131,7 +133,7 @@ def tile_list_spill_slot_advisor_kernel(
         )
         v_codes.append(pick_words(1, "v1_first", 0, 1))
 
-        zeroed_page("w1_raw")
+        zeroed_page("w1_plane_raw")
         cap_rows = cap.rearrange("(a p t) m -> a p t m", a=2, t=PACK)
 
         w2_codes = [held(f"w2_codes{a}", [P, 512], U32) for a in range(2)]
@@ -222,7 +224,7 @@ def tile_list_spill_slot_advisor_kernel(
             nc.vector.tensor_tensor(pages[t][:].indirect(offsets), values, wgs_sb[:, t, span], ALU.mult)
 
         first_features()
-        wgs_sb = held("wgs_sb", [P, PACK, S], F32, tag="w1_plane_raw")
+        wgs_sb = held("wgs_sb", [P, PACK, S], F32, tag="w1_raw")
         wgs_rows = wgs.rearrange("(p t) s -> p t s", t=PACK)
         for span in (cols(0), cols(1), slice(2 * PIECE, S)):
             for q in (0, 2, 1, 3):
@@ -232,8 +234,6 @@ def tile_list_spill_slot_advisor_kernel(
         v_codes[1].extend(pick_words(1, "v1_second", 1, 2))
         v_codes[0].extend(pick_words(0, "v0_back", 2, PIECES, tag="picked_scales"))
         v_codes[1].extend(pick_words(1, "v1_back", 2, PIECES, tag="e_grouped01"))
-        zeroed_page("v1_first")
-        zeroed_page("e_grouped00")
         w2_raw.append(held("w2_raw1", [P, PACK, 512], F32, tag="v1_second"))
         squashed = []
         for j in range(PIECES):
@@ -242,6 +242,7 @@ def tile_list_spill_slot_advisor_kernel(
                 costs(0, [(t, j)], h0[t][:])
             if j == 0:
                 quantize_w2(0, 2, PACK, tag="th01")
+                zeroed_page("th01")
             put(0, idx2[:, entries(j)], h0[0][:, 0, :], cols(j))
             for t in range(2, PACK):
                 costs(0, [(t, j)], h0[t][:])

@@ -23,6 +23,9 @@ PIECES = S // PIECE
 LIST_COLS = PIECE // 16
 
 
+HALF = 128
+
+
 def tile_list_spill_slot_advisor_kernel(
     tc, tab_words, tab_scales, offs, w1_words, w1_scales, b1, gain, w2, wgs, offs2, offs3, cap, w3_words, w3_scales, out
 ):
@@ -30,54 +33,66 @@ def tile_list_spill_slot_advisor_kernel(
     with ExitStack() as ctx:
         lists = ctx.enter_context(tc.tile_pool(name="lists", bufs=1))
         sb = ctx.enter_context(tc.tile_pool(name="sb", bufs=1))
-        ring = ctx.enter_context(tc.tile_pool(name="ring", bufs=2))
-        psum = ctx.enter_context(tc.psum_pool(name="psum", bufs=4))
+        psum = ctx.enter_context(tc.psum_pool(name="psum", bufs=1))
 
         def held(name, shape, dtype, tag=None):
             return sb.tile(shape, dtype, name=name, tag=tag or name, align_bytes=64)
 
-        def ringed(name, shape, dtype):
-            return ring.tile(shape, dtype, name=name, tag=name, align_bytes=64)
+        def bank(n, shape):
+            return psum.tile(shape, F32, name=f"bank{n}", tag=f"bank{n}")
 
-        def cols(j):
-            return slice(j * PIECE, (j + 1) * PIECE)
+        def cols(j, last=None):
+            return slice(j * PIECE, ((j if last is None else last) + 1) * PIECE)
 
-        def entries(j):
-            return slice(j * LIST_COLS, (j + 1) * LIST_COLS)
+        def entries(j, last=None):
+            return slice(j * LIST_COLS, ((j if last is None else last) + 1) * LIST_COLS)
 
-        def interleave(engine_copy, dst, src):
-            engine_copy(
-                dst.rearrange("p (c i) t -> p c t i", i=4),
-                src.rearrange("p t (c i) -> p c t i", i=4),
-            )
+        def by_word(grouped):
+            return grouped.rearrange("p (c i) t -> p c t i", i=4)
+
+        def by_row(rows):
+            return rows.rearrange("p t (c i) -> p c t i", i=4)
+
+        def quantize(codes, plane, grouped):
+            nc.vector.quantize_mx(out=codes.bitcast(FP8X4), scales=plane, in_=grouped)
+
+        pages = []
+
+        def zeroed_page(engine, tag=None):
+            page = held(f"page{len(pages)}", [P, T2], F32, tag=tag)
+            for c0 in range(0, T2, 512):
+                engine.memset(page[:, c0 : c0 + 512], 0.0)
+            pages.append(page)
 
         tab_plane = held("tab_plane", [P, T], U8)
         w1_plane_raw = held("w1_plane_raw", [P, 2, M], U8)
         v_plane = [held(f"v_plane{a}", [P, S], U8) for a in range(2)]
-        pages = []
-
-        def zeroed_page(tag):
-            page = held(f"page{len(pages)}", [P, T2], F32, tag=tag)
-            for c0 in range(0, T2, 512):
-                nc.gpsimd.memset(page[:, c0 : c0 + 512], 0.0)
-            pages.append(page)
-
+        warm_in = held("warm_in", [P, 1], F32)
+        warm_out = held("warm_out", [P, 1], F32)
         nc.gpsimd.memset(w1_plane_raw[:].rearrange("p a c -> p (a c)").bitcast(I32), 0)
+        nc.vector.memset(warm_in[:], 0.0)
+        nc.scalar.activation(warm_out[:], warm_in[:], ACT.Tanh)
         for q in range(4):
             nc.vector.memset(tab_plane[32 * q : 32 * q + 24, :].bitcast(I32), 0)
         for a in range(2):
             nc.vector.memset(v_plane[a][96:128, :].bitcast(I32), 0)
-
-        warm_in = held("warm_in", [P, 1], F32)
-        warm_out = held("warm_out", [P, 1], F32)
-        nc.vector.memset(warm_in[:], 0.0)
-        nc.scalar.activation(warm_out[:], warm_in[:], ACT.Tanh)
 
         idx = lists.tile([P, S // 16], U16, name="idx")
         idx2 = lists.tile([P, S // 16], U16, name="idx2")
         idx3 = lists.tile([P, PICKS // 16], U16, name="idx3")
         b1_sb = held("b1_sb", [P, PACK], F32)
         gain_sb = held("gain_sb", [P, PACK], F32)
+        tab = [held(f"tab{a}", [P, T], I32) for a in range(2)]
+        w1_raw = held("w1_raw", [P, 2, M // 2], I32)
+        w2_rows = w2.rearrange("(p j) r -> p j r", j=PACK)
+
+        def load_scale_rows(plane, scales):
+            for q in range(4):
+                nc.sync.dma_start(
+                    plane[32 * q : 32 * q + 4, :, :].bitcast(I32),
+                    scales[:, 4 * q : 4 * q + 4, :].rearrange("a r c -> r a c").bitcast(I32),
+                )
+
         nc.sync.dma_start(idx[:], offs)
         for q in range(4):
             nc.sync.dma_start(
@@ -85,210 +100,221 @@ def tile_list_spill_slot_advisor_kernel(
             )
         nc.sync.dma_start(idx2[:], offs2)
         nc.sync.dma_start(idx3[:], offs3)
-        tab = [held(f"tab{a}", [P, T], I32) for a in range(2)]
-        w1_raw = held("w1_raw", [P, 2, M // 2], I32)
         nc.sync.dma_start(tab[0][:], tab_words[0].rearrange("p t i -> p (t i)").bitcast(I32))
         nc.sync.dma_start(w1_raw[:], w1_words.rearrange("a p b -> p a b").bitcast(I32))
-
-        def load_scale_rows(queue, plane, scales, q):
-            queue.dma_start(
-                plane[32 * q : 32 * q + 4, :, :].bitcast(I32),
-                scales[:, 4 * q : 4 * q + 4, :].rearrange("a r c -> r a c").bitcast(I32),
-            )
-
-        for q in range(4):
-            load_scale_rows(nc.sync, w1_plane_raw, w1_scales, q)
+        load_scale_rows(w1_plane_raw, w1_scales)
         nc.sync.dma_start(tab[1][:], tab_words[1].rearrange("p t i -> p (t i)").bitcast(I32))
         nc.sync.dma_start(b1_sb[:], b1.rearrange("(p t) -> p t", t=PACK))
         nc.sync.dma_start(gain_sb[:], gain.rearrange("(p t) -> p t", t=PACK))
-        w2_rows = w2.rearrange("(p j) r -> p j r", j=PACK)
-        zeroed_page("warm_in")
-        zeroed_page("warm_out")
+        zeroed_page(nc.gpsimd, "warm_in")
+        zeroed_page(nc.gpsimd, "warm_out")
 
-        picked_scales = held("picked_scales", [P, S], U8)
-        nc.vector.tensor_copy(picked_scales[:], tab_plane[:].indirect(idx[:]))
-        for a in range(2):
-            shift = 24 + 4 * a
-            nc.sync.dma_start(v_plane[a][0 : P - shift, :].bitcast(I32), picked_scales[shift:P, :].bitcast(I32))
+        def pick_scales(first, last):
+            picked = held(f"picked{first}", [P, (last - first + 1) * PIECE], U8)
+            nc.vector.tensor_copy(picked[:], tab_plane[:].indirect(idx[:, entries(first, last)]))
+            for a in range(2):
+                shift = 24 + 4 * a
+                nc.sync.dma_start(
+                    v_plane[a][0 : P - shift, cols(first, last)].bitcast(I32), picked[shift:P, :].bitcast(I32)
+                )
 
-        def pick_words(a, name, first, last, tag=None):
-            codes = held(name, [P, (last - first) * PIECE], U32, tag=tag)
-            offsets = idx[:, first * LIST_COLS : last * LIST_COLS]
-            nc.vector.tensor_copy(codes[:], tab[a][:].bitcast(U32).indirect(offsets))
-            return [codes[:, (j - first) * PIECE : (j - first + 1) * PIECE] for j in range(first, last)]
+        v_codes = [[], []]
 
+        def pick_words(passes, first, last, tag=None):
+            width = (last - first + 1) * PIECE
+            codes = held(f"v{passes[0]}_{first}", [P, len(passes) * width], U32, tag=tag)
+            for u, a in enumerate(passes):
+                part = codes[:, u * width : (u + 1) * width]
+                nc.vector.tensor_copy(part, tab[a][:].bitcast(U32).indirect(idx[:, entries(first, last)]))
+                v_codes[a].extend(part[:, cols(j)] for j in range(last - first + 1))
 
+        pick_scales(0, PIECES - 1)
+        w2_raw = [held("w2_raw0", [P, PACK, 512], F32, tag="tab_plane")]
+        nc.sync.dma_start(w2_raw[0][:], w2_rows[:, :, 0:512])
+        pick_words((0,), 0, 1)
         w1_codes = held("w1_codes", [P, 2, M // 2], I32)
         nc.vector.tensor_copy(
             w1_codes[:].bitcast(U16).rearrange("p a (t m) -> p a m t", t=PACK),
             w1_raw[:].bitcast(U16).rearrange("p a (m t) -> p a m t", t=PACK),
         )
-        w2_raw = [held("w2_raw0", [P, PACK, 512], F32, tag="tab_plane")]
-        nc.sync.dma_start(w2_raw[0][:], w2_rows[:, :, 0:512])
-        v_codes = [pick_words(0, "v0_front", 0, 2)]
         w1_plane = held("w1_plane", [P, 2, M], U8)
         nc.vector.tensor_copy(
             w1_plane[:].rearrange("p a (t m) -> p a m t", t=PACK),
             w1_plane_raw[:].rearrange("p a (m t) -> p a m t", t=PACK),
         )
-        v_codes.append(pick_words(1, "v1_first", 0, 1))
+        pick_words((1,), 0, 0)
+        pick_words((1,), 1, 1)
 
-        zeroed_page("w1_plane_raw")
-        cap_rows = cap.rearrange("(a p t) m -> a p t m", a=2, t=PACK)
+        wgs_rows = wgs.rearrange("(p t) s -> p t s", t=PACK)
+        wgs_first = held("wgs_first", [P, PACK, PIECE], F32, tag="w1_raw")
+        wgs_rest = held("wgs_rest", [P, PACK, S - PIECE], F32, tag="w1_plane_raw")
+        for tile, span in ((wgs_first, cols(0)), (wgs_rest, cols(1, PIECES - 1))):
+            for q in (0, 2, 1, 3):
+                nc.sync.dma_start(tile[32 * q : 32 * q + 32, :, :], wgs_rows[:, :, span])
 
-        w2_codes = [held(f"w2_codes{a}", [P, 512], U32) for a in range(2)]
-        w2_plane = [held(f"w2_plane{a}", [P, 512], U8) for a in range(2)]
+        def first_product(dst, j, slots, halves):
+            steps = [(a, u, n) for a in range(2) for u in range(len(slots)) for n in range(len(halves))]
+            for a, u, n in steps:
+                t, c0 = slots[u], halves[n] * HALF
+                nc.tensor.matmul_mx(
+                    out=dst[:, u, HALF * n : HALF * n + HALF],
+                    lhsT=w1_codes[:, a, 64 * t : 64 * t + 64].bitcast(FP4X4),
+                    lhsT_scale=w1_plane[:, a, 128 * t : 128 * t + 128],
+                    rhs=v_codes[a][j][:, c0 : c0 + HALF].bitcast(FP8X4),
+                    rhs_scale=v_plane[a][:, j * PIECE + c0 : j * PIECE + c0 + HALF],
+                    start=((a, u, n) == steps[0]),
+                    stop=((a, u, n) == steps[-1]),
+                )
 
-        def quantize(codes, plane, grouped):
-            nc.vector.quantize_mx(out=codes.bitcast(FP8X4), scales=plane, in_=grouped)
-
-        def quantize_w2(a, t0, t1, copy=nc.scalar.copy, tag=None):
-            grouped = held(f"w2_grouped{a}{t0}", [P, t1 - t0, 128, PACK], BF16, tag=tag)
+        def round_w2(copy, a, grouped, t0):
             copy(
-                grouped[:].rearrange("p t m j -> p m j t"),
-                w2_raw[a][:].rearrange("p j (m t) -> p m j t", t=PACK)[:, :, :, t0:t1],
+                grouped.rearrange("p t m j -> p m j t"),
+                w2_raw[a][:].rearrange("p j (m t) -> p m j t", t=PACK)[:, :, :, t0 : t0 + 2],
             )
-            span = slice(128 * t0, 128 * t1)
-            quantize(w2_codes[a][:, span], w2_plane[a][:, span], grouped[:].rearrange("p t m j -> p (t m j)"))
 
-        e_codes = []
+        e_codes = [held("e_codes0", [P, PIECE], U32)]
         e_plane = held("e_plane", [P, S], U8)
+        w2_codes = [held("w2_codes0", [P, 256], U32)]
+        w2_plane = [held(f"w2_plane{a}", [P, 512], U8) for a in range(2)]
+        th0 = []
+        for half in range(2):
+            pre = bank(half, [P, PACK, HALF])
+            first_product(pre, 0, range(PACK), (half,))
+            th0.append(held(f"th0{half}", [P, PACK, HALF], F32))
+            for t in range(PACK):
+                nc.scalar.activation(th0[half][:, t, :], pre[:, t, :], ACT.Tanh, bias=b1_sb[:, t : t + 1])
+        w2_front = [held(f"w2_front{u}", [P, 2, 128, PACK], BF16) for u in range(2)]
+        round_w2(nc.vector.tensor_copy, 0, w2_front[0][:], 0)
+        round_w2(nc.scalar.copy, 0, w2_front[1][:], 2)
+        e_first = [held(f"e_first{half}", [P, HALF, PACK], BF16) for half in range(2)]
+        for half in range(2):
+            nc.vector.tensor_tensor(
+                by_word(e_first[half][:]),
+                by_row(th0[half][:]),
+                gain_sb[:].unsqueeze(1).unsqueeze(3).to_broadcast([P, HALF // 4, PACK, 4]),
+                ALU.mult,
+            )
+            if half == 0:
+                quantize(w2_codes[0][:], w2_plane[0][:, 0:256], w2_front[0][:].rearrange("p t m j -> p (t m j)"))
+        for half in range(2):
+            span = slice(HALF * half, HALF * half + HALF)
+            quantize(e_codes[0][:, span], e_plane[:, span], e_first[half][:].rearrange("p n t -> p (n t)"))
+        pick_words((0, 1), 2, PIECES - 1, tag="e_first0")
+        zeroed_page(nc.gpsimd, "e_first1")
+        w2_codes.append(held("w2_codes1", [P, 256], U32, tag="tab1"))
+        quantize(w2_codes[1][:], w2_plane[0][:, 256:512], w2_front[1][:].rearrange("p t m j -> p (t m j)"))
+        zeroed_page(nc.gpsimd, "w2_front1")
 
-        def first_product(j, bank_cols, t, halves):
-            for a in range(2):
-                for n, half in enumerate(halves):
-                    c0 = half * 128
-                    nc.tensor.matmul_mx(
-                        out=bank_cols[:, 128 * n : 128 * n + 128],
-                        lhsT=w1_codes[:, a, 64 * t : 64 * t + 64].bitcast(FP4X4),
-                        lhsT_scale=w1_plane[:, a, 128 * t : 128 * t + 128],
-                        rhs=v_codes[a][j][:, c0 : c0 + 128].bitcast(FP8X4),
-                        rhs_scale=v_plane[a][:, j * PIECE + c0 : j * PIECE + c0 + 128],
-                        start=(a == 0 and n == 0),
-                        stop=(a == 1 and n == len(halves) - 1),
-                    )
+        def front_bank(j):
+            return 0 if j % 2 else 4
+
+        def grouped_tag(j):
+            return f"e_grouped{j}"
 
         def squash(j):
-            th = held(f"th{j}", [P, PACK, PIECE], F32)
-            for t in range(PACK):
-                bank = psum.tile([P, PIECE], F32, name=f"pre{t}", tag="bank_a")
-                first_product(j, bank[:], t, (0, 1))
-                nc.scalar.activation(th[:, t, :], bank[:], ACT.Tanh, bias=b1_sb[:, t : t + 1])
+            th = held(f"th{j}", [P, PACK, PIECE], F32, tag=grouped_tag(j - 1) if j > 1 else None)
+            for pair in range(2):
+                pre = bank(2 + pair if j == 1 else front_bank(j - 2) + pair, [P, 2, PIECE])
+                first_product(pre, j, (2 * pair, 2 * pair + 1), (0, 1))
+                for u in range(2):
+                    t = 2 * pair + u
+                    nc.scalar.activation(th[:, t, :], pre[:, u, :], ACT.Tanh, bias=b1_sb[:, t : t + 1])
             return th
 
-        def features(j, th, codes_tag):
-            e_rows = held(f"e_rows{j}", [P, PACK, PIECE], BF16)
+        def rows_tag(j):
+            return "w2_front0" if j == 1 else f"e_rows{j}"
+
+        def features(j, th):
+            e_rows = held(f"e_rows{j}", [P, PACK, PIECE], BF16, tag=rows_tag(j))
             for t in range(PACK):
                 nc.scalar.activation(e_rows[:, t, :], th[:, t, :], ACT.Copy, scale=gain_sb[:, t : t + 1])
             e_grouped = held(f"e_grouped{j}", [P, PIECE, PACK], BF16)
-            interleave(nc.scalar.copy, e_grouped[:], e_rows[:])
-            e_codes.append(held(f"e_codes{j}", [P, PIECE], U32, tag=codes_tag))
+            nc.scalar.copy(by_word(e_grouped[:]), by_row(e_rows[:]))
+            e_codes.append(held(f"e_codes{j}", [P, PIECE], U32, tag=f"front{j - 1}0"))
             quantize(e_codes[j][:], e_plane[:, cols(j)], e_grouped[:].rearrange("p n t -> p (n t)"))
 
-        def first_features():
-            e_codes.append(held("e_codes0", [P, PIECE], U32))
-            for half in range(2):
-                th = held(f"th0{half}", [P, PACK, 128], F32)
-                for pair in range(2):
-                    bank = psum.tile([P, 2, 128], F32, name=f"pre{pair}", tag="bank_a")
-                    for u in range(2):
-                        first_product(0, bank[:, u, :], 2 * pair + u, (half,))
-                    for u in range(2):
-                        t = 2 * pair + u
-                        nc.scalar.activation(th[:, t, :], bank[:, u, :], ACT.Tanh, bias=b1_sb[:, t : t + 1])
-                e_grouped = held(f"e_grouped0{half}", [P, 128, PACK], BF16)
-                nc.vector.tensor_tensor(
-                    e_grouped[:].rearrange("p (c i) t -> p c t i", i=4),
-                    th[:].rearrange("p t (c i) -> p c t i", i=4),
-                    gain_sb[:].unsqueeze(1).unsqueeze(3).to_broadcast([P, 128 // 4, PACK, 4]),
-                    ALU.mult,
-                )
-                span = slice(128 * half, 128 * half + 128)
-                quantize(e_codes[0][:, span], e_plane[:, span], e_grouped[:].rearrange("p n t -> p (n t)"))
+        def w2_slot(a, t):
+            if a == 0:
+                return w2_codes[t // 2][:, 128 * (t % 2) : 128 * (t % 2) + 128]
+            return w2_codes[2][:, 128 * t : 128 * t + 128]
 
-        def costs(a, parts, dst):
-            bank = psum.tile([P, len(parts), PIECE], F32, name="bank_b", tag="bank_b")
+        def front_tag(j, t):
+            return {(0, 1): "tab0", (1, 1): "tab_plane"}.get((j, t))
+
+        def costs(a, parts, n, dst):
+            acc = bank(n, [P, len(parts) * PIECE])
             for u, (t, j) in enumerate(parts):
                 nc.tensor.matmul_mx(
-                    out=bank[:, u, :],
-                    lhsT=w2_codes[a][:, 128 * t : 128 * t + 128].bitcast(FP8X4),
+                    out=acc[:, cols(u)],
+                    lhsT=w2_slot(a, t).bitcast(FP8X4),
                     lhsT_scale=w2_plane[a][:, 128 * t : 128 * t + 128],
                     rhs=e_codes[j][:].bitcast(FP8X4),
                     rhs_scale=e_plane[:, cols(j)],
                     start=True,
                     stop=True,
                 )
-            nc.scalar.copy(dst, bank[:])
+            nc.scalar.copy(dst, acc[:])
 
-        def put(t, offsets, values, span):
-            nc.vector.tensor_tensor(pages[t][:].indirect(offsets), values, wgs_sb[:, t, span], ALU.mult)
+        def put(t, first, last, values):
+            weights = wgs_first[:, t, :] if first == 0 else wgs_rest[:, t, cols(first - 1, last - 1)]
+            nc.vector.tensor_tensor(pages[t][:].indirect(idx2[:, entries(first, last)]), values, weights, ALU.mult)
 
-        first_features()
-        wgs_sb = held("wgs_sb", [P, PACK, S], F32, tag="w1_raw")
-        wgs_rows = wgs.rearrange("(p t) s -> p t s", t=PACK)
-        for span in (cols(0), cols(1), slice(2 * PIECE, S)):
-            for q in (0, 2, 1, 3):
-                nc.sync.dma_start(wgs_sb[32 * q : 32 * q + 32, :, span], wgs_rows[:, :, span])
-        quantize_w2(0, 0, 1, nc.vector.tensor_copy, tag="th00")
-        quantize_w2(0, 1, 2, tag="e_grouped00")
-        v_codes[1].extend(pick_words(1, "v1_second", 1, 2))
-        v_codes[0].extend(pick_words(0, "v0_back", 2, PIECES, tag="picked_scales"))
-        v_codes[1].extend(pick_words(1, "v1_back", 2, PIECES, tag="e_grouped01"))
-        w2_raw.append(held("w2_raw1", [P, PACK, 512], F32, tag="v1_second"))
-        squashed = []
+        cap_rows = cap.rearrange("(a p t) m -> a p t m", a=2, t=PACK)
         for j in range(PIECES):
-            h0 = [held(f"h0_{j}{t}", [P, 1, PIECE], F32) for t in range(PACK)]
             for t in range(2):
-                costs(0, [(t, j)], h0[t][:])
+                front = held(f"front{j}{t}", [P, PIECE], F32, tag=front_tag(j, t))
+                costs(0, [(t, j)], front_bank(j) + t, front[:])
+                put(t, j, j, front[:])
             if j == 0:
-                quantize_w2(0, 2, PACK, tag="th01")
-                zeroed_page("th01")
-            put(0, idx2[:, entries(j)], h0[0][:, 0, :], cols(j))
-            for t in range(2, PACK):
-                costs(0, [(t, j)], h0[t][:])
-            put(1, idx2[:, entries(j)], h0[1][:, 0, :], cols(j))
-            put(2, idx2[:, entries(j)], h0[2][:, 0, :], cols(j))
-            if j + 1 < PIECES:
-                features(j + 1, squashed.pop() if j > 0 else squash(1), f"h0_{j}1")
-            if j + 2 < PIECES:
-                squashed.append(squash(j + 2))
-            if j == 0:
+                w2_raw.append(held("w2_raw1", [P, PACK, 512], F32, tag="tab0"))
                 nc.sync.dma_start(w2_raw[1][:], w2_rows[:, :, 512:1024])
-            put(PACK - 1, idx2[:, entries(j)], h0[PACK - 1][:, 0, :], cols(j))
-        cap0 = held("cap0", [P, PACK, PICKS], F32, tag="tab0")
-        nc.sync.dma_start(cap0[:], cap_rows[0])
-        w3_codes = held("w3_codes", [P, 2, N], I32, tag="v_plane1")
-        nc.sync.dma_start(w3_codes[:], w3_words.rearrange("a p c i -> p a (c i)").bitcast(I32))
-        for t in (0, 2):
-            quantize_w2(1, t, t + 2, tag=f"h0_{PIECES - 1}{PACK - 1}")
+            if j + 1 < PIECES:
+                features(j + 1, squash(j + 1))
+            back = held(f"back{j}", [P, 2 * PIECE], F32, tag=rows_tag(j + 1))
+            costs(0, [(2, j), (3, j)], 6 + j % 2, back[:])
+            put(2, j, j, back[:, cols(0)])
+            if j == PIECES - 1:
+                w2_back = held("w2_back", [P, PACK, 128, PACK], BF16, tag="e_grouped3")
+                for t0 in (0, 2):
+                    round_w2(nc.scalar.copy, 1, w2_back[:, t0 : t0 + 2], t0)
+                cap1 = held("cap1", [P, PACK, PICKS], F32, tag="tab0")
+                nc.sync.dma_start(cap1[:], cap_rows[1])
+                w2_codes.append(held("w2_codes2", [P, 512], U32, tag="front31"))
+                quantize(w2_codes[2][:], w2_plane[1][:], w2_back[:].rearrange("p t m j -> p (t m j)"))
+            put(3, j, j, back[:, cols(1)])
+            if j == 1:
+                cap0 = held("cap0", [P, PACK, PICKS], F32, tag="tab_plane")
+                nc.sync.dma_start(cap0[:], cap_rows[0])
+                w3_plane = held("w3_plane", [P, 2, N], U8, tag="picked0")
+                nc.gpsimd.memset(w3_plane[:].rearrange("p a c -> p (a c)").bitcast(I32), 0)
+                load_scale_rows(w3_plane, w3_scales)
+            if j == PIECES - 2:
+                w3_codes = held("w3_codes", [P, 2, N], I32, tag="v_plane1")
+                nc.sync.dma_start(w3_codes[:], w3_words.rearrange("a p c i -> p a (c i)").bitcast(I32))
 
-        h1 = [held(f"h1{t}", [P, PIECES, PIECE], F32) for t in range(PACK)]
+        h1 = [held(f"h1{t}", [P, S], F32) for t in range(PACK)]
         for t in range(PACK):
             for half in range(2):
-                costs(1, [(t, 2 * half), (t, 2 * half + 1)], h1[t][:, 2 * half : 2 * half + 2, :])
+                span = cols(2 * half, 2 * half + 1)
+                costs(1, [(t, 2 * half), (t, 2 * half + 1)], (2 * t + half) % 8, h1[t][:, span])
 
-        w3_plane = held("w3_plane", [P, 2, N], U8, tag="h0_03")
-        nc.gpsimd.memset(w3_plane[:].rearrange("p a c -> p (a c)").bitcast(I32), 0)
-        for q in range(4):
-            load_scale_rows(nc.sync, w3_plane, w3_scales, q)
+        def limit(grouped, picked, caps):
+            nc.vector.tensor_tensor(by_word(grouped), by_row(picked), by_row(caps), ALU.min)
 
-        x = held("x", [P, PACK, PICKS], F32)
-        z_rows0 = held("z_rows0", [P, PACK, PICKS], BF16, tag="tab_plane")
-        for t in range(PACK):
-            nc.vector.tensor_copy(x[:, t, :], pages[t][:].indirect(idx3[:]))
-        for t in range(0, PACK, 2):
-            nc.vector.tensor_tensor(z_rows0[:, t : t + 2, :], x[:, t : t + 2, :], cap0[:, t : t + 2, :], ALU.min)
-        z_grouped0 = held("z_grouped0", [P, PICKS, PACK], BF16)
-        interleave(nc.scalar.copy, z_grouped0[:], z_rows0[:])
-        cap1 = held("cap1", [P, PACK, PICKS], F32, tag="tab0")
-        nc.sync.dma_start(cap1[:], cap_rows[1])
-
+        x0 = held("x0", [P, PACK, PICKS], F32, tag="e_grouped3")
+        z0 = held("z0", [P, PICKS, PACK], BF16)
+        z_codes = [held(f"z_codes{a}", [P, PICKS], U32) for a in range(2)]
         z_plane = [held(f"z_plane{a}", [P, PICKS], U8) for a in range(2)]
-        for t in range(PACK - 1):
-            put(t, idx2[:], h1[t][:].rearrange("p j c -> p (j c)"), slice(0, S))
-        z_codes = [held("z_codes0", [P, PICKS], U32, tag="h12"), held("z_codes1", [P, PICKS], U32)]
-        quantize(z_codes[0][:], z_plane[0][:], z_grouped0[:].rearrange("p n t -> p (n t)"))
-        put(PACK - 1, idx2[:], h1[PACK - 1][:].rearrange("p j c -> p (j c)"), slice(0, S))
+        for t in range(PACK):
+            nc.vector.tensor_copy(x0[:, t, :], pages[t][:].indirect(idx3[:]))
+        for t in range(PACK):
+            put(t, 1, PIECES - 1, h1[t][:, cols(1, PIECES - 1)])
+            if t == 0:
+                limit(z0[:], x0[:], cap0[:])
+            if t == 1:
+                quantize(z_codes[0][:], z_plane[0][:], z0[:].rearrange("p n t -> p (n t)"))
+        for t in range(PACK):
+            put(t, 0, 0, h1[t][:, cols(0)])
 
         out_rows = out.rearrange("(c p) m -> p c m", p=P)
         last = PIECES - 1
@@ -308,43 +334,13 @@ def tile_list_spill_slot_advisor_kernel(
 
         def open_scores(n):
             span = spans[n]
-            tag = "bank_a" if n % 2 == 0 else "bank_b"
-            banks = [psum.tile([P, 2, span.stop - span.start], F32, name=f"acc{c}", tag=tag) for c in range(2)]
+            banks = [bank((2 * n + c) % 8, [P, 2, span.stop - span.start]) for c in range(2)]
             score_pass(0, banks, span)
             return banks
 
-        def fetch(j, slots, tag):
-            picked = held(f"x{j}{slots[0]}", [P, len(slots), PIECE], F32, tag=tag)
-            for u, t in enumerate(slots):
-                nc.vector.tensor_copy(picked[:, u, :], pages[t][:].indirect(idx3[:, entries(j)]))
-            return picked
-
-        def fetch_pairs(j):
-            return [fetch(j, (0, 1), "x_low"), fetch(j, (2, 3), "x_high")]
-
-        def limit(j, pairs):
-            z_rows = held(f"z_rows_p{j}", [P, PACK, PIECE], BF16, tag="z_rows_p")
-            for u in range(2):
-                slots = slice(2 * u, 2 * u + 2)
-                nc.vector.tensor_tensor(z_rows[:, slots, :], pairs[u][:], cap1[:, slots, cols(j)], ALU.min)
-            z_grouped = held(f"z_grouped_p{j}", [P, PIECE, PACK], BF16)
-            interleave(nc.scalar.copy, z_grouped[:], z_rows[:])
-            return z_grouped
-
-        def limit_last(picked, half, tag):
-            span = spans[last + half]
-            z_grouped = held(f"z_grouped_last{half}", [P, 128, PACK], BF16, tag=tag)
-            nc.vector.tensor_tensor(
-                z_grouped[:].rearrange("p (c i) t -> p c t i", i=4),
-                picked[:, :, 128 * half : 128 * half + 128].rearrange("p t (c i) -> p c t i", i=4),
-                cap1[:, :, span].rearrange("p t (c i) -> p c t i", i=4),
-                ALU.min,
-            )
-            return z_grouped
-
-        def scores(n, z_grouped):
+        def finish(n, grouped):
             span = spans[n]
-            quantize(z_codes[1][:, span], z_plane[1][:, span], z_grouped[:].rearrange("p n t -> p (n t)"))
+            quantize(z_codes[1][:, span], z_plane[1][:, span], grouped.rearrange("p n t -> p (n t)"))
             score_pass(1, opened[n], span)
 
         def store(n):
@@ -356,16 +352,29 @@ def tile_list_spill_slot_advisor_kernel(
                 nc.sync.dma_start(out_rows[:, 2 * pair : 2 * pair + 2, span], staged[:])
 
         opened = [open_scores(n) for n in range(PIECES)]
-        picked = fetch_pairs(0)
-        for n in range(last):
-            z_grouped = limit(n, picked)
-            picked = fetch_pairs(n + 1) if n + 1 < last else fetch(last, (0, 1, 2, 3), "x_low")
-            scores(n, z_grouped)
-            store(n)
-            if n == 0:
+        x1 = [held(f"x1{j}", [P, PACK, PIECE], F32, tag=(None, "th1", grouped_tag(1), grouped_tag(2))[j]) for j in range(PIECES)]
+        z1 = [held(f"z1{j}", [P, PIECE, PACK], BF16, tag=("front30", "front31", "front20", "front10")[j]) for j in range(PIECES)]
+
+        def fetch(j, t):
+            nc.vector.tensor_copy(x1[j][:, t, :], pages[t][:].indirect(idx3[:, entries(j)]))
+
+        for t in range(PACK):
+            fetch(0, t)
+        for j in range(last):
+            finish_after = 1 if j + 1 < last else 3
+            for t in range(PACK):
+                fetch(j + 1, t)
+                if t == 0:
+                    limit(z1[j][:], x1[j][:], cap1[:, :, cols(j)])
+                if t == finish_after:
+                    finish(j, z1[j][:])
+                    store(j)
+            if j == 0:
                 opened.append(open_scores(PIECES))
-        halves = [limit_last(picked, 0, "z_rows_p"), limit_last(picked, 1, None)]
-        for n in range(2):
-            scores(last + n, halves[n])
-        for n in range(2):
-            store(last + n)
+        for half in range(2):
+            inner = slice(HALF * half, HALF * half + HALF)
+            limit(z1[last][:, inner, :], x1[last][:, :, inner], cap1[:, :, spans[last + half]])
+        for half in range(2):
+            finish(last + half, z1[last][:, HALF * half : HALF * half + HALF, :])
+        for half in range(2):
+            store(last + half)

@@ -142,15 +142,16 @@ def tile_list_spill_slot_advisor_kernel(
             w1_plane[:].rearrange("p a (t m) -> p a m t", t=PACK),
             w1_plane_raw[:].rearrange("p a (m t) -> p a m t", t=PACK),
         )
+        zeroed_page(nc.gpsimd, "w1_plane_raw")
         pick_words((1,), 0, 0)
         pick_words((1,), 1, 1)
+        pick_words((0,), 2, PIECES - 1, tag="picked0")
 
         wgs_rows = wgs.rearrange("(p t) s -> p t s", t=PACK)
-        wgs_first = held("wgs_first", [P, PACK, PIECE], F32, tag="w1_raw")
-        wgs_rest = held("wgs_rest", [P, PACK, S - PIECE], F32, tag="w1_plane_raw")
-        for tile, span in ((wgs_first, cols(0)), (wgs_rest, cols(1, PIECES - 1))):
+        wgs_sb = held("wgs_sb", [P, PACK, S], F32, tag="w1_raw")
+        for span in (cols(0), cols(1, PIECES - 1)):
             for q in (0, 2, 1, 3):
-                nc.sync.dma_start(tile[32 * q : 32 * q + 32, :, :], wgs_rows[:, :, span])
+                nc.sync.dma_start(wgs_sb[32 * q : 32 * q + 32, :, span], wgs_rows[:, :, span])
 
         def first_product(dst, j, slots, halves):
             steps = [(a, u, n) for a in range(2) for u in range(len(slots)) for n in range(len(halves))]
@@ -199,8 +200,7 @@ def tile_list_spill_slot_advisor_kernel(
         for half in range(2):
             span = slice(HALF * half, HALF * half + HALF)
             quantize(e_codes[0][:, span], e_plane[:, span], e_first[half][:].rearrange("p n t -> p (n t)"))
-        pick_words((0, 1), 2, PIECES - 1, tag="e_first0")
-        zeroed_page(nc.gpsimd, "e_first1")
+        pick_words((1,), 2, PIECES - 1, tag="e_first0")
         w2_codes.append(held("w2_codes1", [P, 256], U32, tag="tab1"))
         quantize(w2_codes[1][:], w2_plane[0][:, 256:512], w2_front[1][:].rearrange("p t m j -> p (t m j)"))
         zeroed_page(nc.gpsimd, "w2_front1")
@@ -256,7 +256,7 @@ def tile_list_spill_slot_advisor_kernel(
             nc.scalar.copy(dst, acc[:])
 
         def put(t, first, last, values):
-            weights = wgs_first[:, t, :] if first == 0 else wgs_rest[:, t, cols(first - 1, last - 1)]
+            weights = wgs_sb[:, t, cols(first, last)]
             nc.vector.tensor_tensor(pages[t][:].indirect(idx2[:, entries(first, last)]), values, weights, ALU.mult)
 
         cap_rows = cap.rearrange("(a p t) m -> a p t m", a=2, t=PACK)
@@ -274,47 +274,54 @@ def tile_list_spill_slot_advisor_kernel(
             costs(0, [(2, j), (3, j)], 6 + j % 2, back[:])
             put(2, j, j, back[:, cols(0)])
             if j == PIECES - 1:
-                w2_back = held("w2_back", [P, PACK, 128, PACK], BF16, tag="e_grouped3")
-                for t0 in (0, 2):
-                    round_w2(nc.scalar.copy, 1, w2_back[:, t0 : t0 + 2], t0)
+                back_tags = ("e_grouped3", rows_tag(3))
+                w2_back = [held(f"w2_back{u}", [P, 2, 128, PACK], BF16, tag=back_tags[u]) for u in range(2)]
+                for u in range(2):
+                    round_w2(nc.scalar.copy, 1, w2_back[u][:], 2 * u)
                 cap1 = held("cap1", [P, PACK, PICKS], F32, tag="tab0")
                 nc.sync.dma_start(cap1[:], cap_rows[1])
                 w2_codes.append(held("w2_codes2", [P, 512], U32, tag="front31"))
-                quantize(w2_codes[2][:], w2_plane[1][:], w2_back[:].rearrange("p t m j -> p (t m j)"))
+                quantize(w2_codes[2][:, 0:256], w2_plane[1][:, 0:256], w2_back[0][:].rearrange("p t m j -> p (t m j)"))
             put(3, j, j, back[:, cols(1)])
+            if j == PIECES - 1:
+                quantize(w2_codes[2][:, 256:512], w2_plane[1][:, 256:512], w2_back[1][:].rearrange("p t m j -> p (t m j)"))
             if j == 1:
                 cap0 = held("cap0", [P, PACK, PICKS], F32, tag="tab_plane")
                 nc.sync.dma_start(cap0[:], cap_rows[0])
-                w3_plane = held("w3_plane", [P, 2, N], U8, tag="picked0")
+                w3_plane = held("w3_plane", [P, 2, N], U8, tag="e_first1")
                 nc.gpsimd.memset(w3_plane[:].rearrange("p a c -> p (a c)").bitcast(I32), 0)
                 load_scale_rows(w3_plane, w3_scales)
             if j == PIECES - 2:
                 w3_codes = held("w3_codes", [P, 2, N], I32, tag="v_plane1")
                 nc.sync.dma_start(w3_codes[:], w3_words.rearrange("a p c i -> p a (c i)").bitcast(I32))
 
-        h1 = [held(f"h1{t}", [P, S], F32) for t in range(PACK)]
-        for t in range(PACK):
+        def whole_costs(t, tag=None):
+            h = held(f"h1{t}", [P, S], F32, tag=tag)
             for half in range(2):
-                span = cols(2 * half, 2 * half + 1)
-                costs(1, [(t, 2 * half), (t, 2 * half + 1)], (2 * t + half) % 8, h1[t][:, span])
+                costs(1, [(t, 2 * half), (t, 2 * half + 1)], 2 * t + half, h[:, cols(2 * half, 2 * half + 1)])
+            return h
 
-        def limit(grouped, picked, caps):
-            nc.vector.tensor_tensor(by_word(grouped), by_row(picked), by_row(caps), ALU.min)
+        h1 = [whole_costs(0)]
 
-        x0 = held("x0", [P, PACK, PICKS], F32, tag="e_grouped3")
+        x0_tags = back_tags
+        x0 = [held(f"x0_{u}", [P, 2, PICKS], F32, tag=x0_tags[u]) for u in range(2)]
+        z0_rows = held("z0_rows", [P, PACK, PICKS], BF16, tag="tab1")
         z0 = held("z0", [P, PICKS, PACK], BF16)
         z_codes = [held(f"z_codes{a}", [P, PICKS], U32) for a in range(2)]
         z_plane = [held(f"z_plane{a}", [P, PICKS], U8) for a in range(2)]
         for t in range(PACK):
-            nc.vector.tensor_copy(x0[:, t, :], pages[t][:].indirect(idx3[:]))
-        for t in range(PACK):
-            put(t, 1, PIECES - 1, h1[t][:, cols(1, PIECES - 1)])
-            if t == 0:
-                limit(z0[:], x0[:], cap0[:])
-            if t == 1:
+            nc.vector.tensor_copy(x0[t // 2][:, t % 2, :], pages[t][:].indirect(idx3[:]))
+        put(0, 0, PIECES - 1, h1[0][:])
+        for u in range(2):
+            slots = slice(2 * u, 2 * u + 2)
+            nc.vector.tensor_tensor(z0_rows[:, slots, :], x0[u][:], cap0[:, slots, :], ALU.min)
+            h1.append(whole_costs(1 + u, x0_tags[u]))
+        nc.scalar.copy(by_word(z0[:]), by_row(z0_rows[:]))
+        h1.append(whole_costs(3, "tab1"))
+        for t in range(1, PACK):
+            if t == PACK - 1:
                 quantize(z_codes[0][:], z_plane[0][:], z0[:].rearrange("p n t -> p (n t)"))
-        for t in range(PACK):
-            put(t, 0, 0, h1[t][:, cols(0)])
+            put(t, 0, PIECES - 1, h1[t][:])
 
         out_rows = out.rearrange("(c p) m -> p c m", p=P)
         last = PIECES - 1
@@ -352,29 +359,45 @@ def tile_list_spill_slot_advisor_kernel(
                 nc.sync.dma_start(out_rows[:, 2 * pair : 2 * pair + 2, span], staged[:])
 
         opened = [open_scores(n) for n in range(PIECES)]
-        x1 = [held(f"x1{j}", [P, PACK, PIECE], F32, tag=(None, "th1", grouped_tag(1), grouped_tag(2))[j]) for j in range(PIECES)]
-        z1 = [held(f"z1{j}", [P, PIECE, PACK], BF16, tag=("front30", "front31", "front20", "front10")[j]) for j in range(PIECES)]
 
-        def fetch(j, t):
-            nc.vector.tensor_copy(x1[j][:, t, :], pages[t][:].indirect(idx3[:, entries(j)]))
+        def fetch(j, slots, tag):
+            picked = held(f"x1_{j}{slots[0]}", [P, len(slots), PIECE], F32, tag=tag)
+            for u, t in enumerate(slots):
+                nc.vector.tensor_copy(picked[:, u, :], pages[t][:].indirect(idx3[:, entries(j)]))
+            return picked
 
-        for t in range(PACK):
-            fetch(0, t)
-        for j in range(last):
-            finish_after = 1 if j + 1 < last else 3
-            for t in range(PACK):
-                fetch(j + 1, t)
-                if t == 0:
-                    limit(z1[j][:], x1[j][:], cap1[:, :, cols(j)])
-                if t == finish_after:
-                    finish(j, z1[j][:])
-                    store(j)
-            if j == 0:
+        def fetch_pairs(j):
+            return [fetch(j, (0, 1), "z0"), fetch(j, (2, 3), "tab1")]
+
+        def limit(j, pairs):
+            rows = held(f"z1_rows{j}", [P, PACK, PIECE], BF16, tag="z1_rows")
+            for u in range(2):
+                slots = slice(2 * u, 2 * u + 2)
+                nc.vector.tensor_tensor(rows[:, slots, :], pairs[u][:], cap1[:, slots, cols(j)], ALU.min)
+            grouped = held(f"z1_{j}", [P, PIECE, PACK], BF16, tag=f"th{j + 1}" if j == 0 else f"e_grouped{j}")
+            nc.scalar.copy(by_word(grouped[:]), by_row(rows[:]))
+            return grouped
+
+        def limit_last(picked, half, tag):
+            grouped = held(f"z1_last{half}", [P, HALF, PACK], BF16, tag=tag)
+            nc.vector.tensor_tensor(
+                by_word(grouped[:]),
+                by_row(picked[:, :, HALF * half : HALF * half + HALF]),
+                by_row(cap1[:, :, spans[last + half]]),
+                ALU.min,
+            )
+            return grouped
+
+        picked = fetch_pairs(0)
+        for n in range(last):
+            grouped = limit(n, picked)
+            picked = fetch_pairs(n + 1) if n + 1 < last else fetch(last, (0, 1, 2, 3), "z0")
+            finish(n, grouped[:])
+            store(n)
+            if n == 0:
                 opened.append(open_scores(PIECES))
+        halves = [limit_last(picked, 0, "z1_rows"), limit_last(picked, 1, None)]
         for half in range(2):
-            inner = slice(HALF * half, HALF * half + HALF)
-            limit(z1[last][:, inner, :], x1[last][:, :, inner], cap1[:, :, spans[last + half]])
-        for half in range(2):
-            finish(last + half, z1[last][:, HALF * half : HALF * half + HALF, :])
+            finish(last + half, halves[half][:])
         for half in range(2):
             store(last + half)

@@ -33,10 +33,14 @@ def tile_list_spill_slot_advisor_kernel(
     with ExitStack() as ctx:
         lists = ctx.enter_context(tc.tile_pool(name="lists", bufs=1))
         sb = ctx.enter_context(tc.tile_pool(name="sb", bufs=1))
+        shared = ctx.enter_context(tc.tile_pool(name="shared", bufs=1))
         psum = ctx.enter_context(tc.psum_pool(name="psum", bufs=1))
 
         def held(name, shape, dtype, tag=None):
             return sb.tile(shape, dtype, name=name, tag=tag or name, align_bytes=64)
+
+        def placed(name, shape, dtype, offset):
+            return shared.tile(shape, dtype, name=name, align_bytes=64, offset=offset)
 
         def bank(n, shape):
             return psum.tile(shape, F32, name=f"bank{n}", tag=f"bank{n}")
@@ -66,16 +70,16 @@ def tile_list_spill_slot_advisor_kernel(
 
         tab_plane = held("tab_plane", [P, T], U8)
         w1_plane_raw = held("w1_plane_raw", [P, 2, M], U8)
-        v_plane = [held(f"v_plane{a}", [P, S], U8) for a in range(2)]
+        shifted = [held("shifted_first", [P, PIECE], U8), held("shifted_rest", [P, S - PIECE], U8)]
         warm_in = held("warm_in", [P, 1], F32)
         warm_out = held("warm_out", [P, 1], F32)
+        nc.gpsimd.memset(tab_plane[:].bitcast(I32), 0)
         nc.gpsimd.memset(w1_plane_raw[:].rearrange("p a c -> p (a c)").bitcast(I32), 0)
         nc.vector.memset(warm_in[:], 0.0)
         nc.scalar.activation(warm_out[:], warm_in[:], ACT.Tanh)
-        for q in range(4):
-            nc.vector.memset(tab_plane[32 * q : 32 * q + 24, :].bitcast(I32), 0)
-        for a in range(2):
-            nc.vector.memset(v_plane[a][96:128, :].bitcast(I32), 0)
+        for plane in shifted:
+            nc.gpsimd.memset(plane[96:128, :].bitcast(I32), 0)
+        zeroed_page(nc.gpsimd)
 
         idx = lists.tile([P, S // 16], U16, name="idx")
         idx2 = lists.tile([P, S // 16], U16, name="idx2")
@@ -94,64 +98,61 @@ def tile_list_spill_slot_advisor_kernel(
                 )
 
         nc.sync.dma_start(idx[:], offs)
+        nc.sync.dma_start(w1_raw[:], w1_words.rearrange("a p b -> p a b").bitcast(I32))
+        nc.sync.dma_start(idx2[:], offs2)
         for q in range(4):
             nc.sync.dma_start(
-                tab_plane[32 * q + 24 : 32 * q + 32, :].bitcast(I32), tab_scales[:, 4 * q : 4 * q + 4, :].bitcast(I32)
+                tab_plane[32 * q : 32 * q + 8, :].bitcast(I32), tab_scales[:, 4 * q : 4 * q + 4, :].bitcast(I32)
             )
-        nc.sync.dma_start(idx2[:], offs2)
-        nc.sync.dma_start(idx3[:], offs3)
         nc.sync.dma_start(tab[0][:], tab_words[0].rearrange("p t i -> p (t i)").bitcast(I32))
-        nc.sync.dma_start(w1_raw[:], w1_words.rearrange("a p b -> p a b").bitcast(I32))
+        nc.sync.dma_start(idx3[:], offs3)
         load_scale_rows(w1_plane_raw, w1_scales)
         nc.sync.dma_start(tab[1][:], tab_words[1].rearrange("p t i -> p (t i)").bitcast(I32))
         nc.sync.dma_start(b1_sb[:], b1.rearrange("(p t) -> p t", t=PACK))
         nc.sync.dma_start(gain_sb[:], gain.rearrange("(p t) -> p t", t=PACK))
-        zeroed_page(nc.gpsimd, "warm_in")
-        zeroed_page(nc.gpsimd, "warm_out")
+
+        v_plane = [[], [shifted[0][:]] + [shifted[1][:, cols(j)] for j in range(PIECES - 1)]]
 
         def pick_scales(first, last):
             picked = held(f"picked{first}", [P, (last - first + 1) * PIECE], U8)
             nc.vector.tensor_copy(picked[:], tab_plane[:].indirect(idx[:, entries(first, last)]))
-            for a in range(2):
-                shift = 24 + 4 * a
-                nc.sync.dma_start(
-                    v_plane[a][0 : P - shift, cols(first, last)].bitcast(I32), picked[shift:P, :].bitcast(I32)
-                )
+            v_plane[0].extend(picked[:, cols(j)] for j in range(last - first + 1))
+            return picked
+
+        def shift(picked, plane):
+            nc.sync.dma_start(plane[0:112, :].bitcast(I32), picked[4:116, :].bitcast(I32))
 
         v_codes = [[], []]
 
-        def pick_words(passes, first, last, tag=None):
-            width = (last - first + 1) * PIECE
-            codes = held(f"v{passes[0]}_{first}", [P, len(passes) * width], U32, tag=tag)
-            for u, a in enumerate(passes):
-                part = codes[:, u * width : (u + 1) * width]
-                nc.vector.tensor_copy(part, tab[a][:].bitcast(U32).indirect(idx[:, entries(first, last)]))
-                v_codes[a].extend(part[:, cols(j)] for j in range(last - first + 1))
+        def pick_words(a, first, last, offset=None):
+            shape = [P, (last - first + 1) * PIECE]
+            codes = held(f"v{a}_{first}", shape, U32) if offset is None else placed(f"v{a}_{first}", shape, U32, offset)
+            nc.vector.tensor_copy(codes[:], tab[a][:].bitcast(U32).indirect(idx[:, entries(first, last)]))
+            v_codes[a].extend(codes[:, cols(j)] for j in range(last - first + 1))
 
-        pick_scales(0, PIECES - 1)
-        w2_raw = [held("w2_raw0", [P, PACK, 512], F32, tag="tab_plane")]
-        nc.sync.dma_start(w2_raw[0][:], w2_rows[:, :, 0:512])
-        pick_words((0,), 0, 1)
         w1_codes = held("w1_codes", [P, 2, M // 2], I32)
         nc.vector.tensor_copy(
             w1_codes[:].bitcast(U16).rearrange("p a (t m) -> p a m t", t=PACK),
             w1_raw[:].bitcast(U16).rearrange("p a (m t) -> p a m t", t=PACK),
         )
+        zeroed_page(nc.gpsimd, "w1_raw")
+        shift(pick_scales(0, 0), shifted[0])
+        picked_rest = pick_scales(1, PIECES - 1)
+        w2_raw = [held("w2_raw0", [P, PACK, 512], F32, tag="tab_plane")]
+        nc.sync.dma_start(w2_raw[0][:], w2_rows[:, :, 0:512])
+        shift(picked_rest, shifted[1])
         w1_plane = held("w1_plane", [P, 2, M], U8)
         nc.vector.tensor_copy(
             w1_plane[:].rearrange("p a (t m) -> p a m t", t=PACK),
             w1_plane_raw[:].rearrange("p a (m t) -> p a m t", t=PACK),
         )
         zeroed_page(nc.gpsimd, "w1_plane_raw")
-        pick_words((1,), 0, 0)
-        pick_words((1,), 1, 1)
-        pick_words((0,), 2, PIECES - 1, tag="picked0")
+        pick_words(0, 0, 0)
+        pick_words(1, 0, 0)
+        pick_words(0, 1, 1)
+        pick_words(1, 1, PIECES - 1)
 
         wgs_rows = wgs.rearrange("(p t) s -> p t s", t=PACK)
-        wgs_sb = held("wgs_sb", [P, PACK, S], F32, tag="w1_raw")
-        for span in (cols(0), cols(1, PIECES - 1)):
-            for q in (0, 2, 1, 3):
-                nc.sync.dma_start(wgs_sb[32 * q : 32 * q + 32, :, span], wgs_rows[:, :, span])
 
         def first_product(dst, j, slots, halves):
             steps = [(a, u, n) for a in range(2) for u in range(len(slots)) for n in range(len(halves))]
@@ -162,7 +163,7 @@ def tile_list_spill_slot_advisor_kernel(
                     lhsT=w1_codes[:, a, 64 * t : 64 * t + 64].bitcast(FP4X4),
                     lhsT_scale=w1_plane[:, a, 128 * t : 128 * t + 128],
                     rhs=v_codes[a][j][:, c0 : c0 + HALF].bitcast(FP8X4),
-                    rhs_scale=v_plane[a][:, j * PIECE + c0 : j * PIECE + c0 + HALF],
+                    rhs_scale=v_plane[a][j][:, c0 : c0 + HALF],
                     start=((a, u, n) == steps[0]),
                     stop=((a, u, n) == steps[-1]),
                 )
@@ -184,7 +185,12 @@ def tile_list_spill_slot_advisor_kernel(
             th0.append(held(f"th0{half}", [P, PACK, HALF], F32))
             for t in range(PACK):
                 nc.scalar.activation(th0[half][:, t, :], pre[:, t, :], ACT.Tanh, bias=b1_sb[:, t : t + 1])
-        w2_front = [held(f"w2_front{u}", [P, 2, 128, PACK], BF16) for u in range(2)]
+        wgs_sb = held("wgs_sb", [P, PACK, S], F32, tag="v0_0")
+        for span in (cols(0), cols(1), cols(2, PIECES - 1)):
+            for q in (0, 2, 1, 3):
+                nc.sync.dma_start(wgs_sb[32 * q : 32 * q + 32, :, span], wgs_rows[:, :, span])
+
+        w2_front = [placed("w2_front0", [P, 2, 128, PACK], BF16, 1024), held("w2_front1", [P, 2, 128, PACK], BF16)]
         round_w2(nc.vector.tensor_copy, 0, w2_front[0][:], 0)
         round_w2(nc.scalar.copy, 0, w2_front[1][:], 2)
         e_first = [held(f"e_first{half}", [P, HALF, PACK], BF16) for half in range(2)]
@@ -200,8 +206,8 @@ def tile_list_spill_slot_advisor_kernel(
         for half in range(2):
             span = slice(HALF * half, HALF * half + HALF)
             quantize(e_codes[0][:, span], e_plane[:, span], e_first[half][:].rearrange("p n t -> p (n t)"))
-        pick_words((1,), 2, PIECES - 1, tag="e_first0")
-        w2_codes.append(held("w2_codes1", [P, 256], U32, tag="tab1"))
+        pick_words(0, 2, PIECES - 1, offset=2048)
+        w2_codes.append(held("w2_codes1", [P, 256], U32, tag="tab0"))
         quantize(w2_codes[1][:], w2_plane[0][:, 256:512], w2_front[1][:].rearrange("p t m j -> p (t m j)"))
         zeroed_page(nc.gpsimd, "w2_front1")
 
@@ -222,10 +228,11 @@ def tile_list_spill_slot_advisor_kernel(
             return th
 
         def rows_tag(j):
-            return "w2_front0" if j == 1 else f"e_rows{j}"
+            return f"e_rows{j}"
 
         def features(j, th):
-            e_rows = held(f"e_rows{j}", [P, PACK, PIECE], BF16, tag=rows_tag(j))
+            shape = [P, PACK, PIECE]
+            e_rows = placed("e_rows1", shape, BF16, 0) if j == 1 else held(f"e_rows{j}", shape, BF16)
             for t in range(PACK):
                 nc.scalar.activation(e_rows[:, t, :], th[:, t, :], ACT.Copy, scale=gain_sb[:, t : t + 1])
             e_grouped = held(f"e_grouped{j}", [P, PIECE, PACK], BF16)
@@ -239,7 +246,7 @@ def tile_list_spill_slot_advisor_kernel(
             return w2_codes[2][:, 128 * t : 128 * t + 128]
 
         def front_tag(j, t):
-            return {(0, 1): "tab0", (1, 1): "tab_plane"}.get((j, t))
+            return {(0, 1): "tab1", (1, 1): "tab_plane"}.get((j, t))
 
         def costs(a, parts, n, dst):
             acc = bank(n, [P, len(parts) * PIECE])
@@ -266,11 +273,12 @@ def tile_list_spill_slot_advisor_kernel(
                 costs(0, [(t, j)], front_bank(j) + t, front[:])
                 put(t, j, j, front[:])
             if j == 0:
-                w2_raw.append(held("w2_raw1", [P, PACK, 512], F32, tag="tab0"))
+                w2_raw.append(held("w2_raw1", [P, PACK, 512], F32, tag="tab1"))
                 nc.sync.dma_start(w2_raw[1][:], w2_rows[:, :, 512:1024])
             if j + 1 < PIECES:
                 features(j + 1, squash(j + 1))
-            back = held(f"back{j}", [P, 2 * PIECE], F32, tag=rows_tag(j + 1))
+            shape = [P, 2 * PIECE]
+            back = placed("back0", shape, F32, 0) if j == 0 else held(f"back{j}", shape, F32, tag=rows_tag(j + 1))
             costs(0, [(2, j), (3, j)], 6 + j % 2, back[:])
             put(2, j, j, back[:, cols(0)])
             if j == PIECES - 1:
@@ -278,7 +286,7 @@ def tile_list_spill_slot_advisor_kernel(
                 w2_back = [held(f"w2_back{u}", [P, 2, 128, PACK], BF16, tag=back_tags[u]) for u in range(2)]
                 for u in range(2):
                     round_w2(nc.scalar.copy, 1, w2_back[u][:], 2 * u)
-                cap1 = held("cap1", [P, PACK, PICKS], F32, tag="tab0")
+                cap1 = held("cap1", [P, PACK, PICKS], F32, tag="tab1")
                 nc.sync.dma_start(cap1[:], cap_rows[1])
                 w2_codes.append(held("w2_codes2", [P, 512], U32, tag="front31"))
                 quantize(w2_codes[2][:, 0:256], w2_plane[1][:, 0:256], w2_back[0][:].rearrange("p t m j -> p (t m j)"))
@@ -288,11 +296,11 @@ def tile_list_spill_slot_advisor_kernel(
             if j == 1:
                 cap0 = held("cap0", [P, PACK, PICKS], F32, tag="tab_plane")
                 nc.sync.dma_start(cap0[:], cap_rows[0])
-                w3_plane = held("w3_plane", [P, 2, N], U8, tag="e_first1")
+            if j == PIECES - 2:
+                w3_plane = held("w3_plane", [P, 2, N], U8, tag=rows_tag(2))
                 nc.gpsimd.memset(w3_plane[:].rearrange("p a c -> p (a c)").bitcast(I32), 0)
                 load_scale_rows(w3_plane, w3_scales)
-            if j == PIECES - 2:
-                w3_codes = held("w3_codes", [P, 2, N], I32, tag="v_plane1")
+                w3_codes = held("w3_codes", [P, 2, N], I32, tag="shifted_rest")
                 nc.sync.dma_start(w3_codes[:], w3_words.rearrange("a p c i -> p a (c i)").bitcast(I32))
 
         def whole_costs(t, tag=None):
@@ -305,7 +313,7 @@ def tile_list_spill_slot_advisor_kernel(
 
         x0_tags = back_tags
         x0 = [held(f"x0_{u}", [P, 2, PICKS], F32, tag=x0_tags[u]) for u in range(2)]
-        z0_rows = held("z0_rows", [P, PACK, PICKS], BF16, tag="tab1")
+        z0_rows = held("z0_rows", [P, PACK, PICKS], BF16, tag="tab0")
         z0 = held("z0", [P, PICKS, PACK], BF16)
         z_codes = [held(f"z_codes{a}", [P, PICKS], U32) for a in range(2)]
         z_plane = [held(f"z_plane{a}", [P, PICKS], U8) for a in range(2)]
@@ -317,7 +325,7 @@ def tile_list_spill_slot_advisor_kernel(
             nc.vector.tensor_tensor(z0_rows[:, slots, :], x0[u][:], cap0[:, slots, :], ALU.min)
             h1.append(whole_costs(1 + u, x0_tags[u]))
         nc.scalar.copy(by_word(z0[:]), by_row(z0_rows[:]))
-        h1.append(whole_costs(3, "tab1"))
+        h1.append(whole_costs(3, "tab0"))
         for t in range(1, PACK):
             if t == PACK - 1:
                 quantize(z_codes[0][:], z_plane[0][:], z0[:].rearrange("p n t -> p (n t)"))
@@ -367,7 +375,7 @@ def tile_list_spill_slot_advisor_kernel(
             return picked
 
         def fetch_pairs(j):
-            return [fetch(j, (0, 1), "z0"), fetch(j, (2, 3), "tab1")]
+            return [fetch(j, (0, 1), "z0"), fetch(j, (2, 3), "tab0")]
 
         def limit(j, pairs):
             rows = held(f"z1_rows{j}", [P, PACK, PIECE], BF16, tag="z1_rows")

@@ -62,8 +62,9 @@ def tile_list_spill_slot_advisor_kernel(
 
         pages = []
 
-        def zeroed_page(engine, tag=None):
-            page = held(f"page{len(pages)}", [P, T2], F32, tag=tag)
+        def zeroed_page(engine, tag=None, offset=None):
+            name = f"page{len(pages)}"
+            page = held(name, [P, T2], F32, tag=tag) if offset is None else placed(name, [P, T2], F32, offset)
             for c0 in range(0, T2, 512):
                 engine.memset(page[:, c0 : c0 + 512], 0.0)
             pages.append(page)
@@ -142,10 +143,11 @@ def tile_list_spill_slot_advisor_kernel(
         nc.sync.dma_start(w2_raw[0][:], w2_rows[:, :, 0:512])
         shift(picked_rest, shifted[1])
         w1_plane = held("w1_plane", [P, 2, M], U8)
-        nc.vector.tensor_copy(
-            w1_plane[:].rearrange("p a (t m) -> p a m t", t=PACK),
-            w1_plane_raw[:].rearrange("p a (m t) -> p a m t", t=PACK),
-        )
+        for a in range(2):
+            nc.gpsimd.tensor_copy(
+                w1_plane[:, a, :].rearrange("p (t m) -> p t m", t=PACK),
+                w1_plane_raw[:, a, :].rearrange("p (m t) -> p t m", t=PACK),
+            )
         zeroed_page(nc.gpsimd, "w1_plane_raw")
         pick_words(0, 0, 0)
         pick_words(1, 0, 0)
@@ -190,8 +192,8 @@ def tile_list_spill_slot_advisor_kernel(
             for q in (0, 2, 1, 3):
                 nc.sync.dma_start(wgs_sb[32 * q : 32 * q + 32, :, span], wgs_rows[:, :, span])
 
-        w2_front = [placed("w2_front0", [P, 2, 128, PACK], BF16, 1024), held("w2_front1", [P, 2, 128, PACK], BF16)]
-        round_w2(nc.vector.tensor_copy, 0, w2_front[0][:], 0)
+        w2_front = [placed("w2_front0", [P, 2, 128, PACK], BF16, 7168), held("w2_front1", [P, 2, 128, PACK], BF16)]
+        round_w2(nc.scalar.copy, 0, w2_front[0][:], 0)
         round_w2(nc.scalar.copy, 0, w2_front[1][:], 2)
         e_first = [held(f"e_first{half}", [P, HALF, PACK], BF16) for half in range(2)]
         for half in range(2):
@@ -201,15 +203,12 @@ def tile_list_spill_slot_advisor_kernel(
                 gain_sb[:].unsqueeze(1).unsqueeze(3).to_broadcast([P, HALF // 4, PACK, 4]),
                 ALU.mult,
             )
-            if half == 0:
-                quantize(w2_codes[0][:], w2_plane[0][:, 0:256], w2_front[0][:].rearrange("p t m j -> p (t m j)"))
         for half in range(2):
             span = slice(HALF * half, HALF * half + HALF)
             quantize(e_codes[0][:, span], e_plane[:, span], e_first[half][:].rearrange("p n t -> p (n t)"))
-        pick_words(0, 2, PIECES - 1, offset=2048)
-        w2_codes.append(held("w2_codes1", [P, 256], U32, tag="tab0"))
-        quantize(w2_codes[1][:], w2_plane[0][:, 256:512], w2_front[1][:].rearrange("p t m j -> p (t m j)"))
-        zeroed_page(nc.gpsimd, "w2_front1")
+        quantize(w2_codes[0][:], w2_plane[0][:, 0:256], w2_front[0][:].rearrange("p t m j -> p (t m j)"))
+        pick_words(0, 2, PIECES - 1, offset=8192)
+        zeroed_page(nc.gpsimd, offset=0)
 
         def front_bank(j):
             return 0 if j % 2 else 4
@@ -218,7 +217,7 @@ def tile_list_spill_slot_advisor_kernel(
             return f"e_grouped{j}"
 
         def squash(j):
-            th = held(f"th{j}", [P, PACK, PIECE], F32, tag=grouped_tag(j - 1) if j > 1 else None)
+            th = held(f"th{j}", [P, PACK, PIECE], F32, tag=grouped_tag(j - 1) if j > 1 else "tab_plane")
             for pair in range(2):
                 pre = bank(2 + pair if j == 1 else front_bank(j - 2) + pair, [P, 2, PIECE])
                 first_product(pre, j, (2 * pair, 2 * pair + 1), (0, 1))
@@ -231,13 +230,15 @@ def tile_list_spill_slot_advisor_kernel(
             return f"e_rows{j}"
 
         def features(j, th):
-            shape = [P, PACK, PIECE]
-            e_rows = placed("e_rows1", shape, BF16, 0) if j == 1 else held(f"e_rows{j}", shape, BF16)
+            e_rows = held(f"e_rows{j}", [P, PACK, PIECE], BF16)
             for t in range(PACK):
                 nc.scalar.activation(e_rows[:, t, :], th[:, t, :], ACT.Copy, scale=gain_sb[:, t : t + 1])
             e_grouped = held(f"e_grouped{j}", [P, PIECE, PACK], BF16)
             nc.scalar.copy(by_word(e_grouped[:]), by_row(e_rows[:]))
-            e_codes.append(held(f"e_codes{j}", [P, PIECE], U32, tag=f"front{j - 1}0"))
+            if j == 1:
+                e_codes.append(placed("e_codes1", [P, PIECE], U32, 11264))
+            else:
+                e_codes.append(held(f"e_codes{j}", [P, PIECE], U32, tag=f"front{j - 1}0"))
             quantize(e_codes[j][:], e_plane[:, cols(j)], e_grouped[:].rearrange("p n t -> p (n t)"))
 
         def w2_slot(a, t):
@@ -268,19 +269,26 @@ def tile_list_spill_slot_advisor_kernel(
 
         cap_rows = cap.rearrange("(a p t) m -> a p t m", a=2, t=PACK)
         for j in range(PIECES):
-            for t in range(2):
-                front = held(f"front{j}{t}", [P, PIECE], F32, tag=front_tag(j, t))
+            ahead = 3 if j == 0 else 2
+            for t in range(ahead):
+                if (j, t) == (0, 0):
+                    front = placed("front00", [P, PIECE], F32, 10752)
+                else:
+                    front = held(f"front{j}{t}", [P, PIECE], F32, tag=front_tag(j, t))
                 costs(0, [(t, j)], front_bank(j) + t, front[:])
                 put(t, j, j, front[:])
-            if j == 0:
-                w2_raw.append(held("w2_raw1", [P, PACK, 512], F32, tag="tab1"))
-                nc.sync.dma_start(w2_raw[1][:], w2_rows[:, :, 512:1024])
+                if (j, t) == (0, 0):
+                    w2_codes.append(placed("w2_codes1", [P, 256], U32, 10240))
+                    quantize(w2_codes[1][:], w2_plane[0][:, 256:512], w2_front[1][:].rearrange("p t m j -> p (t m j)"))
+                if (j, t) == (0, 1):
+                    w2_raw.append(held("w2_raw1", [P, PACK, 512], F32, tag="tab1"))
+                    nc.sync.dma_start(w2_raw[1][:], w2_rows[:, :, 512:1024])
             if j + 1 < PIECES:
                 features(j + 1, squash(j + 1))
-            shape = [P, 2 * PIECE]
-            back = placed("back0", shape, F32, 0) if j == 0 else held(f"back{j}", shape, F32, tag=rows_tag(j + 1))
-            costs(0, [(2, j), (3, j)], 6 + j % 2, back[:])
-            put(2, j, j, back[:, cols(0)])
+            back = held(f"back{j}", [P, (PACK - ahead) * PIECE], F32, tag=rows_tag(j + 1))
+            costs(0, [(t, j) for t in range(ahead, PACK)], 7 - j % 2, back[:])
+            if ahead == 2:
+                put(2, j, j, back[:, cols(0)])
             if j == PIECES - 1:
                 back_tags = ("e_grouped3", rows_tag(3))
                 w2_back = [held(f"w2_back{u}", [P, 2, 128, PACK], BF16, tag=back_tags[u]) for u in range(2)]
@@ -290,7 +298,7 @@ def tile_list_spill_slot_advisor_kernel(
                 nc.sync.dma_start(cap1[:], cap_rows[1])
                 w2_codes.append(held("w2_codes2", [P, 512], U32, tag="front31"))
                 quantize(w2_codes[2][:, 0:256], w2_plane[1][:, 0:256], w2_back[0][:].rearrange("p t m j -> p (t m j)"))
-            put(3, j, j, back[:, cols(1)])
+            put(3, j, j, back[:, cols(PACK - 1 - ahead)])
             if j == PIECES - 1:
                 quantize(w2_codes[2][:, 256:512], w2_plane[1][:, 256:512], w2_back[1][:].rearrange("p t m j -> p (t m j)"))
             if j == 1:

@@ -33,14 +33,10 @@ def tile_list_spill_slot_advisor_kernel(
     with ExitStack() as ctx:
         lists = ctx.enter_context(tc.tile_pool(name="lists", bufs=1))
         sb = ctx.enter_context(tc.tile_pool(name="sb", bufs=1))
-        shared = ctx.enter_context(tc.tile_pool(name="shared", bufs=1))
         psum = ctx.enter_context(tc.psum_pool(name="psum", bufs=1))
 
         def held(name, shape, dtype, tag=None):
             return sb.tile(shape, dtype, name=name, tag=tag or name, align_bytes=64)
-
-        def placed(name, shape, dtype, offset):
-            return shared.tile(shape, dtype, name=name, align_bytes=64, offset=offset)
 
         def bank(n, shape):
             return psum.tile(shape, F32, name=f"bank{n}", tag=f"bank{n}")
@@ -62,9 +58,8 @@ def tile_list_spill_slot_advisor_kernel(
 
         pages = []
 
-        def zeroed_page(engine, tag=None, offset=None):
-            name = f"page{len(pages)}"
-            page = held(name, [P, T2], F32, tag=tag) if offset is None else placed(name, [P, T2], F32, offset)
+        def zeroed_page(engine, tag=None):
+            page = held(f"page{len(pages)}", [P, T2], F32, tag=tag)
             for c0 in range(0, T2, 512):
                 engine.memset(page[:, c0 : c0 + 512], 0.0)
             pages.append(page)
@@ -125,9 +120,8 @@ def tile_list_spill_slot_advisor_kernel(
 
         v_codes = [[], []]
 
-        def pick_words(a, first, last, offset=None):
-            shape = [P, (last - first + 1) * PIECE]
-            codes = held(f"v{a}_{first}", shape, U32) if offset is None else placed(f"v{a}_{first}", shape, U32, offset)
+        def pick_words(a, first, last, tag=None):
+            codes = held(f"v{a}_{first}", [P, (last - first + 1) * PIECE], U32, tag=tag)
             nc.vector.tensor_copy(codes[:], tab[a][:].bitcast(U32).indirect(idx[:, entries(first, last)]))
             v_codes[a].extend(codes[:, cols(j)] for j in range(last - first + 1))
 
@@ -151,7 +145,7 @@ def tile_list_spill_slot_advisor_kernel(
         zeroed_page(nc.gpsimd, "w1_plane_raw")
         pick_words(0, 0, 0)
         pick_words(1, 0, 0)
-        pick_words(0, 1, 1)
+        pick_words(0, 1, 2)
         pick_words(1, 1, PIECES - 1)
 
         wgs_rows = wgs.rearrange("(p t) s -> p t s", t=PACK)
@@ -182,17 +176,17 @@ def tile_list_spill_slot_advisor_kernel(
         w2_plane = [held(f"w2_plane{a}", [P, 512], U8) for a in range(2)]
         th0 = []
         for half in range(2):
-            pre = bank(half, [P, PACK, HALF])
-            first_product(pre, 0, range(PACK), (half,))
             th0.append(held(f"th0{half}", [P, PACK, HALF], F32))
             for t in range(PACK):
-                nc.scalar.activation(th0[half][:, t, :], pre[:, t, :], ACT.Tanh, bias=b1_sb[:, t : t + 1])
+                pre = bank(PACK * half + t, [P, 1, HALF])
+                first_product(pre, 0, (t,), (half,))
+                nc.scalar.activation(th0[half][:, t, :], pre[:, 0, :], ACT.Tanh, bias=b1_sb[:, t : t + 1])
         wgs_sb = held("wgs_sb", [P, PACK, S], F32, tag="v0_0")
         for span in (cols(0), cols(1), cols(2, PIECES - 1)):
             for q in (0, 2, 1, 3):
                 nc.sync.dma_start(wgs_sb[32 * q : 32 * q + 32, :, span], wgs_rows[:, :, span])
 
-        w2_front = [placed("w2_front0", [P, 2, 128, PACK], BF16, 7168), held("w2_front1", [P, 2, 128, PACK], BF16)]
+        w2_front = [held(f"w2_front{u}", [P, 2, 128, PACK], BF16) for u in range(2)]
         round_w2(nc.scalar.copy, 0, w2_front[0][:], 0)
         round_w2(nc.scalar.copy, 0, w2_front[1][:], 2)
         e_first = [held(f"e_first{half}", [P, HALF, PACK], BF16) for half in range(2)]
@@ -207,8 +201,7 @@ def tile_list_spill_slot_advisor_kernel(
             span = slice(HALF * half, HALF * half + HALF)
             quantize(e_codes[0][:, span], e_plane[:, span], e_first[half][:].rearrange("p n t -> p (n t)"))
         quantize(w2_codes[0][:], w2_plane[0][:, 0:256], w2_front[0][:].rearrange("p t m j -> p (t m j)"))
-        pick_words(0, 2, PIECES - 1, offset=8192)
-        zeroed_page(nc.gpsimd, offset=0)
+        pick_words(0, 3, 3, tag="w2_front0")
 
         def front_bank(j):
             return 0 if j % 2 else 4
@@ -235,10 +228,7 @@ def tile_list_spill_slot_advisor_kernel(
                 nc.scalar.activation(e_rows[:, t, :], th[:, t, :], ACT.Copy, scale=gain_sb[:, t : t + 1])
             e_grouped = held(f"e_grouped{j}", [P, PIECE, PACK], BF16)
             nc.scalar.copy(by_word(e_grouped[:]), by_row(e_rows[:]))
-            if j == 1:
-                e_codes.append(placed("e_codes1", [P, PIECE], U32, 11264))
-            else:
-                e_codes.append(held(f"e_codes{j}", [P, PIECE], U32, tag=f"front{j - 1}0"))
+            e_codes.append(held(f"e_codes{j}", [P, PIECE], U32, tag=f"front{j - 1}0"))
             quantize(e_codes[j][:], e_plane[:, cols(j)], e_grouped[:].rearrange("p n t -> p (n t)"))
 
         def w2_slot(a, t):
@@ -249,7 +239,7 @@ def tile_list_spill_slot_advisor_kernel(
         def front_tag(j, t):
             return {(0, 1): "tab1", (1, 1): "tab_plane"}.get((j, t))
 
-        def costs(a, parts, n, dst):
+        def costs(a, parts, n, dst, copy=nc.scalar.copy):
             acc = bank(n, [P, len(parts) * PIECE])
             for u, (t, j) in enumerate(parts):
                 nc.tensor.matmul_mx(
@@ -261,7 +251,7 @@ def tile_list_spill_slot_advisor_kernel(
                     start=True,
                     stop=True,
                 )
-            nc.scalar.copy(dst, acc[:])
+            copy(dst, acc[:])
 
         def put(t, first, last, values):
             weights = wgs_sb[:, t, cols(first, last)]
@@ -271,15 +261,14 @@ def tile_list_spill_slot_advisor_kernel(
         for j in range(PIECES):
             ahead = 3 if j == 0 else 2
             for t in range(ahead):
-                if (j, t) == (0, 0):
-                    front = placed("front00", [P, PIECE], F32, 10752)
-                else:
-                    front = held(f"front{j}{t}", [P, PIECE], F32, tag=front_tag(j, t))
-                costs(0, [(t, j)], front_bank(j) + t, front[:])
-                put(t, j, j, front[:])
-                if (j, t) == (0, 0):
-                    w2_codes.append(placed("w2_codes1", [P, 256], U32, 10240))
+                front = held(f"front{j}{t}", [P, PIECE], F32, tag=front_tag(j, t))
+                very_first = (j, t) == (0, 0)
+                costs(0, [(t, j)], front_bank(j) + t, front[:], nc.vector.tensor_copy if very_first else nc.scalar.copy)
+                if very_first:
+                    w2_codes.append(held("w2_codes1", [P, 256], U32, tag="tab0"))
                     quantize(w2_codes[1][:], w2_plane[0][:, 256:512], w2_front[1][:].rearrange("p t m j -> p (t m j)"))
+                    zeroed_page(nc.gpsimd, "w2_front1")
+                put(t, j, j, front[:])
                 if (j, t) == (0, 1):
                     w2_raw.append(held("w2_raw1", [P, PACK, 512], F32, tag="tab1"))
                     nc.sync.dma_start(w2_raw[1][:], w2_rows[:, :, 512:1024])

@@ -33,9 +33,14 @@ def tile_list_spill_slot_advisor_kernel(
     with ExitStack() as ctx:
         lists = ctx.enter_context(tc.tile_pool(name="lists", bufs=1))
         sb = ctx.enter_context(tc.tile_pool(name="sb", bufs=1))
+        shared = ctx.enter_context(tc.tile_pool(name="shared", bufs=1))
         psum = ctx.enter_context(tc.psum_pool(name="psum", bufs=1))
 
+        places = {"cap0": 0, "w2_raw0": 8192, "th1": 8192, "front11": 8192, "tab_plane": 15360, "wgs_sb": 16384}
+
         def held(name, shape, dtype, tag=None):
+            if name in places:
+                return shared.tile(shape, dtype, name=name, align_bytes=64, offset=places[name])
             return sb.tile(shape, dtype, name=name, tag=tag or name, align_bytes=64)
 
         def bank(n, shape):
@@ -60,8 +65,7 @@ def tile_list_spill_slot_advisor_kernel(
 
         def zeroed_page(engine, tag=None):
             page = held(f"page{len(pages)}", [P, T2], F32, tag=tag)
-            for c0 in range(0, T2, 512):
-                engine.memset(page[:, c0 : c0 + 512], 0.0)
+            engine.memset(page[:], 0.0)
             pages.append(page)
 
         tab_plane = held("tab_plane", [P, T], U8)
@@ -74,7 +78,7 @@ def tile_list_spill_slot_advisor_kernel(
         nc.vector.memset(warm_in[:], 0.0)
         nc.scalar.activation(warm_out[:], warm_in[:], ACT.Tanh)
         for plane in shifted:
-            nc.gpsimd.memset(plane[96:128, :].bitcast(I32), 0)
+            nc.vector.memset(plane[96:128, :].bitcast(I32), 0)
         zeroed_page(nc.gpsimd)
 
         idx = lists.tile([P, S // 16], U16, name="idx")
@@ -135,7 +139,18 @@ def tile_list_spill_slot_advisor_kernel(
         picked_rest = pick_scales(1, PIECES - 1)
         w2_raw = [held("w2_raw0", [P, PACK, 512], F32, tag="tab_plane")]
         nc.sync.dma_start(w2_raw[0][:], w2_rows[:, :, 0:512])
+        wgs_rows = wgs.rearrange("(p t) s -> p t s", t=PACK)
+        wgs_sb = held("wgs_sb", [P, PACK, S], F32)
+
+        def load_weights(slots, span):
+            for q in (0, 2, 1, 3):
+                nc.sync.dma_start(wgs_sb[32 * q : 32 * q + 32, slots, span], wgs_rows[:, slots, span])
+
         shift(picked_rest, shifted[1])
+        load_weights(slice(0, 2), cols(0))
+        load_weights(slice(2, PACK), cols(0))
+        load_weights(slice(0, PACK), cols(1))
+        load_weights(slice(0, PACK), cols(2, PIECES - 1))
         w1_plane = held("w1_plane", [P, 2, M], U8)
         for a in range(2):
             nc.gpsimd.tensor_copy(
@@ -148,7 +163,6 @@ def tile_list_spill_slot_advisor_kernel(
         pick_words(0, 1, 2)
         pick_words(1, 1, PIECES - 1)
 
-        wgs_rows = wgs.rearrange("(p t) s -> p t s", t=PACK)
 
         def first_product(dst, j, slots, halves):
             steps = [(a, u, n) for a in range(2) for u in range(len(slots)) for n in range(len(halves))]
@@ -181,11 +195,6 @@ def tile_list_spill_slot_advisor_kernel(
                 pre = bank(PACK * half + t, [P, 1, HALF])
                 first_product(pre, 0, (t,), (half,))
                 nc.scalar.activation(th0[half][:, t, :], pre[:, 0, :], ACT.Tanh, bias=b1_sb[:, t : t + 1])
-        wgs_sb = held("wgs_sb", [P, PACK, S], F32, tag="v0_0")
-        for span in (cols(0), cols(1), cols(2, PIECES - 1)):
-            for q in (0, 2, 1, 3):
-                nc.sync.dma_start(wgs_sb[32 * q : 32 * q + 32, :, span], wgs_rows[:, :, span])
-
         w2_front = [held(f"w2_front{u}", [P, 2, 128, PACK], BF16) for u in range(2)]
         round_w2(nc.scalar.copy, 0, w2_front[0][:], 0)
         round_w2(nc.scalar.copy, 0, w2_front[1][:], 2)

@@ -36,7 +36,9 @@ def tile_list_spill_slot_advisor_kernel(
         shared = ctx.enter_context(tc.tile_pool(name="shared", bufs=1))
         psum = ctx.enter_context(tc.psum_pool(name="psum", bufs=1))
 
-        places = {"cap0": 0, "w2_raw0": 8192, "th1": 8192, "front11": 8192, "tab_plane": 15360, "wgs_sb": 16384}
+        places = {"cap0": 0, "w2_raw0": 8192, "th1": 8192, "front11": 8192, "w1_raw": 8192,
+                  "page1": 16384, "w1_plane_raw": 24064, "page2": 24576}
+
 
         def held(name, shape, dtype, tag=None):
             if name in places:
@@ -98,18 +100,17 @@ def tile_list_spill_slot_advisor_kernel(
                 )
 
         nc.sync.dma_start(idx[:], offs)
+        scale_rows = tab_scales.rearrange("a (q r) c -> r q a c", r=4)
+        for r in range(4):
+            nc.sync.dma_start(tab_plane[r:P:16, :].bitcast(I32), scale_rows[r].bitcast(I32))
         nc.sync.dma_start(w1_raw[:], w1_words.rearrange("a p b -> p a b").bitcast(I32))
-        nc.sync.dma_start(idx2[:], offs2)
-        for q in range(4):
-            nc.sync.dma_start(
-                tab_plane[32 * q : 32 * q + 8, :].bitcast(I32), tab_scales[:, 4 * q : 4 * q + 4, :].bitcast(I32)
-            )
         nc.sync.dma_start(tab[0][:], tab_words[0].rearrange("p t i -> p (t i)").bitcast(I32))
-        nc.sync.dma_start(idx3[:], offs3)
         load_scale_rows(w1_plane_raw, w1_scales)
         nc.sync.dma_start(tab[1][:], tab_words[1].rearrange("p t i -> p (t i)").bitcast(I32))
         nc.sync.dma_start(b1_sb[:], b1.rearrange("(p t) -> p t", t=PACK))
         nc.sync.dma_start(gain_sb[:], gain.rearrange("(p t) -> p t", t=PACK))
+        nc.sync.dma_start(idx2[:], offs2)
+        nc.sync.dma_start(idx3[:], offs3)
 
         v_plane = [[], [shifted[0][:]] + [shifted[1][:, cols(j)] for j in range(PIECES - 1)]]
 
@@ -120,7 +121,7 @@ def tile_list_spill_slot_advisor_kernel(
             return picked
 
         def shift(picked, plane):
-            nc.sync.dma_start(plane[0:112, :].bitcast(I32), picked[4:116, :].bitcast(I32))
+            nc.sync.dma_start(plane[0:112, :].bitcast(I32), picked[16:P, :].bitcast(I32))
 
         v_codes = [[], []]
 
@@ -129,18 +130,17 @@ def tile_list_spill_slot_advisor_kernel(
             nc.vector.tensor_copy(codes[:], tab[a][:].bitcast(U32).indirect(idx[:, entries(first, last)]))
             v_codes[a].extend(codes[:, cols(j)] for j in range(last - first + 1))
 
+        shift(pick_scales(0, 0), shifted[0])
         w1_codes = held("w1_codes", [P, 2, M // 2], I32)
         nc.vector.tensor_copy(
             w1_codes[:].bitcast(U16).rearrange("p a (t m) -> p a m t", t=PACK),
             w1_raw[:].bitcast(U16).rearrange("p a (m t) -> p a m t", t=PACK),
         )
-        zeroed_page(nc.gpsimd, "w1_raw")
-        shift(pick_scales(0, 0), shifted[0])
-        picked_rest = pick_scales(1, PIECES - 1)
-        w2_raw = [held("w2_raw0", [P, PACK, 512], F32, tag="tab_plane")]
+        w2_raw = [held("w2_raw0", [P, PACK, 512], F32)]
         nc.sync.dma_start(w2_raw[0][:], w2_rows[:, :, 0:512])
+        picked_rest = pick_scales(1, PIECES - 1)
         wgs_rows = wgs.rearrange("(p t) s -> p t s", t=PACK)
-        wgs_sb = held("wgs_sb", [P, PACK, S], F32)
+        wgs_sb = held("wgs_sb", [P, PACK, S], F32, tag="tab_plane")
 
         def load_weights(slots, span):
             for q in (0, 2, 1, 3):
@@ -157,7 +157,8 @@ def tile_list_spill_slot_advisor_kernel(
                 w1_plane[:, a, :].rearrange("p (t m) -> p t m", t=PACK),
                 w1_plane_raw[:, a, :].rearrange("p (m t) -> p t m", t=PACK),
             )
-        zeroed_page(nc.gpsimd, "w1_plane_raw")
+        zeroed_page(nc.gpsimd)
+        zeroed_page(nc.gpsimd)
         pick_words(0, 0, 0)
         pick_words(1, 0, 0)
         pick_words(0, 1, 2)

@@ -73,12 +73,8 @@ def tile_list_spill_slot_advisor_kernel(
         tab_plane = held("tab_plane", [P, T], U8)
         w1_plane_raw = held("w1_plane_raw", [P, 2, M], U8)
         shifted = [held("shifted_first", [P, PIECE], U8), held("shifted_rest", [P, S - PIECE], U8)]
-        warm_in = held("warm_in", [P, 1], F32)
-        warm_out = held("warm_out", [P, 1], F32)
         nc.gpsimd.memset(tab_plane[:].bitcast(I32), 0)
         nc.gpsimd.memset(w1_plane_raw[:].rearrange("p a c -> p (a c)").bitcast(I32), 0)
-        nc.vector.memset(warm_in[:], 0.0)
-        nc.scalar.activation(warm_out[:], warm_in[:], ACT.Tanh)
         for plane in shifted:
             nc.vector.memset(plane[96:128, :].bitcast(I32), 0)
         zeroed_page(nc.gpsimd)

@@ -21,9 +21,22 @@ PACK = 4
 PIECE = 256
 PIECES = S // PIECE
 LIST_COLS = PIECE // 16
-
-
 HALF = 128
+
+PLACES = {
+    "wgs_sb": 0,
+    "tab_plane": 15360,
+    "gain_sb": 16384,
+    "w2_early": 17408,
+    "w1_raw": 17408,
+    "th1": 41984,
+    "front11": 41984,
+    "w2_front1": 45056,
+    "page3": 46080,
+    "cap0": 29696,
+    "w1_plane_raw": 54272,
+    "page2": 54272,
+}
 
 
 def tile_list_spill_slot_advisor_kernel(
@@ -33,31 +46,27 @@ def tile_list_spill_slot_advisor_kernel(
     with ExitStack() as ctx:
         lists = ctx.enter_context(tc.tile_pool(name="lists", bufs=1))
         sb = ctx.enter_context(tc.tile_pool(name="sb", bufs=1))
-        shared = ctx.enter_context(tc.tile_pool(name="shared", bufs=1))
+        placed = ctx.enter_context(tc.tile_pool(name="placed", bufs=1))
         psum = ctx.enter_context(tc.psum_pool(name="psum", bufs=1))
 
-        places = {"cap0": 0, "w2_raw0": 8192, "th1": 8192, "front11": 8192, "w1_raw": 8192,
-                  "page1": 16384, "w1_plane_raw": 24064, "page2": 24576}
-
-
-        def held(name, shape, dtype, tag=None):
-            if name in places:
-                return shared.tile(shape, dtype, name=name, align_bytes=64, offset=places[name])
-            return sb.tile(shape, dtype, name=name, tag=tag or name, align_bytes=64)
+        def tile(name, shape, dtype, after=None):
+            if name in PLACES:
+                return placed.tile(shape, dtype, name=name, align_bytes=64, offset=PLACES[name])
+            return sb.tile(shape, dtype, name=name, tag=after or name, align_bytes=64)
 
         def bank(n, shape):
             return psum.tile(shape, F32, name=f"bank{n}", tag=f"bank{n}")
 
-        def cols(j, last=None):
-            return slice(j * PIECE, ((j if last is None else last) + 1) * PIECE)
+        def cols(first, last=None):
+            return slice(first * PIECE, ((first if last is None else last) + 1) * PIECE)
 
-        def entries(j, last=None):
-            return slice(j * LIST_COLS, ((j if last is None else last) + 1) * LIST_COLS)
+        def entries(span):
+            return slice(span.start // 16, span.stop // 16)
 
-        def by_word(grouped):
+        def word_order(grouped):
             return grouped.rearrange("p (c i) t -> p c t i", i=4)
 
-        def by_row(rows):
+        def row_order(rows):
             return rows.rearrange("p t (c i) -> p c t i", i=4)
 
         def quantize(codes, plane, grouped):
@@ -65,28 +74,10 @@ def tile_list_spill_slot_advisor_kernel(
 
         pages = []
 
-        def zeroed_page(engine, tag=None):
-            page = held(f"page{len(pages)}", [P, T2], F32, tag=tag)
-            engine.memset(page[:], 0.0)
+        def new_page(after=None):
+            page = tile(f"page{len(pages)}", [P, T2], F32, after)
+            nc.gpsimd.memset(page[:], 0.0)
             pages.append(page)
-
-        tab_plane = held("tab_plane", [P, T], U8)
-        w1_plane_raw = held("w1_plane_raw", [P, 2, M], U8)
-        shifted = [held("shifted_first", [P, PIECE], U8), held("shifted_rest", [P, S - PIECE], U8)]
-        nc.gpsimd.memset(tab_plane[:].bitcast(I32), 0)
-        nc.gpsimd.memset(w1_plane_raw[:].rearrange("p a c -> p (a c)").bitcast(I32), 0)
-        for plane in shifted:
-            nc.vector.memset(plane[96:128, :].bitcast(I32), 0)
-        zeroed_page(nc.gpsimd)
-
-        idx = lists.tile([P, S // 16], U16, name="idx")
-        idx2 = lists.tile([P, S // 16], U16, name="idx2")
-        idx3 = lists.tile([P, PICKS // 16], U16, name="idx3")
-        b1_sb = held("b1_sb", [P, PACK], F32)
-        gain_sb = held("gain_sb", [P, PACK], F32)
-        tab = [held(f"tab{a}", [P, T], I32) for a in range(2)]
-        w1_raw = held("w1_raw", [P, 2, M // 2], I32)
-        w2_rows = w2.rearrange("(p j) r -> p j r", j=PACK)
 
         def load_scale_rows(plane, scales):
             for q in range(4):
@@ -94,6 +85,24 @@ def tile_list_spill_slot_advisor_kernel(
                     plane[32 * q : 32 * q + 4, :, :].bitcast(I32),
                     scales[:, 4 * q : 4 * q + 4, :].rearrange("a r c -> r a c").bitcast(I32),
                 )
+
+        tab_plane = tile("tab_plane", [P, T], U8)
+        w1_plane_raw = tile("w1_plane_raw", [P, 2, M], U8)
+        shifted = [tile("shifted_first", [P, PIECE], U8), tile("shifted_rest", [P, S - PIECE], U8)]
+        nc.gpsimd.memset(tab_plane[:].bitcast(I32), 0)
+        nc.gpsimd.memset(w1_plane_raw[:].rearrange("p a c -> p (a c)").bitcast(I32), 0)
+        for plane in shifted:
+            nc.vector.memset(plane[96:128, :].bitcast(I32), 0)
+        new_page()
+        new_page()
+
+        idx = lists.tile([P, S // 16], U16, name="idx")
+        idx2 = lists.tile([P, S // 16], U16, name="idx2")
+        idx3 = lists.tile([P, PICKS // 16], U16, name="idx3")
+        b1_sb = tile("b1_sb", [P, PACK], F32)
+        tab = [tile(f"tab{a}", [P, T], I32) for a in range(2)]
+        w1_raw = tile("w1_raw", [P, 2, M // 2], I32)
+        w2_rows = w2.rearrange("(p j) r -> p j r", j=PACK)
 
         nc.sync.dma_start(idx[:], offs)
         scale_rows = tab_scales.rearrange("a (q r) c -> r q a c", r=4)
@@ -104,102 +113,101 @@ def tile_list_spill_slot_advisor_kernel(
         load_scale_rows(w1_plane_raw, w1_scales)
         nc.sync.dma_start(tab[1][:], tab_words[1].rearrange("p t i -> p (t i)").bitcast(I32))
         nc.sync.dma_start(b1_sb[:], b1.rearrange("(p t) -> p t", t=PACK))
-        nc.sync.dma_start(gain_sb[:], gain.rearrange("(p t) -> p t", t=PACK))
         nc.sync.dma_start(idx2[:], offs2)
         nc.sync.dma_start(idx3[:], offs3)
 
-        v_plane = [[], [shifted[0][:]] + [shifted[1][:, cols(j)] for j in range(PIECES - 1)]]
-
-        def pick_scales(first, last):
-            picked = held(f"picked{first}", [P, (last - first + 1) * PIECE], U8)
-            nc.vector.tensor_copy(picked[:], tab_plane[:].indirect(idx[:, entries(first, last)]))
-            v_plane[0].extend(picked[:, cols(j)] for j in range(last - first + 1))
+        def pick_scales(name, span):
+            picked = tile(name, [P, span.stop - span.start], U8)
+            nc.vector.tensor_copy(picked[:], tab_plane[:].indirect(idx[:, entries(span)]))
             return picked
 
         def shift(picked, plane):
             nc.sync.dma_start(plane[0:112, :].bitcast(I32), picked[16:P, :].bitcast(I32))
 
-        v_codes = [[], []]
+        def pick_words(a, span, after=None):
+            codes = tile(f"v{a}_{span.start}", [P, span.stop - span.start], U32, after)
+            nc.vector.tensor_copy(codes[:], tab[a][:].bitcast(U32).indirect(idx[:, entries(span)]))
+            return [codes[:, cols(j)] for j in range((span.stop - span.start) // PIECE)]
 
-        def pick_words(a, first, last, tag=None):
-            codes = held(f"v{a}_{first}", [P, (last - first + 1) * PIECE], U32, tag=tag)
-            nc.vector.tensor_copy(codes[:], tab[a][:].bitcast(U32).indirect(idx[:, entries(first, last)]))
-            v_codes[a].extend(codes[:, cols(j)] for j in range(last - first + 1))
-
-        shift(pick_scales(0, 0), shifted[0])
-        w1_codes = held("w1_codes", [P, 2, M // 2], I32)
-        nc.vector.tensor_copy(
-            w1_codes[:].bitcast(U16).rearrange("p a (t m) -> p a m t", t=PACK),
-            w1_raw[:].bitcast(U16).rearrange("p a (m t) -> p a m t", t=PACK),
-        )
-        w2_raw = [held("w2_raw0", [P, PACK, 512], F32)]
-        nc.sync.dma_start(w2_raw[0][:], w2_rows[:, :, 0:512])
-        picked_rest = pick_scales(1, PIECES - 1)
+        picked_first = pick_scales("picked_first", cols(0))
+        shift(picked_first, shifted[0])
+        picked_rest = pick_scales("picked_rest", cols(1, PIECES - 1))
+        v_plane = [
+            [picked_first[:]] + [picked_rest[:, cols(j)] for j in range(PIECES - 1)],
+            [shifted[0][:]] + [shifted[1][:, cols(j)] for j in range(PIECES - 1)],
+        ]
+        w2_early = tile("w2_early", [P, PACK, 512], F32)
+        nc.sync.dma_start(w2_early[:, :, cols(0)], w2_rows[:, :, cols(0)])
+        shift(picked_rest, shifted[1])
+        nc.sync.dma_start(w2_early[:, :, cols(1)], w2_rows[:, :, cols(1)])
+        gain_sb = tile("gain_sb", [P, PACK], F32)
+        nc.sync.dma_start(gain_sb[:], gain.rearrange("(p t) -> p t", t=PACK))
         wgs_rows = wgs.rearrange("(p t) s -> p t s", t=PACK)
-        wgs_sb = held("wgs_sb", [P, PACK, S], F32, tag="tab_plane")
+        wgs_sb = tile("wgs_sb", [P, PACK, S], F32, "tab_plane")
 
         def load_weights(slots, span):
             for q in (0, 2, 1, 3):
                 nc.sync.dma_start(wgs_sb[32 * q : 32 * q + 32, slots, span], wgs_rows[:, slots, span])
 
-        shift(picked_rest, shifted[1])
         load_weights(slice(0, 2), cols(0))
         load_weights(slice(2, PACK), cols(0))
         load_weights(slice(0, PACK), cols(1))
         load_weights(slice(0, PACK), cols(2, PIECES - 1))
-        w1_plane = held("w1_plane", [P, 2, M], U8)
+
+        w1_codes = tile("w1_codes", [P, 2, M // 2], I32)
+        nc.scalar.copy(
+            w1_codes[:].bitcast(U16).rearrange("p a (t m) -> p a m t", t=PACK),
+            w1_raw[:].bitcast(U16).rearrange("p a (m t) -> p a m t", t=PACK),
+        )
+        w1_plane = tile("w1_plane", [P, 2, M], U8)
         for a in range(2):
             nc.gpsimd.tensor_copy(
                 w1_plane[:, a, :].rearrange("p (t m) -> p t m", t=PACK),
                 w1_plane_raw[:, a, :].rearrange("p (m t) -> p t m", t=PACK),
             )
-        zeroed_page(nc.gpsimd)
-        zeroed_page(nc.gpsimd)
-        pick_words(0, 0, 0)
-        pick_words(1, 0, 0)
-        pick_words(0, 1, 2)
-        pick_words(1, 1, PIECES - 1)
+        new_page()
+        v_codes = [pick_words(a, cols(0)) for a in range(2)]
+        v_codes[0].extend(pick_words(0, cols(1, PIECES - 1)))
+        v_codes[1].extend(pick_words(1, cols(1, PIECES - 1)))
 
-
-        def first_product(dst, j, slots, halves):
-            steps = [(a, u, n) for a in range(2) for u in range(len(slots)) for n in range(len(halves))]
-            for a, u, n in steps:
-                t, c0 = slots[u], halves[n] * HALF
-                nc.tensor.matmul_mx(
-                    out=dst[:, u, HALF * n : HALF * n + HALF],
-                    lhsT=w1_codes[:, a, 64 * t : 64 * t + 64].bitcast(FP4X4),
-                    lhsT_scale=w1_plane[:, a, 128 * t : 128 * t + 128],
-                    rhs=v_codes[a][j][:, c0 : c0 + HALF].bitcast(FP8X4),
-                    rhs_scale=v_plane[a][j][:, c0 : c0 + HALF],
-                    start=((a, u, n) == steps[0]),
-                    stop=((a, u, n) == steps[-1]),
-                )
-
-        def round_w2(copy, a, grouped, t0):
-            copy(
-                grouped.rearrange("p t m j -> p m j t"),
-                w2_raw[a][:].rearrange("p j (m t) -> p m j t", t=PACK)[:, :, :, t0 : t0 + 2],
+        def first_pass(dst, a, j, t, span, start, stop):
+            nc.tensor.matmul_mx(
+                out=dst,
+                lhsT=w1_codes[:, a, 64 * t : 64 * t + 64].bitcast(FP4X4),
+                lhsT_scale=w1_plane[:, a, 128 * t : 128 * t + 128],
+                rhs=v_codes[a][j][:, span].bitcast(FP8X4),
+                rhs_scale=v_plane[a][j][:, span],
+                start=start,
+                stop=stop,
             )
 
-        e_codes = [held("e_codes0", [P, PIECE], U32)]
-        e_plane = held("e_plane", [P, S], U8)
-        w2_codes = [held("w2_codes0", [P, 256], U32)]
-        w2_plane = [held(f"w2_plane{a}", [P, 512], U8) for a in range(2)]
-        th0 = []
+        def round_w2(raw, grouped, t0):
+            nc.scalar.copy(
+                grouped.rearrange("p t m j -> p m j t"),
+                raw.rearrange("p j (m t) -> p m j t", t=PACK)[:, :, :, t0 : t0 + 2],
+            )
+
+        e_codes = [tile("e_codes0", [P, PIECE], U32)]
+        e_plane = tile("e_plane", [P, S], U8)
+        w2_codes = [tile("w2_codes0", [P, 256], U32)]
+        w2_plane = [tile(f"w2_plane{a}", [P, 512], U8) for a in range(2)]
+        halves = [slice(0, HALF), slice(HALF, PIECE)]
+        sums = [(half, t, bank(PACK * half + t, [P, HALF])) for half in range(2) for t in range(PACK)]
+        for half, t, pre in sums:
+            first_pass(pre[:], 0, 0, t, halves[half], True, False)
+        th0 = [tile(f"th0{half}", [P, PACK, HALF], F32) for half in range(2)]
+        for half, t, pre in sums:
+            first_pass(pre[:], 1, 0, t, halves[half], False, True)
+            nc.scalar.activation(th0[half][:, t, :], pre[:], ACT.Tanh, bias=b1_sb[:, t : t + 1])
+        w2_front = [tile(f"w2_front{u}", [P, 2, 128, PACK], BF16) for u in range(2)]
         for half in range(2):
-            th0.append(held(f"th0{half}", [P, PACK, HALF], F32))
-            for t in range(PACK):
-                pre = bank(PACK * half + t, [P, 1, HALF])
-                first_product(pre, 0, (t,), (half,))
-                nc.scalar.activation(th0[half][:, t, :], pre[:, 0, :], ACT.Tanh, bias=b1_sb[:, t : t + 1])
-        w2_front = [held(f"w2_front{u}", [P, 2, 128, PACK], BF16) for u in range(2)]
-        round_w2(nc.scalar.copy, 0, w2_front[0][:], 0)
-        round_w2(nc.scalar.copy, 0, w2_front[1][:], 2)
-        e_first = [held(f"e_first{half}", [P, HALF, PACK], BF16) for half in range(2)]
+            round_w2(w2_early[:, :, cols(half)], w2_front[0][:, :, 64 * half : 64 * half + 64, :], 0)
+        round_w2(w2_early[:], w2_front[1][:], 2)
+        e_first = [tile(f"e_first{half}", [P, HALF, PACK], BF16) for half in range(2)]
         for half in range(2):
             nc.vector.tensor_tensor(
-                by_word(e_first[half][:]),
-                by_row(th0[half][:]),
+                word_order(e_first[half][:]),
+                row_order(th0[half][:]),
                 gain_sb[:].unsqueeze(1).unsqueeze(3).to_broadcast([P, HALF // 4, PACK, 4]),
                 ALU.mult,
             )
@@ -207,34 +215,29 @@ def tile_list_spill_slot_advisor_kernel(
             span = slice(HALF * half, HALF * half + HALF)
             quantize(e_codes[0][:, span], e_plane[:, span], e_first[half][:].rearrange("p n t -> p (n t)"))
         quantize(w2_codes[0][:], w2_plane[0][:, 0:256], w2_front[0][:].rearrange("p t m j -> p (t m j)"))
-        pick_words(0, 3, 3, tag="w2_front0")
 
         def front_bank(j):
             return 0 if j % 2 else 4
 
-        def grouped_tag(j):
-            return f"e_grouped{j}"
-
         def squash(j):
-            th = held(f"th{j}", [P, PACK, PIECE], F32, tag=grouped_tag(j - 1) if j > 1 else "tab_plane")
+            th = tile(f"th{j}", [P, PACK, PIECE], F32, f"e_grouped{j - 1}")
             for pair in range(2):
-                pre = bank(2 + pair if j == 1 else front_bank(j - 2) + pair, [P, 2, PIECE])
-                first_product(pre, j, (2 * pair, 2 * pair + 1), (0, 1))
+                pre = bank(2 + 2 * pair if j == 1 else front_bank(j) + pair, [P, 2, PIECE])
+                for a in range(2):
+                    for u in range(2):
+                        first_pass(pre[:, u, :], a, j, 2 * pair + u, cols(0), (a, u) == (0, 0), (a, u) == (1, 1))
                 for u in range(2):
                     t = 2 * pair + u
                     nc.scalar.activation(th[:, t, :], pre[:, u, :], ACT.Tanh, bias=b1_sb[:, t : t + 1])
             return th
 
-        def rows_tag(j):
-            return f"e_rows{j}"
-
         def features(j, th):
-            e_rows = held(f"e_rows{j}", [P, PACK, PIECE], BF16)
+            e_rows = tile(f"e_rows{j}", [P, PACK, PIECE], BF16)
             for t in range(PACK):
                 nc.scalar.activation(e_rows[:, t, :], th[:, t, :], ACT.Copy, scale=gain_sb[:, t : t + 1])
-            e_grouped = held(f"e_grouped{j}", [P, PIECE, PACK], BF16)
-            nc.scalar.copy(by_word(e_grouped[:]), by_row(e_rows[:]))
-            e_codes.append(held(f"e_codes{j}", [P, PIECE], U32, tag=f"front{j - 1}0"))
+            e_grouped = tile(f"e_grouped{j}", [P, PIECE, PACK], BF16)
+            nc.scalar.copy(word_order(e_grouped[:]), row_order(e_rows[:]))
+            e_codes.append(tile(f"e_codes{j}", [P, PIECE], U32, f"front{j - 1}0"))
             quantize(e_codes[j][:], e_plane[:, cols(j)], e_grouped[:].rearrange("p n t -> p (n t)"))
 
         def w2_slot(a, t):
@@ -242,10 +245,7 @@ def tile_list_spill_slot_advisor_kernel(
                 return w2_codes[t // 2][:, 128 * (t % 2) : 128 * (t % 2) + 128]
             return w2_codes[2][:, 128 * t : 128 * t + 128]
 
-        def front_tag(j, t):
-            return {(0, 1): "tab1", (1, 1): "tab_plane"}.get((j, t))
-
-        def costs(a, parts, n, dst, copy=nc.scalar.copy):
+        def costs(a, parts, n, dst):
             acc = bank(n, [P, len(parts) * PIECE])
             for u, (t, j) in enumerate(parts):
                 nc.tensor.matmul_mx(
@@ -257,82 +257,81 @@ def tile_list_spill_slot_advisor_kernel(
                     start=True,
                     stop=True,
                 )
-            copy(dst, acc[:])
+            nc.scalar.copy(dst, acc[:])
 
-        def put(t, first, last, values):
-            weights = wgs_sb[:, t, cols(first, last)]
-            nc.vector.tensor_tensor(pages[t][:].indirect(idx2[:, entries(first, last)]), values, weights, ALU.mult)
+        def put(t, span, values):
+            nc.vector.tensor_tensor(pages[t][:].indirect(idx2[:, entries(span)]), values, wgs_sb[:, t, span], ALU.mult)
 
         cap_rows = cap.rearrange("(a p t) m -> a p t m", a=2, t=PACK)
         for j in range(PIECES):
             ahead = 3 if j == 0 else 2
             for t in range(ahead):
-                front = held(f"front{j}{t}", [P, PIECE], F32, tag=front_tag(j, t))
+                front = tile(f"front{j}{t}", [P, PIECE], F32, "tab0" if (j, t) == (0, 1) else None)
                 very_first = (j, t) == (0, 0)
-                costs(0, [(t, j)], front_bank(j) + t, front[:], nc.vector.tensor_copy if very_first else nc.scalar.copy)
+                costs(0, [(t, j)], front_bank(j) + t, front[:])
                 if very_first:
-                    w2_codes.append(held("w2_codes1", [P, 256], U32, tag="tab0"))
+                    w2_codes.append(tile("w2_codes1", [P, 256], U32, "tab1"))
                     quantize(w2_codes[1][:], w2_plane[0][:, 256:512], w2_front[1][:].rearrange("p t m j -> p (t m j)"))
-                    zeroed_page(nc.gpsimd, "w2_front1")
-                put(t, j, j, front[:])
+                    new_page()
+                put(t, cols(j), front[:])
                 if (j, t) == (0, 1):
-                    w2_raw.append(held("w2_raw1", [P, PACK, 512], F32, tag="tab1"))
-                    nc.sync.dma_start(w2_raw[1][:], w2_rows[:, :, 512:1024])
+                    w2_late = tile("w2_late", [P, PACK, 512], F32, "tab0")
+                    nc.sync.dma_start(w2_late[:], w2_rows[:, :, 512:1024])
             if j + 1 < PIECES:
                 features(j + 1, squash(j + 1))
-            back = held(f"back{j}", [P, (PACK - ahead) * PIECE], F32, tag=rows_tag(j + 1))
+            back = tile(f"back{j}", [P, (PACK - ahead) * PIECE], F32, f"e_rows{j + 1}")
             costs(0, [(t, j) for t in range(ahead, PACK)], 7 - j % 2, back[:])
             if ahead == 2:
-                put(2, j, j, back[:, cols(0)])
+                put(2, cols(j), back[:, cols(0)])
             if j == PIECES - 1:
-                back_tags = ("e_grouped3", rows_tag(3))
-                w2_back = [held(f"w2_back{u}", [P, 2, 128, PACK], BF16, tag=back_tags[u]) for u in range(2)]
+                back_tags = ("e_grouped3", "e_rows3")
+                w2_back = [tile(f"w2_back{u}", [P, 2, 128, PACK], BF16, back_tags[u]) for u in range(2)]
                 for u in range(2):
-                    round_w2(nc.scalar.copy, 1, w2_back[u][:], 2 * u)
-                cap1 = held("cap1", [P, PACK, PICKS], F32, tag="tab1")
+                    round_w2(w2_late[:], w2_back[u][:], 2 * u)
+                cap1 = tile("cap1", [P, PACK, PICKS], F32, "tab0")
                 nc.sync.dma_start(cap1[:], cap_rows[1])
-                w2_codes.append(held("w2_codes2", [P, 512], U32, tag="front31"))
+                w2_codes.append(tile("w2_codes2", [P, 512], U32, "front31"))
                 quantize(w2_codes[2][:, 0:256], w2_plane[1][:, 0:256], w2_back[0][:].rearrange("p t m j -> p (t m j)"))
-            put(3, j, j, back[:, cols(PACK - 1 - ahead)])
+            put(3, cols(j), back[:, cols(PACK - 1 - ahead)])
             if j == PIECES - 1:
                 quantize(w2_codes[2][:, 256:512], w2_plane[1][:, 256:512], w2_back[1][:].rearrange("p t m j -> p (t m j)"))
             if j == 1:
-                cap0 = held("cap0", [P, PACK, PICKS], F32, tag="tab_plane")
+                cap0 = tile("cap0", [P, PACK, PICKS], F32)
                 nc.sync.dma_start(cap0[:], cap_rows[0])
             if j == PIECES - 2:
-                w3_plane = held("w3_plane", [P, 2, N], U8, tag=rows_tag(2))
+                w3_plane = tile("w3_plane", [P, 2, N], U8, "e_rows2")
                 nc.gpsimd.memset(w3_plane[:].rearrange("p a c -> p (a c)").bitcast(I32), 0)
                 load_scale_rows(w3_plane, w3_scales)
-                w3_codes = held("w3_codes", [P, 2, N], I32, tag="shifted_rest")
+                w3_codes = tile("w3_codes", [P, 2, N], I32, "shifted_rest")
                 nc.sync.dma_start(w3_codes[:], w3_words.rearrange("a p c i -> p a (c i)").bitcast(I32))
 
-        def whole_costs(t, tag=None):
-            h = held(f"h1{t}", [P, S], F32, tag=tag)
+        def whole_costs(t, after=None):
+            h = tile(f"h1{t}", [P, S], F32, after)
             for half in range(2):
                 costs(1, [(t, 2 * half), (t, 2 * half + 1)], 2 * t + half, h[:, cols(2 * half, 2 * half + 1)])
             return h
 
         h1 = [whole_costs(0)]
+        whole = cols(0, PIECES - 1)
 
-        x0_tags = back_tags
-        x0 = [held(f"x0_{u}", [P, 2, PICKS], F32, tag=x0_tags[u]) for u in range(2)]
-        z0_rows = held("z0_rows", [P, PACK, PICKS], BF16, tag="tab0")
-        z0 = held("z0", [P, PICKS, PACK], BF16)
-        z_codes = [held(f"z_codes{a}", [P, PICKS], U32) for a in range(2)]
-        z_plane = [held(f"z_plane{a}", [P, PICKS], U8) for a in range(2)]
+        x0 = [tile(f"x0_{u}", [P, 2, PICKS], F32, back_tags[u]) for u in range(2)]
+        z0_rows = tile("z0_rows", [P, PACK, PICKS], BF16, "tab1")
+        z0 = tile("z0", [P, PICKS, PACK], BF16)
+        z_codes = [tile(f"z_codes{a}", [P, PICKS], U32) for a in range(2)]
+        z_plane = [tile(f"z_plane{a}", [P, PICKS], U8) for a in range(2)]
         for t in range(PACK):
             nc.vector.tensor_copy(x0[t // 2][:, t % 2, :], pages[t][:].indirect(idx3[:]))
-        put(0, 0, PIECES - 1, h1[0][:])
+        put(0, whole, h1[0][:])
         for u in range(2):
             slots = slice(2 * u, 2 * u + 2)
             nc.vector.tensor_tensor(z0_rows[:, slots, :], x0[u][:], cap0[:, slots, :], ALU.min)
-            h1.append(whole_costs(1 + u, x0_tags[u]))
-        nc.scalar.copy(by_word(z0[:]), by_row(z0_rows[:]))
-        h1.append(whole_costs(3, "tab0"))
+            h1.append(whole_costs(1 + u, back_tags[u]))
+        nc.scalar.copy(word_order(z0[:]), row_order(z0_rows[:]))
+        h1.append(whole_costs(3, "tab1"))
         for t in range(1, PACK):
             if t == PACK - 1:
                 quantize(z_codes[0][:], z_plane[0][:], z0[:].rearrange("p n t -> p (n t)"))
-            put(t, 0, PIECES - 1, h1[t][:])
+            put(t, whole, h1[t][:])
 
         out_rows = out.rearrange("(c p) m -> p c m", p=P)
         last = PIECES - 1
@@ -364,37 +363,37 @@ def tile_list_spill_slot_advisor_kernel(
         def store(n):
             span = spans[n]
             for pair in range(2):
-                staged = held(f"staged{n}{pair}", [P, 2, span.stop - span.start], F32)
+                staged = tile(f"staged{n}{pair}", [P, 2, span.stop - span.start], F32)
                 copy = nc.vector.tensor_copy if (n >= last and pair == 0) else nc.scalar.copy
                 copy(staged[:], opened[n][pair][:])
                 nc.sync.dma_start(out_rows[:, 2 * pair : 2 * pair + 2, span], staged[:])
 
         opened = [open_scores(n) for n in range(PIECES)]
 
-        def fetch(j, slots, tag):
-            picked = held(f"x1_{j}{slots[0]}", [P, len(slots), PIECE], F32, tag=tag)
+        def fetch(j, slots, after):
+            picked = tile(f"x1_{j}{slots[0]}", [P, len(slots), PIECE], F32, after)
             for u, t in enumerate(slots):
-                nc.vector.tensor_copy(picked[:, u, :], pages[t][:].indirect(idx3[:, entries(j)]))
+                nc.vector.tensor_copy(picked[:, u, :], pages[t][:].indirect(idx3[:, entries(cols(j))]))
             return picked
 
         def fetch_pairs(j):
-            return [fetch(j, (0, 1), "z0"), fetch(j, (2, 3), "tab0")]
+            return [fetch(j, (0, 1), "z0"), fetch(j, (2, 3), "tab1")]
 
         def limit(j, pairs):
-            rows = held(f"z1_rows{j}", [P, PACK, PIECE], BF16, tag="z1_rows")
+            rows = tile(f"z1_rows{j}", [P, PACK, PIECE], BF16, "z1_rows")
             for u in range(2):
                 slots = slice(2 * u, 2 * u + 2)
                 nc.vector.tensor_tensor(rows[:, slots, :], pairs[u][:], cap1[:, slots, cols(j)], ALU.min)
-            grouped = held(f"z1_{j}", [P, PIECE, PACK], BF16, tag=f"th{j + 1}" if j == 0 else f"e_grouped{j}")
-            nc.scalar.copy(by_word(grouped[:]), by_row(rows[:]))
+            grouped = tile(f"z1_{j}", [P, PIECE, PACK], BF16, f"e_grouped{j}")
+            nc.scalar.copy(word_order(grouped[:]), row_order(rows[:]))
             return grouped
 
-        def limit_last(picked, half, tag):
-            grouped = held(f"z1_last{half}", [P, HALF, PACK], BF16, tag=tag)
+        def limit_last(picked, half, after):
+            grouped = tile(f"z1_last{half}", [P, HALF, PACK], BF16, after)
             nc.vector.tensor_tensor(
-                by_word(grouped[:]),
-                by_row(picked[:, :, HALF * half : HALF * half + HALF]),
-                by_row(cap1[:, :, spans[last + half]]),
+                word_order(grouped[:]),
+                row_order(picked[:, :, HALF * half : HALF * half + HALF]),
+                row_order(cap1[:, :, spans[last + half]]),
                 ALU.min,
             )
             return grouped
@@ -407,8 +406,8 @@ def tile_list_spill_slot_advisor_kernel(
             store(n)
             if n == 0:
                 opened.append(open_scores(PIECES))
-        halves = [limit_last(picked, 0, "z1_rows"), limit_last(picked, 1, None)]
+        ends = [limit_last(picked, 0, "z1_rows"), limit_last(picked, 1, None)]
         for half in range(2):
-            finish(last + half, halves[half][:])
+            finish(last + half, ends[half][:])
         for half in range(2):
             store(last + half)

@@ -137,9 +137,8 @@ def tile_list_spill_slot_advisor_kernel(
             [shifted[0][:]] + [shifted[1][:, cols(j)] for j in range(PIECES - 1)],
         ]
         w2_early = tile("w2_early", [P, PACK, 512], F32)
-        nc.sync.dma_start(w2_early[:, :, cols(0)], w2_rows[:, :, cols(0)])
+        nc.sync.dma_start(w2_early[:], w2_rows[:, :, 0:512])
         shift(picked_rest, shifted[1])
-        nc.sync.dma_start(w2_early[:, :, cols(1)], w2_rows[:, :, cols(1)])
         gain_sb = tile("gain_sb", [P, PACK], F32)
         nc.sync.dma_start(gain_sb[:], gain.rearrange("(p t) -> p t", t=PACK))
         wgs_rows = wgs.rearrange("(p t) s -> p t s", t=PACK)
@@ -156,8 +155,8 @@ def tile_list_spill_slot_advisor_kernel(
 
         w1_codes = tile("w1_codes", [P, 2, M // 2], I32)
         nc.scalar.copy(
-            w1_codes[:].bitcast(U16).rearrange("p a (t m) -> p a m t", t=PACK),
-            w1_raw[:].bitcast(U16).rearrange("p a (m t) -> p a m t", t=PACK),
+            w1_codes[:].bitcast(U16).rearrange("p a (t m) -> p a t m", t=PACK),
+            w1_raw[:].bitcast(U16).rearrange("p a (m t) -> p a t m", t=PACK),
         )
         w1_plane = tile("w1_plane", [P, 2, M], U8)
         for a in range(2):
@@ -200,9 +199,8 @@ def tile_list_spill_slot_advisor_kernel(
             first_pass(pre[:], 1, 0, t, halves[half], False, True)
             nc.scalar.activation(th0[half][:, t, :], pre[:], ACT.Tanh, bias=b1_sb[:, t : t + 1])
         w2_front = [tile(f"w2_front{u}", [P, 2, 128, PACK], BF16) for u in range(2)]
-        for half in range(2):
-            round_w2(w2_early[:, :, cols(half)], w2_front[0][:, :, 64 * half : 64 * half + 64, :], 0)
-        round_w2(w2_early[:], w2_front[1][:], 2)
+        for u in range(2):
+            round_w2(w2_early[:], w2_front[u][:], 2 * u)
         e_first = [tile(f"e_first{half}", [P, HALF, PACK], BF16) for half in range(2)]
         for half in range(2):
             nc.vector.tensor_tensor(

@@ -26,7 +26,6 @@ HALF = 128
 PLACES = {
     "wgs_sb": 0,
     "tab_plane": 15360,
-    "gain_sb": 16384,
     "w2_early": 17408,
     "w1_raw": 17408,
     "th1": 41984,
@@ -34,8 +33,9 @@ PLACES = {
     "w2_front1": 45056,
     "page3": 46080,
     "cap0": 29696,
-    "w1_plane_raw": 54272,
-    "page2": 54272,
+    "page1": 54272,
+    "w1_plane_raw": 61952,
+    "page2": 62464,
 }
 
 
@@ -94,12 +94,12 @@ def tile_list_spill_slot_advisor_kernel(
         for plane in shifted:
             nc.vector.memset(plane[96:128, :].bitcast(I32), 0)
         new_page()
-        new_page()
 
         idx = lists.tile([P, S // 16], U16, name="idx")
         idx2 = lists.tile([P, S // 16], U16, name="idx2")
         idx3 = lists.tile([P, PICKS // 16], U16, name="idx3")
         b1_sb = tile("b1_sb", [P, PACK], F32)
+        gain_sb = tile("gain_sb", [P, PACK], F32)
         tab = [tile(f"tab{a}", [P, T], I32) for a in range(2)]
         w1_raw = tile("w1_raw", [P, 2, M // 2], I32)
         w2_rows = w2.rearrange("(p j) r -> p j r", j=PACK)
@@ -113,6 +113,7 @@ def tile_list_spill_slot_advisor_kernel(
         load_scale_rows(w1_plane_raw, w1_scales)
         nc.sync.dma_start(tab[1][:], tab_words[1].rearrange("p t i -> p (t i)").bitcast(I32))
         nc.sync.dma_start(b1_sb[:], b1.rearrange("(p t) -> p t", t=PACK))
+        nc.sync.dma_start(gain_sb[:], gain.rearrange("(p t) -> p t", t=PACK))
         nc.sync.dma_start(idx2[:], offs2)
         nc.sync.dma_start(idx3[:], offs3)
 
@@ -139,8 +140,6 @@ def tile_list_spill_slot_advisor_kernel(
         w2_early = tile("w2_early", [P, PACK, 512], F32)
         nc.sync.dma_start(w2_early[:], w2_rows[:, :, 0:512])
         shift(picked_rest, shifted[1])
-        gain_sb = tile("gain_sb", [P, PACK], F32)
-        nc.sync.dma_start(gain_sb[:], gain.rearrange("(p t) -> p t", t=PACK))
         wgs_rows = wgs.rearrange("(p t) s -> p t s", t=PACK)
         wgs_sb = tile("wgs_sb", [P, PACK, S], F32, "tab_plane")
 
@@ -164,6 +163,7 @@ def tile_list_spill_slot_advisor_kernel(
                 w1_plane[:, a, :].rearrange("p (t m) -> p t m", t=PACK),
                 w1_plane_raw[:, a, :].rearrange("p (m t) -> p t m", t=PACK),
             )
+        new_page()
         new_page()
         v_codes = [pick_words(a, cols(0)) for a in range(2)]
         v_codes[0].extend(pick_words(0, cols(1, PIECES - 1)))

@@ -33,9 +33,8 @@ PLACES = {
     "w2_front1": 45056,
     "page3": 46080,
     "cap0": 29696,
-    "page1": 54272,
-    "w1_plane_raw": 61952,
-    "page2": 62464,
+    "w1_plane_raw": 54272,
+    "page2": 54272,
 }
 
 
@@ -92,7 +91,8 @@ def tile_list_spill_slot_advisor_kernel(
         nc.gpsimd.memset(tab_plane[:].bitcast(I32), 0)
         nc.gpsimd.memset(w1_plane_raw[:].rearrange("p a c -> p (a c)").bitcast(I32), 0)
         for plane in shifted:
-            nc.vector.memset(plane[96:128, :].bitcast(I32), 0)
+            nc.gpsimd.memset(plane[96:128, :].bitcast(I32), 0)
+        new_page()
         new_page()
 
         idx = lists.tile([P, S // 16], U16, name="idx")
@@ -163,7 +163,6 @@ def tile_list_spill_slot_advisor_kernel(
                 w1_plane[:, a, :].rearrange("p (t m) -> p t m", t=PACK),
                 w1_plane_raw[:, a, :].rearrange("p (m t) -> p t m", t=PACK),
             )
-        new_page()
         new_page()
         v_codes = [pick_words(a, cols(0)) for a in range(2)]
         v_codes[0].extend(pick_words(0, cols(1, PIECES - 1)))

@@ -32,7 +32,9 @@ PLACES = {
     "front11": 41984,
     "w2_front1": 45056,
     "page3": 46080,
-    "cap0": 29696,
+    "cap0": 62464,
+    "back3": 77824,
+    "cap1": 78848,
     "w1_plane_raw": 54272,
     "page2": 54272,
 }
@@ -285,22 +287,22 @@ def tile_list_spill_slot_advisor_kernel(
                 w2_back = [tile(f"w2_back{u}", [P, 2, 128, PACK], BF16, back_tags[u]) for u in range(2)]
                 for u in range(2):
                     round_w2(w2_late[:], w2_back[u][:], 2 * u)
-                cap1 = tile("cap1", [P, PACK, PICKS], F32, "tab0")
-                nc.sync.dma_start(cap1[:], cap_rows[1])
                 w2_codes.append(tile("w2_codes2", [P, 512], U32, "front31"))
                 quantize(w2_codes[2][:, 0:256], w2_plane[1][:, 0:256], w2_back[0][:].rearrange("p t m j -> p (t m j)"))
             put(3, cols(j), back[:, cols(PACK - 1 - ahead)])
             if j == PIECES - 1:
                 quantize(w2_codes[2][:, 256:512], w2_plane[1][:, 256:512], w2_back[1][:].rearrange("p t m j -> p (t m j)"))
-            if j == 1:
-                cap0 = tile("cap0", [P, PACK, PICKS], F32)
-                nc.sync.dma_start(cap0[:], cap_rows[0])
             if j == PIECES - 2:
                 w3_plane = tile("w3_plane", [P, 2, N], U8, "e_rows2")
                 nc.gpsimd.memset(w3_plane[:].rearrange("p a c -> p (a c)").bitcast(I32), 0)
                 load_scale_rows(w3_plane, w3_scales)
                 w3_codes = tile("w3_codes", [P, 2, N], I32, "shifted_rest")
                 nc.sync.dma_start(w3_codes[:], w3_words.rearrange("a p c i -> p a (c i)").bitcast(I32))
+
+        cap0 = tile("cap0", [P, PACK, PICKS], F32)
+        nc.sync.dma_start(cap0[:], cap_rows[0])
+        cap1 = tile("cap1", [P, PACK, PICKS], F32)
+        nc.sync.dma_start(cap1[:], cap_rows[1])
 
         def whole_costs(t, after=None):
             h = tile(f"h1{t}", [P, S], F32, after)
@@ -367,44 +369,45 @@ def tile_list_spill_slot_advisor_kernel(
 
         opened = [open_scores(n) for n in range(PIECES)]
 
-        def fetch(j, slots, after):
-            picked = tile(f"x1_{j}{slots[0]}", [P, len(slots), PIECE], F32, after)
+        def fetch(name, span, slots, after):
+            picked = tile(name, [P, len(slots), span.stop - span.start], F32, after)
             for u, t in enumerate(slots):
-                nc.vector.tensor_copy(picked[:, u, :], pages[t][:].indirect(idx3[:, entries(cols(j))]))
+                nc.vector.tensor_copy(picked[:, u, :], pages[t][:].indirect(idx3[:, entries(span)]))
             return picked
 
         def fetch_pairs(j):
-            return [fetch(j, (0, 1), "z0"), fetch(j, (2, 3), "tab1")]
+            return [fetch(f"x1_{j}0", cols(j), (0, 1), "z0"), fetch(f"x1_{j}2", cols(j), (2, 3), "tab1")]
 
         def limit(j, pairs):
             rows = tile(f"z1_rows{j}", [P, PACK, PIECE], BF16, "z1_rows")
             for u in range(2):
                 slots = slice(2 * u, 2 * u + 2)
                 nc.vector.tensor_tensor(rows[:, slots, :], pairs[u][:], cap1[:, slots, cols(j)], ALU.min)
-            grouped = tile(f"z1_{j}", [P, PIECE, PACK], BF16, f"e_grouped{j}")
+            grouped = tile(f"z1_{j}", [P, PIECE, PACK], BF16)
             nc.scalar.copy(word_order(grouped[:]), row_order(rows[:]))
             return grouped
 
-        def limit_last(picked, half, after):
-            grouped = tile(f"z1_last{half}", [P, HALF, PACK], BF16, after)
-            nc.vector.tensor_tensor(
-                word_order(grouped[:]),
-                row_order(picked[:, :, HALF * half : HALF * half + HALF]),
-                row_order(cap1[:, :, spans[last + half]]),
-                ALU.min,
-            )
+        def limit_grouped(n, picked, after=None):
+            span = spans[n]
+            grouped = tile(f"z1_{n}", [P, span.stop - span.start, PACK], BF16, after)
+            nc.vector.tensor_tensor(word_order(grouped[:]), row_order(picked[:]), row_order(cap1[:, :, span]), ALU.min)
             return grouped
 
-        picked = fetch_pairs(0)
-        for n in range(last):
-            grouped = limit(n, picked)
-            picked = fetch_pairs(n + 1) if n + 1 < last else fetch(last, (0, 1, 2, 3), "z0")
-            finish(n, grouped[:])
-            store(n)
-            if n == 0:
-                opened.append(open_scores(PIECES))
-        ends = [limit_last(picked, 0, "z1_rows"), limit_last(picked, 1, None)]
-        for half in range(2):
-            finish(last + half, ends[half][:])
-        for half in range(2):
-            store(last + half)
+        every = (0, 1, 2, 3)
+        grouped = limit(0, fetch_pairs(0))
+        picked = fetch_pairs(1)
+        finish(0, grouped[:])
+        store(0)
+        opened.append(open_scores(PIECES))
+        grouped = limit(1, picked)
+        picked = fetch("x1_2", spans[2], every, "z0")
+        finish(1, grouped[:])
+        store(1)
+        finish(2, limit_grouped(2, picked, "z1_rows")[:])
+        store(2)
+        first_half = fetch("x1_3", spans[3], every, "z1_1")
+        finish(3, limit_grouped(3, first_half)[:])
+        second_half = fetch("x1_4", spans[4], every, "z0")
+        finish(4, limit_grouped(4, second_half)[:])
+        store(3)
+        store(4)

@@ -28,15 +28,31 @@ PLACES = {
     "tab_plane": 15360,
     "w2_early": 17408,
     "w1_raw": 17408,
-    "th1": 41984,
-    "front11": 41984,
-    "w2_front1": 45056,
-    "page3": 46080,
-    "cap0": 62464,
-    "back3": 77824,
-    "cap1": 78848,
-    "w1_plane_raw": 54272,
-    "page2": 54272,
+    "w2_late": 17408,
+    "th2": 16384,
+    "front13": 24576,
+    "th1": 25600,
+    "front11": 25600,
+    "w2_codes2": 25600,
+    "w2_front1": 28672,
+    "page3": 29696,
+    "w1_plane_raw": 37888,
+    "page2": 37888,
+    "page5": 46080,
+    "e_grouped1": 53248,
+    "page6": 54272,
+    "w2_back": 62464,
+    "e_rows1": 63488,
+    "back0": 64000,
+    "page7": 65536,
+    "cap0": 73728,
+    "rest02": 73728,
+    "cap1": 73728,
+    "x0_0": 90112,
+    "rest11": 90112,
+    "rest03": 97280,
+    "x0_1": 98304,
+    "rest12": 98304,
 }
 
 
@@ -130,14 +146,16 @@ def tile_list_spill_slot_advisor_kernel(
         def pick_words(a, span, after=None):
             codes = tile(f"v{a}_{span.start}", [P, span.stop - span.start], U32, after)
             nc.vector.tensor_copy(codes[:], tab[a][:].bitcast(U32).indirect(idx[:, entries(span)]))
-            return [codes[:, cols(j)] for j in range((span.stop - span.start) // PIECE)]
+            return codes
 
         picked_first = pick_scales("picked_first", cols(0))
         shift(picked_first, shifted[0])
         picked_rest = pick_scales("picked_rest", cols(1, PIECES - 1))
+        parts = [cols(0), cols(1), cols(2, 3)]
+        later = [slice(0, PIECE), slice(PIECE, S - PIECE)]
         v_plane = [
-            [picked_first[:]] + [picked_rest[:, cols(j)] for j in range(PIECES - 1)],
-            [shifted[0][:]] + [shifted[1][:, cols(j)] for j in range(PIECES - 1)],
+            [picked_first[:]] + [picked_rest[:, span] for span in later],
+            [shifted[0][:]] + [shifted[1][:, span] for span in later],
         ]
         w2_early = tile("w2_early", [P, PACK, 512], F32)
         nc.sync.dma_start(w2_early[:], w2_rows[:, :, 0:512])
@@ -166,9 +184,10 @@ def tile_list_spill_slot_advisor_kernel(
                 w1_plane_raw[:, a, :].rearrange("p (m t) -> p t m", t=PACK),
             )
         new_page()
-        v_codes = [pick_words(a, cols(0)) for a in range(2)]
-        v_codes[0].extend(pick_words(0, cols(1, PIECES - 1)))
-        v_codes[1].extend(pick_words(1, cols(1, PIECES - 1)))
+        v_codes = [[pick_words(a, cols(0))[:]] for a in range(2)]
+        for a in range(2):
+            rest = pick_words(a, cols(1, PIECES - 1))
+            v_codes[a].extend(rest[:, span] for span in later)
 
         def first_pass(dst, a, j, t, span, start, stop):
             nc.tensor.matmul_mx(
@@ -215,142 +234,143 @@ def tile_list_spill_slot_advisor_kernel(
             quantize(e_codes[0][:, span], e_plane[:, span], e_first[half][:].rearrange("p n t -> p (n t)"))
         quantize(w2_codes[0][:], w2_plane[0][:, 0:256], w2_front[0][:].rearrange("p t m j -> p (t m j)"))
 
-        def front_bank(j):
-            return 0 if j % 2 else 4
-
-        def squash(j):
-            th = tile(f"th{j}", [P, PACK, PIECE], F32, f"e_grouped{j - 1}")
-            for pair in range(2):
-                pre = bank(2 + 2 * pair if j == 1 else front_bank(j) + pair, [P, 2, PIECE])
+        def squash(j, th, banks, share):
+            width = parts[j].stop - parts[j].start
+            for n, number in enumerate(banks):
+                pre = bank(number, [P, share, width])
                 for a in range(2):
-                    for u in range(2):
-                        first_pass(pre[:, u, :], a, j, 2 * pair + u, cols(0), (a, u) == (0, 0), (a, u) == (1, 1))
-                for u in range(2):
-                    t = 2 * pair + u
+                    for u in range(share):
+                        first_pass(pre[:, u, :], a, j, share * n + u, slice(0, width), (a, u) == (0, 0), (a, u) == (1, share - 1))
+                for u in range(share):
+                    t = share * n + u
                     nc.scalar.activation(th[:, t, :], pre[:, u, :], ACT.Tanh, bias=b1_sb[:, t : t + 1])
-            return th
 
-        def features(j, th):
-            e_rows = tile(f"e_rows{j}", [P, PACK, PIECE], BF16)
+        def features(j, th, rows_after, codes_after):
+            width = parts[j].stop - parts[j].start
+            e_rows = tile(f"e_rows{j}", [P, PACK, width], BF16, rows_after)
             for t in range(PACK):
                 nc.scalar.activation(e_rows[:, t, :], th[:, t, :], ACT.Copy, scale=gain_sb[:, t : t + 1])
-            e_grouped = tile(f"e_grouped{j}", [P, PIECE, PACK], BF16)
+            e_grouped = tile(f"e_grouped{j}", [P, width, PACK], BF16)
             nc.scalar.copy(word_order(e_grouped[:]), row_order(e_rows[:]))
-            e_codes.append(tile(f"e_codes{j}", [P, PIECE], U32, f"front{j - 1}0"))
-            quantize(e_codes[j][:], e_plane[:, cols(j)], e_grouped[:].rearrange("p n t -> p (n t)"))
+            e_codes.append(tile(f"e_codes{j}", [P, width], U32, codes_after))
+            quantize(e_codes[j][:], e_plane[:, parts[j]], e_grouped[:].rearrange("p n t -> p (n t)"))
 
         def w2_slot(a, t):
             if a == 0:
                 return w2_codes[t // 2][:, 128 * (t % 2) : 128 * (t % 2) + 128]
             return w2_codes[2][:, 128 * t : 128 * t + 128]
 
-        def costs(a, parts, n, dst):
-            acc = bank(n, [P, len(parts) * PIECE])
-            for u, (t, j) in enumerate(parts):
+        def costs(name, a, terms, number, after=None):
+            widths = [parts[j].stop - parts[j].start for t, j in terms]
+            h = tile(name, [P, sum(widths)], F32, after)
+            acc = bank(number, [P, sum(widths)])
+            for u, (t, j) in enumerate(terms):
                 nc.tensor.matmul_mx(
-                    out=acc[:, cols(u)],
+                    out=acc[:, sum(widths[:u]) : sum(widths[: u + 1])],
                     lhsT=w2_slot(a, t).bitcast(FP8X4),
                     lhsT_scale=w2_plane[a][:, 128 * t : 128 * t + 128],
                     rhs=e_codes[j][:].bitcast(FP8X4),
-                    rhs_scale=e_plane[:, cols(j)],
+                    rhs_scale=e_plane[:, parts[j]],
                     start=True,
                     stop=True,
                 )
-            nc.scalar.copy(dst, acc[:])
-
-        def put(t, span, values):
-            nc.vector.tensor_tensor(pages[t][:].indirect(idx2[:, entries(span)]), values, wgs_sb[:, t, span], ALU.mult)
-
-        cap_rows = cap.rearrange("(a p t) m -> a p t m", a=2, t=PACK)
-        for j in range(PIECES):
-            ahead = 3 if j == 0 else 2
-            for t in range(ahead):
-                front = tile(f"front{j}{t}", [P, PIECE], F32, "tab0" if (j, t) == (0, 1) else None)
-                very_first = (j, t) == (0, 0)
-                costs(0, [(t, j)], front_bank(j) + t, front[:])
-                if very_first:
-                    w2_codes.append(tile("w2_codes1", [P, 256], U32, "tab1"))
-                    quantize(w2_codes[1][:], w2_plane[0][:, 256:512], w2_front[1][:].rearrange("p t m j -> p (t m j)"))
-                    new_page()
-                put(t, cols(j), front[:])
-                if (j, t) == (0, 1):
-                    w2_late = tile("w2_late", [P, PACK, 512], F32, "tab0")
-                    nc.sync.dma_start(w2_late[:], w2_rows[:, :, 512:1024])
-            if j + 1 < PIECES:
-                features(j + 1, squash(j + 1))
-            back = tile(f"back{j}", [P, (PACK - ahead) * PIECE], F32, f"e_rows{j + 1}")
-            costs(0, [(t, j) for t in range(ahead, PACK)], 7 - j % 2, back[:])
-            if ahead == 2:
-                put(2, cols(j), back[:, cols(0)])
-            if j == PIECES - 1:
-                back_tags = ("e_grouped3", "e_rows3")
-                w2_back = [tile(f"w2_back{u}", [P, 2, 128, PACK], BF16, back_tags[u]) for u in range(2)]
-                for u in range(2):
-                    round_w2(w2_late[:], w2_back[u][:], 2 * u)
-                w2_codes.append(tile("w2_codes2", [P, 512], U32, "front31"))
-                quantize(w2_codes[2][:, 0:256], w2_plane[1][:, 0:256], w2_back[0][:].rearrange("p t m j -> p (t m j)"))
-            put(3, cols(j), back[:, cols(PACK - 1 - ahead)])
-            if j == PIECES - 1:
-                quantize(w2_codes[2][:, 256:512], w2_plane[1][:, 256:512], w2_back[1][:].rearrange("p t m j -> p (t m j)"))
-            if j == PIECES - 2:
-                w3_plane = tile("w3_plane", [P, 2, N], U8, "e_rows2")
-                nc.gpsimd.memset(w3_plane[:].rearrange("p a c -> p (a c)").bitcast(I32), 0)
-                load_scale_rows(w3_plane, w3_scales)
-                w3_codes = tile("w3_codes", [P, 2, N], I32, "shifted_rest")
-                nc.sync.dma_start(w3_codes[:], w3_words.rearrange("a p c i -> p a (c i)").bitcast(I32))
-
-        cap0 = tile("cap0", [P, PACK, PICKS], F32)
-        nc.sync.dma_start(cap0[:], cap_rows[0])
-        cap1 = tile("cap1", [P, PACK, PICKS], F32)
-        nc.sync.dma_start(cap1[:], cap_rows[1])
-
-        def whole_costs(t, after=None):
-            h = tile(f"h1{t}", [P, S], F32, after)
-            for half in range(2):
-                costs(1, [(t, 2 * half), (t, 2 * half + 1)], 2 * t + half, h[:, cols(2 * half, 2 * half + 1)])
+            nc.scalar.copy(h[:], acc[:])
             return h
 
-        h1 = [whole_costs(0)]
-        whole = cols(0, PIECES - 1)
+        def put(a, t, span, values):
+            page = pages[PACK * a + t]
+            nc.vector.tensor_tensor(page[:].indirect(idx2[:, entries(span)]), values, wgs_sb[:, t, span], ALU.mult)
 
-        x0 = [tile(f"x0_{u}", [P, 2, PICKS], F32, back_tags[u]) for u in range(2)]
-        z0_rows = tile("z0_rows", [P, PACK, PICKS], BF16, "tab1")
-        z0 = tile("z0", [P, PICKS, PACK], BF16)
+        w2_late = tile("w2_late", [P, PACK, 512], F32)
+        nc.sync.dma_start(w2_late[:], w2_rows[:, :, 512:1024])
+        front = costs("front00", 0, [(0, 0)], 4)
+        w2_codes.append(tile("w2_codes1", [P, 256], U32, "tab1"))
+        quantize(w2_codes[1][:], w2_plane[0][:, 256:512], w2_front[1][:].rearrange("p t m j -> p (t m j)"))
+        new_page()
+        put(0, 0, parts[0], front[:])
+        new_page("front00")
+        for t in (1, 2):
+            put(0, t, parts[0], costs(f"front0{t}", 0, [(t, 0)], 4 + t)[:])
+        th = tile("th1", [P, PACK, PIECE], F32)
+        squash(1, th, (2, 4), 2)
+        features(1, th, None, "front01")
+        new_page()
+        new_page()
+        put(0, 3, parts[0], costs("back0", 0, [(3, 0)], 7)[:])
+
+        for t in range(2):
+            put(0, t, parts[1], costs(f"front1{t}", 0, [(t, 1)], t)[:])
+        put(0, 2, parts[1], costs("back1", 0, [(2, 1)], 6)[:])
+        w2_back = tile("w2_back", [P, PACK, 128, PACK], BF16)
+        for u in range(2):
+            round_w2(w2_late[:], w2_back[:, 2 * u : 2 * u + 2, :, :], 2 * u)
+        w2_codes.append(tile("w2_codes2", [P, 512], U32))
+        quantize(w2_codes[2][:], w2_plane[1][:], w2_back[:].rearrange("p t m j -> p (t m j)"))
+        put(0, 3, parts[1], costs("front13", 0, [(3, 1)], 7)[:])
+        new_page()
+
+        for t in range(PACK - 1):
+            put(1, t, cols(0, 1), costs(f"first1{t}", 1, [(t, 0), (t, 1)], 2 + t)[:])
+        w3_plane = tile("w3_plane", [P, 2, N], U8, "front10")
+        nc.gpsimd.memset(w3_plane[:].rearrange("p a c -> p (a c)").bitcast(I32), 0)
+        load_scale_rows(w3_plane, w3_scales)
+        w3_codes = tile("w3_codes", [P, 2, N], I32, "shifted_rest")
+        nc.sync.dma_start(w3_codes[:], w3_words.rearrange("a p c i -> p a (c i)").bitcast(I32))
+        th = tile("th2", [P, PACK, 2 * PIECE], F32)
+        squash(2, th, (0, 1, 0, 1), 1)
+        features(2, th, "first10", "first11")
+        put(1, 3, cols(0, 1), costs("first13", 1, [(3, 0), (3, 1)], 5, "first10")[:])
+
+        for t in range(PACK):
+            put(0, t, parts[2], costs(f"rest0{t}", 0, [(t, 2)], 4 + t)[:])
+        cap_rows = cap.rearrange("(a p t) m -> a p t m", a=2, t=PACK)
+        cap0 = tile("cap0", [P, PACK, PICKS], F32)
+        nc.sync.dma_start(cap0[:], cap_rows[0])
+        rest = [costs("rest10", 1, [(0, 2)], 0)]
+        x0 = [tile(f"x0_{u}", [P, 2, PICKS], F32) for u in range(2)]
+        z0_rows = tile("z0_rows", [P, PACK, PICKS], BF16, "tab0")
+        z0 = tile("z0", [P, PICKS, PACK], BF16, "v0_256")
         z_codes = [tile(f"z_codes{a}", [P, PICKS], U32) for a in range(2)]
         z_plane = [tile(f"z_plane{a}", [P, PICKS], U8) for a in range(2)]
         for t in range(PACK):
             nc.vector.tensor_copy(x0[t // 2][:, t % 2, :], pages[t][:].indirect(idx3[:]))
-        put(0, whole, h1[0][:])
+        put(1, 0, parts[2], rest[0][:])
         for u in range(2):
             slots = slice(2 * u, 2 * u + 2)
             nc.vector.tensor_tensor(z0_rows[:, slots, :], x0[u][:], cap0[:, slots, :], ALU.min)
-            h1.append(whole_costs(1 + u, back_tags[u]))
+            rest.append(costs(f"rest1{1 + u}", 1, [(1 + u, 2)], 1 + u))
+        cap1 = tile("cap1", [P, PACK, PICKS], F32)
+        nc.sync.dma_start(cap1[:], cap_rows[1])
         nc.scalar.copy(word_order(z0[:]), row_order(z0_rows[:]))
-        h1.append(whole_costs(3, "tab1"))
+        rest.append(costs("rest13", 1, [(3, 2)], 3, "tab0"))
         for t in range(1, PACK):
             if t == PACK - 1:
                 quantize(z_codes[0][:], z_plane[0][:], z0[:].rearrange("p n t -> p (n t)"))
-            put(t, whole, h1[t][:])
+            put(1, t, parts[2], rest[t][:])
 
         out_rows = out.rearrange("(c p) m -> p c m", p=P)
         last = PIECES - 1
         spans = [cols(j) for j in range(last)] + [slice(768, 896), slice(896, 1024)]
 
         def score_pass(a, banks, span):
+            share = 4 // len(banks)
             for c in range(4):
                 nc.tensor.matmul_mx(
-                    out=banks[c // 2][:, c % 2, :],
+                    out=banks[c // share][:, c % share, :],
                     lhsT=w3_codes[:, a, 128 * c : 128 * c + 128].bitcast(FP8X4),
                     lhsT_scale=w3_plane[:, a, 128 * c : 128 * c + 128],
                     rhs=z_codes[a][:, span].bitcast(FP8X4),
                     rhs_scale=z_plane[a][:, span],
-                    start=(a == 0 and c % 2 == 0),
-                    stop=(a == 1 and c % 2 == 1),
+                    start=(a == 0 and c % share == 0),
+                    stop=(a == 1 and c % share == share - 1),
                 )
 
         def open_scores(n):
             span = spans[n]
-            banks = [bank((2 * n + c) % 8, [P, 2, span.stop - span.start]) for c in range(2)]
+            if n == PIECES:
+                banks = [bank(c, [P, 1, HALF]) for c in range(4)]
+            else:
+                banks = [bank(2 * n + c, [P, 2, span.stop - span.start]) for c in range(2)]
             score_pass(0, banks, span)
             return banks
 
@@ -363,8 +383,7 @@ def tile_list_spill_slot_advisor_kernel(
             span = spans[n]
             for pair in range(2):
                 staged = tile(f"staged{n}{pair}", [P, 2, span.stop - span.start], F32)
-                copy = nc.vector.tensor_copy if (n >= last and pair == 0) else nc.scalar.copy
-                copy(staged[:], opened[n][pair][:])
+                nc.scalar.copy(staged[:], opened[n][pair][:])
                 nc.sync.dma_start(out_rows[:, 2 * pair : 2 * pair + 2, span], staged[:])
 
         opened = [open_scores(n) for n in range(PIECES)]
@@ -372,11 +391,11 @@ def tile_list_spill_slot_advisor_kernel(
         def fetch(name, span, slots, after):
             picked = tile(name, [P, len(slots), span.stop - span.start], F32, after)
             for u, t in enumerate(slots):
-                nc.vector.tensor_copy(picked[:, u, :], pages[t][:].indirect(idx3[:, entries(span)]))
+                nc.vector.tensor_copy(picked[:, u, :], pages[PACK + t][:].indirect(idx3[:, entries(span)]))
             return picked
 
         def fetch_pairs(j):
-            return [fetch(f"x1_{j}0", cols(j), (0, 1), "z0"), fetch(f"x1_{j}2", cols(j), (2, 3), "tab1")]
+            return [fetch(f"x1_{j}0", cols(j), (0, 1), "v0_256"), fetch(f"x1_{j}2", cols(j), (2, 3), "tab0")]
 
         def limit(j, pairs):
             rows = tile(f"z1_rows{j}", [P, PACK, PIECE], BF16, "z1_rows")
@@ -398,16 +417,20 @@ def tile_list_spill_slot_advisor_kernel(
         picked = fetch_pairs(1)
         finish(0, grouped[:])
         store(0)
-        opened.append(open_scores(PIECES))
         grouped = limit(1, picked)
-        picked = fetch("x1_2", spans[2], every, "z0")
+        picked = fetch("x1_2", spans[2], every, "v0_256")
         finish(1, grouped[:])
         store(1)
+        opened.append(open_scores(PIECES))
         finish(2, limit_grouped(2, picked, "z1_rows")[:])
         store(2)
         first_half = fetch("x1_3", spans[3], every, "z1_1")
         finish(3, limit_grouped(3, first_half)[:])
-        second_half = fetch("x1_4", spans[4], every, "z0")
+        second_half = fetch("x1_4", spans[4], every, "v0_256")
         finish(4, limit_grouped(4, second_half)[:])
         store(3)
-        store(4)
+        for pair in range(2):
+            staged = tile(f"staged4{pair}", [P, 2, HALF], F32)
+            nc.vector.tensor_copy(staged[:, 0, :], opened[PIECES][2 * pair][:, 0, :])
+            nc.scalar.copy(staged[:, 1, :], opened[PIECES][2 * pair + 1][:, 0, :])
+            nc.sync.dma_start(out_rows[:, 2 * pair : 2 * pair + 2, spans[PIECES]], staged[:])

@@ -26,33 +26,30 @@ HALF = 128
 PLACES = {
     "wgs_sb": 0,
     "tab_plane": 15360,
-    "w2_early": 17408,
-    "w1_raw": 17408,
-    "w2_late": 17408,
-    "th2": 16384,
-    "front13": 24576,
-    "th1": 25600,
-    "front11": 25600,
-    "w2_codes2": 25600,
-    "w2_front1": 28672,
-    "page3": 29696,
-    "w1_plane_raw": 37888,
-    "page2": 37888,
-    "page5": 46080,
-    "e_grouped1": 53248,
-    "page6": 54272,
-    "w2_back": 62464,
-    "e_rows1": 63488,
-    "back0": 64000,
-    "page7": 65536,
-    "cap0": 73728,
-    "rest02": 73728,
-    "cap1": 73728,
-    "x0_0": 90112,
-    "rest11": 90112,
-    "rest03": 97280,
-    "x0_1": 98304,
-    "rest12": 98304,
+    "w2_late": 16384,
+    "cost03": 16384,
+    "th1": 17408,
+    "th2": 17408,
+    "w2_early": 24576,
+    "w1_raw": 24576,
+    "page2": 32768,
+    "w1_plane_raw": 40448,
+    "page3": 40960,
+    "page4": 49152,
+    "w2_front1": 56320,
+    "page5": 57344,
+    "page6": 65536,
+    "cost00": 71680,
+    "w2_back": 71680,
+    "page7": 73728,
+    "cap0": 81920,
+    "rest02": 81920,
+    "cap1": 81920,
+    "x0_0": 16384,
+    "rest11": 16384,
+    "rest03": 23552,
+    "x0_1": 24576,
+    "rest12": 24576,
 }
 
 
@@ -169,6 +166,8 @@ def tile_list_spill_slot_advisor_kernel(
 
         load_weights(slice(0, 2), cols(0))
         load_weights(slice(2, PACK), cols(0))
+        w2_late = tile("w2_late", [P, PACK, 512], F32)
+        nc.sync.dma_start(w2_late[:], w2_rows[:, :, 512:1024])
         load_weights(slice(0, PACK), cols(1))
         load_weights(slice(0, PACK), cols(2, PIECES - 1))
 
@@ -183,6 +182,7 @@ def tile_list_spill_slot_advisor_kernel(
                 w1_plane[:, a, :].rearrange("p (t m) -> p t m", t=PACK),
                 w1_plane_raw[:, a, :].rearrange("p (m t) -> p t m", t=PACK),
             )
+        new_page()
         new_page()
         v_codes = [[pick_words(a, cols(0))[:]] for a in range(2)]
         for a in range(2):
@@ -281,45 +281,40 @@ def tile_list_spill_slot_advisor_kernel(
             page = pages[PACK * a + t]
             nc.vector.tensor_tensor(page[:].indirect(idx2[:, entries(span)]), values, wgs_sb[:, t, span], ALU.mult)
 
-        w2_late = tile("w2_late", [P, PACK, 512], F32)
-        nc.sync.dma_start(w2_late[:], w2_rows[:, :, 512:1024])
-        front = costs("front00", 0, [(0, 0)], 4)
+        h = costs("cost00", 0, [(0, 0)], 4)
         w2_codes.append(tile("w2_codes1", [P, 256], U32, "tab1"))
         quantize(w2_codes[1][:], w2_plane[0][:, 256:512], w2_front[1][:].rearrange("p t m j -> p (t m j)"))
         new_page()
-        put(0, 0, parts[0], front[:])
-        new_page("front00")
+        new_page()
+        put(0, 0, parts[0], h[:])
         for t in (1, 2):
-            put(0, t, parts[0], costs(f"front0{t}", 0, [(t, 0)], 4 + t)[:])
-        th = tile("th1", [P, PACK, PIECE], F32)
-        squash(1, th, (2, 4), 2)
-        features(1, th, None, "front01")
-        new_page()
-        new_page()
-        put(0, 3, parts[0], costs("back0", 0, [(3, 0)], 7)[:])
-
-        for t in range(2):
-            put(0, t, parts[1], costs(f"front1{t}", 0, [(t, 1)], t)[:])
-        put(0, 2, parts[1], costs("back1", 0, [(2, 1)], 6)[:])
+            put(0, t, parts[0], costs(f"cost0{t}", 0, [(t, 0)], 4 + t)[:])
         w2_back = tile("w2_back", [P, PACK, 128, PACK], BF16)
         for u in range(2):
             round_w2(w2_late[:], w2_back[:, 2 * u : 2 * u + 2, :, :], 2 * u)
-        w2_codes.append(tile("w2_codes2", [P, 512], U32))
+        w2_codes.append(tile("w2_codes2", [P, 512], U32, "cost01"))
         quantize(w2_codes[2][:], w2_plane[1][:], w2_back[:].rearrange("p t m j -> p (t m j)"))
-        put(0, 3, parts[1], costs("front13", 0, [(3, 1)], 7)[:])
         new_page()
-
+        new_page()
+        put(0, 3, parts[0], costs("cost03", 0, [(3, 0)], 7)[:])
         for t in range(PACK - 1):
-            put(1, t, cols(0, 1), costs(f"first1{t}", 1, [(t, 0), (t, 1)], 2 + t)[:])
-        w3_plane = tile("w3_plane", [P, 2, N], U8, "front10")
+            put(1, t, parts[0], costs(f"cost0{4 + t}", 1, [(t, 0)], t)[:])
+        th = tile("th1", [P, PACK, PIECE], F32)
+        squash(1, th, (4, 5), 2)
+        features(1, th, None, "cost05")
+        put(1, 3, parts[0], costs("cost07", 1, [(3, 0)], 3, "e_rows1")[:])
+
+        for n in range(2 * PACK - 1):
+            put(n // PACK, n % PACK, parts[1], costs(f"cost1{n}", n // PACK, [(n % PACK, 1)], 2 + n % 6)[:])
+        w3_plane = tile("w3_plane", [P, 2, N], U8, "cost11")
         nc.gpsimd.memset(w3_plane[:].rearrange("p a c -> p (a c)").bitcast(I32), 0)
         load_scale_rows(w3_plane, w3_scales)
         w3_codes = tile("w3_codes", [P, 2, N], I32, "shifted_rest")
         nc.sync.dma_start(w3_codes[:], w3_words.rearrange("a p c i -> p a (c i)").bitcast(I32))
         th = tile("th2", [P, PACK, 2 * PIECE], F32)
         squash(2, th, (0, 1, 0, 1), 1)
-        features(2, th, "first10", "first11")
-        put(1, 3, cols(0, 1), costs("first13", 1, [(3, 0), (3, 1)], 5, "first10")[:])
+        features(2, th, "cost10", "cost15")
+        put(1, 3, parts[1], costs("cost17", 1, [(3, 1)], 3, "cost10")[:])
 
         for t in range(PACK):
             put(0, t, parts[2], costs(f"rest0{t}", 0, [(t, 2)], 4 + t)[:])

@@ -43,13 +43,17 @@ PLACES = {
     "w2_back": 71680,
     "page7": 73728,
     "cap0": 81920,
-    "rest02": 81920,
     "cap1": 81920,
     "x0_0": 16384,
     "rest11": 16384,
-    "rest03": 23552,
-    "x0_1": 24576,
-    "rest12": 24576,
+    "rest02": 16384,
+    "rest03": 97280,
+    "x0_1": 98304,
+    "rest12": 98304,
+    "z1_rows0": 16384,
+    "z1_rows1": 18368,
+    "staged01": 18432,
+    "z1_2": 20480,
 }
 
 
@@ -374,9 +378,9 @@ def tile_list_spill_slot_advisor_kernel(
             quantize(z_codes[1][:, span], z_plane[1][:, span], grouped.rearrange("p n t -> p (n t)"))
             score_pass(1, opened[n], span)
 
-        def store(n):
+        def store(n, pairs=(0, 1)):
             span = spans[n]
-            for pair in range(2):
+            for pair in pairs:
                 staged = tile(f"staged{n}{pair}", [P, 2, span.stop - span.start], F32)
                 nc.scalar.copy(staged[:], opened[n][pair][:])
                 nc.sync.dma_start(out_rows[:, 2 * pair : 2 * pair + 2, span], staged[:])
@@ -393,12 +397,12 @@ def tile_list_spill_slot_advisor_kernel(
             return [fetch(f"x1_{j}0", cols(j), (0, 1), "v0_256"), fetch(f"x1_{j}2", cols(j), (2, 3), "tab0")]
 
         def limit(j, pairs):
-            rows = tile(f"z1_rows{j}", [P, PACK, PIECE], BF16, "z1_rows")
+            rows = tile(f"z1_rows{j}", [P, PACK * (1 + j), PIECE], BF16)[:, 0:PACK, :]
             for u in range(2):
                 slots = slice(2 * u, 2 * u + 2)
                 nc.vector.tensor_tensor(rows[:, slots, :], pairs[u][:], cap1[:, slots, cols(j)], ALU.min)
             grouped = tile(f"z1_{j}", [P, PIECE, PACK], BF16)
-            nc.scalar.copy(word_order(grouped[:]), row_order(rows[:]))
+            nc.scalar.copy(word_order(grouped[:]), row_order(rows))
             return grouped
 
         def limit_grouped(n, picked, after=None):
@@ -411,13 +415,14 @@ def tile_list_spill_slot_advisor_kernel(
         grouped = limit(0, fetch_pairs(0))
         picked = fetch_pairs(1)
         finish(0, grouped[:])
-        store(0)
+        store(0, (0,))
         grouped = limit(1, picked)
+        store(0, (1,))
         picked = fetch("x1_2", spans[2], every, "v0_256")
         finish(1, grouped[:])
         store(1)
         opened.append(open_scores(PIECES))
-        finish(2, limit_grouped(2, picked, "z1_rows")[:])
+        finish(2, limit_grouped(2, picked)[:])
         store(2)
         first_half = fetch("x1_3", spans[3], every, "z1_1")
         finish(3, limit_grouped(3, first_half)[:])

@@ -369,7 +369,7 @@ def tile_list_spill_slot_advisor_kernel(
             if n == PIECES:
                 banks = [bank(c, [P, 1, HALF]) for c in range(4)]
             else:
-                banks = [bank(2 * n + c, [P, 2, span.stop - span.start]) for c in range(2)]
+                banks = [bank(2 * min(n, last - 1) + c, [P, 2, span.stop - span.start]) for c in range(2)]
             score_pass(0, banks, span)
             return banks
 
@@ -385,7 +385,7 @@ def tile_list_spill_slot_advisor_kernel(
                 nc.scalar.copy(staged[:], opened[n][pair][:])
                 nc.sync.dma_start(out_rows[:, 2 * pair : 2 * pair + 2, span], staged[:])
 
-        opened = [open_scores(n) for n in range(PIECES)]
+        opened = {n: open_scores(n) for n in range(last)}
 
         def fetch(name, span, slots, after):
             picked = tile(name, [P, len(slots), span.stop - span.start], F32, after)
@@ -421,9 +421,10 @@ def tile_list_spill_slot_advisor_kernel(
         picked = fetch("x1_2", spans[2], every, "v0_256")
         finish(1, grouped[:])
         store(1)
-        opened.append(open_scores(PIECES))
+        opened[PIECES] = open_scores(PIECES)
         finish(2, limit_grouped(2, picked)[:])
         store(2)
+        opened[last] = open_scores(last)
         first_half = fetch("x1_3", spans[3], every, "z1_1")
         finish(3, limit_grouped(3, first_half)[:])
         second_half = fetch("x1_4", spans[4], every, "v0_256")

@@ -33,7 +33,7 @@ PLACES = {
     "w2_early": 24576,
     "w1_raw": 24576,
     "page2": 32768,
-    "w1_plane_raw": 40448,
+    "w1_plane_raw": 40960,
     "page3": 40960,
     "page4": 49152,
     "w2_front1": 56320,
@@ -92,10 +92,15 @@ def tile_list_spill_slot_advisor_kernel(
 
         pages = []
 
-        def new_page(after=None):
-            page = tile(f"page{len(pages)}", [P, T2], F32, after)
+        def new_page():
+            page = tile(f"page{len(pages)}", [P, T2], F32)
             nc.gpsimd.memset(page[:], 0.0)
             pages.append(page)
+
+        def zero_on_vector(words, zero):
+            last = words.shape[1] - 1
+            nc.vector.memset(words[:, 0:last], zero)
+            nc.vector.memset(words[:, last : last + 1], zero)
 
         def load_scale_rows(plane, scales):
             for q in range(4):
@@ -108,6 +113,8 @@ def tile_list_spill_slot_advisor_kernel(
         w1_plane_raw = tile("w1_plane_raw", [P, 2, M], U8)
         shifted = [tile("shifted_first", [P, PIECE], U8), tile("shifted_rest", [P, S - PIECE], U8)]
         nc.gpsimd.memset(tab_plane[:].bitcast(I32), 0)
+        pages.append(tile("page0", [P, T2], F32))
+        zero_on_vector(pages[0][:], 0.0)
         nc.gpsimd.memset(w1_plane_raw[:].rearrange("p a c -> p (a c)").bitcast(I32), 0)
         for plane in shifted:
             nc.gpsimd.memset(plane[96:128, :].bitcast(I32), 0)
@@ -187,7 +194,6 @@ def tile_list_spill_slot_advisor_kernel(
                 w1_plane_raw[:, a, :].rearrange("p (m t) -> p t m", t=PACK),
             )
         new_page()
-        new_page()
         v_codes = [[pick_words(a, cols(0))[:]] for a in range(2)]
         for a in range(2):
             rest = pick_words(a, cols(1, PIECES - 1))
@@ -218,10 +224,10 @@ def tile_list_spill_slot_advisor_kernel(
         sums = [(half, t, bank(PACK * half + t, [P, HALF])) for half in range(2) for t in range(PACK)]
         for half, t, pre in sums:
             first_pass(pre[:], 0, 0, t, halves[half], True, False)
-        th0 = [tile(f"th0{half}", [P, PACK, HALF], F32) for half in range(2)]
+        th0 = [tile(f"th0{half}", [P, HALF // 4, PACK, 4], F32) for half in range(2)]
         for half, t, pre in sums:
             first_pass(pre[:], 1, 0, t, halves[half], False, True)
-            nc.scalar.activation(th0[half][:, t, :], pre[:], ACT.Tanh, bias=b1_sb[:, t : t + 1])
+            nc.scalar.activation(th0[half][:, :, t, :], pre[:].rearrange("p (c i) -> p c i", i=4), ACT.Tanh, bias=b1_sb[:, t : t + 1])
         w2_front = [tile(f"w2_front{u}", [P, 2, 128, PACK], BF16) for u in range(2)]
         for u in range(2):
             round_w2(w2_early[:], w2_front[u][:], 2 * u)
@@ -229,7 +235,7 @@ def tile_list_spill_slot_advisor_kernel(
         for half in range(2):
             nc.vector.tensor_tensor(
                 word_order(e_first[half][:]),
-                row_order(th0[half][:]),
+                th0[half][:],
                 gain_sb[:].unsqueeze(1).unsqueeze(3).to_broadcast([P, HALF // 4, PACK, 4]),
                 ALU.mult,
             )

@@ -33,10 +33,10 @@ PLACES = {
     "w2_early": 24576,
     "w1_raw": 24576,
     "page2": 32768,
-    "w1_plane_raw": 40960,
+    "w1_plane_raw": 48640,
     "page3": 40960,
     "page4": 49152,
-    "w2_front1": 56320,
+    "w2_front1": 57344,
     "page5": 57344,
     "page6": 65536,
     "cost00": 71680,
@@ -194,6 +194,7 @@ def tile_list_spill_slot_advisor_kernel(
                 w1_plane_raw[:, a, :].rearrange("p (m t) -> p t m", t=PACK),
             )
         new_page()
+        new_page()
         v_codes = [[pick_words(a, cols(0))[:]] for a in range(2)]
         for a in range(2):
             rest = pick_words(a, cols(1, PIECES - 1))
@@ -295,7 +296,6 @@ def tile_list_spill_slot_advisor_kernel(
         w2_codes.append(tile("w2_codes1", [P, 256], U32, "tab1"))
         quantize(w2_codes[1][:], w2_plane[0][:, 256:512], w2_front[1][:].rearrange("p t m j -> p (t m j)"))
         new_page()
-        new_page()
         put(0, 0, parts[0], h[:])
         for t in (1, 2):
             put(0, t, parts[0], costs(f"cost0{t}", 0, [(t, 0)], 4 + t)[:])
@@ -314,7 +314,7 @@ def tile_list_spill_slot_advisor_kernel(
         features(1, th, None, "cost05")
         put(1, 3, parts[0], costs("cost07", 1, [(3, 0)], 3, "e_rows1")[:])
 
-        for n in range(2 * PACK - 1):
+        for n in range(2 * PACK - 2):
             put(n // PACK, n % PACK, parts[1], costs(f"cost1{n}", n // PACK, [(n % PACK, 1)], 2 + n % 6)[:])
         w3_plane = tile("w3_plane", [P, 2, N], U8, "cost11")
         nc.gpsimd.memset(w3_plane[:].rearrange("p a c -> p (a c)").bitcast(I32), 0)
@@ -323,8 +323,10 @@ def tile_list_spill_slot_advisor_kernel(
         nc.sync.dma_start(w3_codes[:], w3_words.rearrange("a p c i -> p a (c i)").bitcast(I32))
         th = tile("th2", [P, PACK, 2 * PIECE], F32)
         squash(2, th, (0, 1, 0, 1), 1)
-        features(2, th, "cost10", "cost15")
-        put(1, 3, parts[1], costs("cost17", 1, [(3, 1)], 3, "cost10")[:])
+        features(2, th, "cost10", "cost14")
+        h = costs("cost16", 1, [(2, 1), (3, 1)], 3, "cost10")
+        for u in range(2):
+            put(1, 2 + u, parts[1], h[:, cols(u)])
 
         for t in range(PACK):
             put(0, t, parts[2], costs(f"rest0{t}", 0, [(t, 2)], 4 + t)[:])

@@ -26,21 +26,22 @@ HALF = 128
 PLACES = {
     "wgs_sb": 0,
     "tab_plane": 15360,
-    "w2_late": 16384,
-    "cost03": 16384,
-    "th1": 17408,
-    "th2": 17408,
+    "tab0": 73728,
+    "w2_late": 74752,
+    "cost02": 74752,
+    "th1": 81920,
+    "th2": 81920,
     "w2_early": 24576,
     "w1_raw": 24576,
     "page2": 32768,
     "w1_plane_raw": 48640,
     "page3": 40960,
     "page4": 49152,
-    "w2_front1": 57344,
+    "w2_front1": 64512,
+    "w2_back": 65536,
+    "cost03": 75776,
     "page5": 57344,
     "page6": 65536,
-    "cost00": 71680,
-    "w2_back": 71680,
     "page7": 73728,
     "cap0": 81920,
     "cap1": 81920,
@@ -176,9 +177,9 @@ def tile_list_spill_slot_advisor_kernel(
                 nc.sync.dma_start(wgs_sb[32 * q : 32 * q + 32, slots, span], wgs_rows[:, slots, span])
 
         load_weights(slice(0, 2), cols(0))
-        load_weights(slice(2, PACK), cols(0))
         w2_late = tile("w2_late", [P, PACK, 512], F32)
         nc.sync.dma_start(w2_late[:], w2_rows[:, :, 512:1024])
+        load_weights(slice(2, PACK), cols(0))
         load_weights(slice(0, PACK), cols(1))
         load_weights(slice(0, PACK), cols(2, PIECES - 1))
 
@@ -297,22 +298,23 @@ def tile_list_spill_slot_advisor_kernel(
         quantize(w2_codes[1][:], w2_plane[0][:, 256:512], w2_front[1][:].rearrange("p t m j -> p (t m j)"))
         new_page()
         put(0, 0, parts[0], h[:])
-        for t in (1, 2):
-            put(0, t, parts[0], costs(f"cost0{t}", 0, [(t, 0)], 4 + t)[:])
+        put(0, 1, parts[0], costs("cost01", 0, [(1, 0)], 5)[:])
         w2_back = tile("w2_back", [P, PACK, 128, PACK], BF16)
         for u in range(2):
             round_w2(w2_late[:], w2_back[:, 2 * u : 2 * u + 2, :, :], 2 * u)
-        w2_codes.append(tile("w2_codes2", [P, 512], U32, "cost01"))
+        w2_codes.append(tile("w2_codes2", [P, 512], U32))
         quantize(w2_codes[2][:], w2_plane[1][:], w2_back[:].rearrange("p t m j -> p (t m j)"))
         new_page()
-        new_page()
-        put(0, 3, parts[0], costs("cost03", 0, [(3, 0)], 7)[:])
-        for t in range(PACK - 1):
-            put(1, t, parts[0], costs(f"cost0{4 + t}", 1, [(t, 0)], t)[:])
+        for n in range(2, 2 * PACK - 2):
+            put(n // PACK, n % PACK, parts[0], costs(f"cost0{n}", n // PACK, [(n % PACK, 0)], (4 + n) % 8)[:])
+            if n == 3:
+                new_page()
         th = tile("th1", [P, PACK, PIECE], F32)
         squash(1, th, (4, 5), 2)
-        features(1, th, None, "cost05")
-        put(1, 3, parts[0], costs("cost07", 1, [(3, 0)], 3, "e_rows1")[:])
+        features(1, th, None, "cost04")
+        h = costs("cost06", 1, [(2, 0), (3, 0)], 7, "e_rows1")
+        for u in range(2):
+            put(1, 2 + u, parts[0], h[:, cols(u)])
 
         for n in range(2 * PACK - 2):
             put(n // PACK, n % PACK, parts[1], costs(f"cost1{n}", n // PACK, [(n % PACK, 1)], 2 + n % 6)[:])

@@ -34,15 +34,16 @@ PLACES = {
     "w2_early": 24576,
     "w1_raw": 24576,
     "page2": 32768,
-    "w1_plane_raw": 48640,
+    "w1_plane_raw": 40960,
     "page3": 40960,
     "page4": 49152,
-    "w2_front1": 64512,
-    "w2_back": 65536,
+    "w2_front1": 56320,
+    "w2_back": 57344,
+    "e_grouped1": 65536,
     "cost03": 75776,
     "page5": 57344,
-    "page6": 65536,
-    "page7": 73728,
+    "page6": 73728,
+    "page7": 65536,
     "cap0": 81920,
     "cap1": 81920,
     "x0_0": 16384,
@@ -195,7 +196,6 @@ def tile_list_spill_slot_advisor_kernel(
                 w1_plane_raw[:, a, :].rearrange("p (m t) -> p t m", t=PACK),
             )
         new_page()
-        new_page()
         v_codes = [[pick_words(a, cols(0))[:]] for a in range(2)]
         for a in range(2):
             rest = pick_words(a, cols(1, PIECES - 1))
@@ -275,6 +275,11 @@ def tile_list_spill_slot_advisor_kernel(
         def costs(name, a, terms, number, after=None):
             widths = [parts[j].stop - parts[j].start for t, j in terms]
             h = tile(name, [P, sum(widths)], F32, after)
+            fill(h[:], a, terms, number)
+            return h
+
+        def fill(h, a, terms, number):
+            widths = [parts[j].stop - parts[j].start for t, j in terms]
             acc = bank(number, [P, sum(widths)])
             for u, (t, j) in enumerate(terms):
                 nc.tensor.matmul_mx(
@@ -286,8 +291,7 @@ def tile_list_spill_slot_advisor_kernel(
                     start=True,
                     stop=True,
                 )
-            nc.scalar.copy(h[:], acc[:])
-            return h
+            nc.scalar.copy(h, acc[:])
 
         def put(a, t, span, values):
             page = pages[PACK * a + t]
@@ -312,9 +316,8 @@ def tile_list_spill_slot_advisor_kernel(
         th = tile("th1", [P, PACK, PIECE], F32)
         squash(1, th, (4, 5), 2)
         features(1, th, None, "cost04")
-        h = costs("cost06", 1, [(2, 0), (3, 0)], 7, "e_rows1")
-        for u in range(2):
-            put(1, 2 + u, parts[0], h[:, cols(u)])
+        new_page()
+        put(1, 2, parts[0], costs("cost06", 1, [(2, 0)], 7, "e_rows1")[:])
 
         for n in range(2 * PACK - 2):
             put(n // PACK, n % PACK, parts[1], costs(f"cost1{n}", n // PACK, [(n % PACK, 1)], 2 + n % 6)[:])
@@ -326,9 +329,11 @@ def tile_list_spill_slot_advisor_kernel(
         th = tile("th2", [P, PACK, 2 * PIECE], F32)
         squash(2, th, (0, 1, 0, 1), 1)
         features(2, th, "cost10", "cost14")
-        h = costs("cost16", 1, [(2, 1), (3, 1)], 3, "cost10")
-        for u in range(2):
-            put(1, 2 + u, parts[1], h[:, cols(u)])
+        h = tile("cost16", [P, 3 * PIECE], F32, "cost10")
+        fill(h[:, cols(0)], 1, [(2, 1)], 3)
+        fill(h[:, cols(1, 2)], 1, [(3, 0), (3, 1)], 2)
+        put(1, 2, parts[1], h[:, cols(0)])
+        put(1, 3, cols(0, 1), h[:, cols(1, 2)])
 
         for t in range(PACK):
             put(0, t, parts[2], costs(f"rest0{t}", 0, [(t, 2)], 4 + t)[:])

@@ -53,8 +53,7 @@ PLACES = {
     "x0_1": 98304,
     "rest12": 98304,
     "z1_rows0": 16384,
-    "z1_rows1": 18368,
-    "staged01": 18432,
+    "z1_rows1": 18432,
     "z1_2": 20480,
 }
 
@@ -408,14 +407,17 @@ def tile_list_spill_slot_advisor_kernel(
                 nc.vector.tensor_copy(picked[:, u, :], pages[PACK + t][:].indirect(idx3[:, entries(span)]))
             return picked
 
-        def fetch_pairs(j):
-            return [fetch(f"x1_{j}0", cols(j), (0, 1), "v0_256"), fetch(f"x1_{j}2", cols(j), (2, 3), "tab0")]
+        lower = fetch("x1_lower", cols(0, 1), (0, 1), "v0_256")
+        upper = fetch("x1_upper", cols(0, 1), (2, 3), "tab0")
+
+        def pairs_of(j):
+            return [lower[:, :, cols(j)], upper[:, :, cols(j)]]
 
         def limit(j, pairs):
             rows = tile(f"z1_rows{j}", [P, PACK * (1 + j), PIECE], BF16)[:, 0:PACK, :]
             for u in range(2):
                 slots = slice(2 * u, 2 * u + 2)
-                nc.vector.tensor_tensor(rows[:, slots, :], pairs[u][:], cap1[:, slots, cols(j)], ALU.min)
+                nc.vector.tensor_tensor(rows[:, slots, :], pairs[u], cap1[:, slots, cols(j)], ALU.min)
             grouped = tile(f"z1_{j}", [P, PIECE, PACK], BF16)
             nc.scalar.copy(word_order(grouped[:]), row_order(rows))
             return grouped
@@ -427,12 +429,10 @@ def tile_list_spill_slot_advisor_kernel(
             return grouped
 
         every = (0, 1, 2, 3)
-        grouped = limit(0, fetch_pairs(0))
-        picked = fetch_pairs(1)
-        finish(0, grouped[:])
-        store(0, (0,))
-        grouped = limit(1, picked)
-        store(0, (1,))
+        first = limit(0, pairs_of(0))
+        grouped = limit(1, pairs_of(1))
+        finish(0, first[:])
+        store(0)
         picked = fetch("x1_2", spans[2], every, "v0_256")
         finish(1, grouped[:])
         store(1)

@@ -34,8 +34,10 @@ PLACES = {
     "w2_early": 24576,
     "w1_raw": 24576,
     "page2": 32768,
-    "w1_plane_raw": 40960,
-    "page3": 40960,
+    "tab1": 40960,
+    "w2_codes1": 40960,
+    "w1_plane_raw": 116736,
+    "page3": 116736,
     "page4": 49152,
     "w2_front1": 56320,
     "w2_back": 57344,
@@ -44,17 +46,28 @@ PLACES = {
     "page5": 57344,
     "page6": 73728,
     "page7": 65536,
-    "cap0": 81920,
     "cap1": 81920,
-    "x0_0": 16384,
-    "rest11": 16384,
-    "rest02": 16384,
-    "rest03": 97280,
-    "x0_1": 98304,
-    "rest12": 98304,
-    "z1_rows0": 16384,
-    "z1_rows1": 18432,
-    "z1_2": 20480,
+    "x0": 16384,
+    "gap2": 20480,
+    "z_0": 20480,
+    "z_3": 20480,
+    "x2": 24576,
+    "z_1": 24576,
+    "z_4": 24576,
+    "take0": 28672,
+    "x_upper": 32768,
+    "cost12": 98304,
+    "cap0_0": 98304,
+    "cost13": 102400,
+    "cap0_1": 102400,
+    "cost15": 106496,
+    "cap0_2": 106496,
+    "x3": 106496,
+    "z_2": 106496,
+    "cost14": 110592,
+    "e_codes2": 110592,
+    "cap0_3": 112640,
+    "cost05": 112640,
 }
 
 
@@ -334,119 +347,174 @@ def tile_list_spill_slot_advisor_kernel(
         put(1, 2, parts[1], h[:, cols(0)])
         put(1, 3, cols(0, 1), h[:, cols(1, 2)])
 
-        for t in range(PACK):
-            put(0, t, parts[2], costs(f"rest0{t}", 0, [(t, 2)], 4 + t)[:])
+        late = parts[2]
+        rest = [costs(f"rest{k}", k // PACK, [(k % PACK, 2)], (4 + k) % 8) for k in range(2 * PACK)]
         cap_rows = cap.rearrange("(a p t) m -> a p t m", a=2, t=PACK)
-        cap0 = tile("cap0", [P, PACK, PICKS], F32)
-        nc.sync.dma_start(cap0[:], cap_rows[0])
-        rest = [costs("rest10", 1, [(0, 2)], 0)]
-        x0 = [tile(f"x0_{u}", [P, 2, PICKS], F32) for u in range(2)]
-        z0_rows = tile("z0_rows", [P, PACK, PICKS], BF16, "tab0")
-        z0 = tile("z0", [P, PICKS, PACK], BF16, "v0_256")
-        z_codes = [tile(f"z_codes{a}", [P, PICKS], U32) for a in range(2)]
-        z_plane = [tile(f"z_plane{a}", [P, PICKS], U8) for a in range(2)]
+        cap0 = [tile(f"cap0_{t}", [P, PICKS], F32) for t in range(PACK)]
         for t in range(PACK):
-            nc.vector.tensor_copy(x0[t // 2][:, t % 2, :], pages[t][:].indirect(idx3[:]))
-        put(1, 0, parts[2], rest[0][:])
-        for u in range(2):
-            slots = slice(2 * u, 2 * u + 2)
-            nc.vector.tensor_tensor(z0_rows[:, slots, :], x0[u][:], cap0[:, slots, :], ALU.min)
-            rest.append(costs(f"rest1{1 + u}", 1, [(1 + u, 2)], 1 + u))
+            nc.sync.dma_start(cap0[t][:], cap_rows[0][:, t, :])
         cap1 = tile("cap1", [P, PACK, PICKS], F32)
         nc.sync.dma_start(cap1[:], cap_rows[1])
-        nc.scalar.copy(word_order(z0[:]), row_order(z0_rows[:]))
-        rest.append(costs("rest13", 1, [(3, 2)], 3, "tab0"))
-        for t in range(1, PACK):
-            if t == PACK - 1:
-                quantize(z_codes[0][:], z_plane[0][:], z0[:].rearrange("p n t -> p (n t)"))
-            put(1, t, parts[2], rest[t][:])
+        z0_rows = tile("z0_rows", [P, PACK, PICKS], BF16)
+        weighted = {}
+
+        def weigh(k):
+            weighted[k] = tile(f"weighted{k}", [P, 2 * PIECE], F32, f"rest{k - 1}")
+            nc.gpsimd.tensor_tensor(weighted[k][:], rest[k][:], wgs_sb[:, k % PACK, late], ALU.mult)
+
+        def place(k):
+            nc.vector.tensor_copy(pages[k][:].indirect(idx2[:, entries(late)]), weighted[k][:])
+
+        def pick(k, dst):
+            nc.vector.tensor_copy(dst, pages[k][:].indirect(idx3[:]))
+
+        def compare(t, x, gap, take):
+            nc.gpsimd.tensor_tensor(gap, x, cap0[t][:], ALU.subtract)
+            nc.scalar.activation(gap, gap, ACT.Sign)
+            nc.scalar.activation(take, gap, ACT.Copy, scale=-0.5, bias=0.5)
+            nc.scalar.activation(gap, gap, ACT.Copy, scale=0.5, bias=0.5)
+
+        def keep_x(x, take):
+            nc.gpsimd.tensor_tensor(x, x, take, ALU.mult)
+
+        def keep_cap(t, gap):
+            nc.gpsimd.tensor_tensor(gap, gap, cap0[t][:], ALU.mult)
+
+        def join(t, x, gap):
+            nc.gpsimd.tensor_tensor(z0_rows[:, t, :], x, gap, ALU.add)
+
+        put(0, 0, late, rest[0][:])
+        weigh(1)
+        x0 = tile("x0", [P, PICKS], F32)[:]
+        pick(0, x0)
+        weigh(2)
+        place(1)
+        on_page0 = tile("on_page0", [P, 2, PICKS], F32, "page0")
+        x1, gap0 = on_page0[:, 0, :], on_page0[:, 1, :]
+        take0 = tile("take0", [P, PICKS], F32)[:]
+        compare(0, x0, gap0, take0)
+        weigh(3)
+        pick(1, x1)
+        weigh(4)
+        place(2)
+        on_page1 = tile("on_page1", [P, 2, PICKS], F32, "page1")
+        gap1, take1 = on_page1[:, 0, :], on_page1[:, 1, :]
+        compare(1, x1, gap1, take1)
+        x2 = tile("x2", [P, PICKS], F32)[:]
+        pick(2, x2)
+        keep_x(x0, take0)
+        keep_cap(0, gap0)
+        place(3)
+        place(4)
+        gap2 = tile("gap2", [P, PICKS], F32)[:]
+        take2 = tile("take2", [P, PICKS], F32, "v0_256")[:]
+        compare(2, x2, gap2, take2)
+        weigh(5)
+        join(0, x0, gap0)
+        x_upper = tile("x_upper", [P, PACK, PICKS], F32)
+        pick(4, x_upper[:, 0, :])
+        keep_x(x1, take1)
+        place(5)
+        weigh(6)
+        keep_cap(1, gap1)
+        pick(5, x_upper[:, 1, :])
+        place(6)
+        weigh(7)
+        join(1, x1, gap1)
+        pick(6, x_upper[:, 2, :])
+        place(7)
+        keep_x(x2, take2)
+        pick(7, x_upper[:, 3, :])
+        keep_cap(2, gap2)
+        x3 = tile("x3", [P, PICKS], F32)[:]
+        pick(3, x3)
+        join(2, x2, gap2)
+
+        def limit_row(span):
+            nc.vector.tensor_tensor(z0_rows[:, 3, span], x3[:, span], cap0[3][:, span], ALU.min)
+
+        limit_row(cols(0))
 
         out_rows = out.rearrange("(c p) m -> p c m", p=P)
-        last = PIECES - 1
-        spans = [cols(j) for j in range(last)] + [slice(768, 896), slice(896, 1024)]
+        spans = [cols(0), cols(1), cols(2), slice(768, 896), slice(896, 1024)]
 
-        def score_pass(a, banks, span):
-            share = 4 // len(banks)
-            for c in range(4):
-                nc.tensor.matmul_mx(
-                    out=banks[c // share][:, c % share, :],
-                    lhsT=w3_codes[:, a, 128 * c : 128 * c + 128].bitcast(FP8X4),
-                    lhsT_scale=w3_plane[:, a, 128 * c : 128 * c + 128],
-                    rhs=z_codes[a][:, span].bitcast(FP8X4),
-                    rhs_scale=z_plane[a][:, span],
-                    start=(a == 0 and c % share == 0),
-                    stop=(a == 1 and c % share == share - 1),
-                )
+        def weave(grouped, span):
+            nc.scalar.copy(word_order(grouped), row_order(z0_rows[:, :, span]))
 
-        def open_scores(n):
+        def limit(grouped, span):
+            nc.vector.tensor_tensor(word_order(grouped), row_order(x_upper[:, :, span]), row_order(cap1[:, :, span]), ALU.min)
+
+        def score(dst, c, a, codes, plane, start, stop):
+            nc.tensor.matmul_mx(
+                out=dst,
+                lhsT=w3_codes[:, a, 128 * c : 128 * c + 128].bitcast(FP8X4),
+                lhsT_scale=w3_plane[:, a, 128 * c : 128 * c + 128],
+                rhs=codes.bitcast(FP8X4),
+                rhs_scale=plane,
+                start=start,
+                stop=stop,
+            )
+
+        def store(n, pair, acc):
             span = spans[n]
-            if n == PIECES:
-                banks = [bank(c, [P, 1, HALF]) for c in range(4)]
+            staged = tile(f"staged{n}{pair}", [P, 2, span.stop - span.start], F32)
+            if n >= 2 and pair == 1:
+                nc.vector.tensor_copy(staged[:], acc[:])
             else:
-                banks = [bank(2 * min(n, last - 1) + c, [P, 2, span.stop - span.start]) for c in range(2)]
-            score_pass(0, banks, span)
-            return banks
+                nc.scalar.copy(staged[:], acc[:])
+            nc.sync.dma_start(out_rows[:, 2 * pair : 2 * pair + 2, span], staged[:])
+
+        def group(n):
+            grouped = tile(f"z_{n}", [P, 2, PIECE, PACK], BF16)
+            weave(grouped[:, 0, :, :], spans[n])
+            limit(grouped[:, 1, :, :], spans[n])
+            return grouped
 
         def finish(n, grouped):
-            span = spans[n]
-            quantize(z_codes[1][:, span], z_plane[1][:, span], grouped.rearrange("p n t -> p (n t)"))
-            score_pass(1, opened[n], span)
+            codes = tile(f"z_codes{n}", [P, 2 * PIECE], U32)
+            plane = tile(f"z_plane{n}", [P, 2 * PIECE], U8)
+            quantize(codes[:], plane[:], grouped[:].rearrange("p a n t -> p (a n t)"))
+            for pair in range(2):
+                acc = bank(2 * n + pair, [P, 2, PIECE])
+                for u in range(2):
+                    for a in range(2):
+                        score(acc[:, u, :], 2 * pair + u, a, codes[:, cols(a)], plane[:, cols(a)], a == 0, a == 1)
+                store(n, pair, acc)
 
-        def store(n, pairs=(0, 1)):
-            span = spans[n]
-            for pair in pairs:
-                staged = tile(f"staged{n}{pair}", [P, 2, span.stop - span.start], F32)
-                nc.scalar.copy(staged[:], opened[n][pair][:])
-                nc.sync.dma_start(out_rows[:, 2 * pair : 2 * pair + 2, span], staged[:])
-
-        opened = {n: open_scores(n) for n in range(last)}
-
-        def fetch(name, span, slots, after):
-            picked = tile(name, [P, len(slots), span.stop - span.start], F32, after)
-            for u, t in enumerate(slots):
-                nc.vector.tensor_copy(picked[:, u, :], pages[PACK + t][:].indirect(idx3[:, entries(span)]))
-            return picked
-
-        lower = fetch("x1_lower", cols(0, 1), (0, 1), "v0_256")
-        upper = fetch("x1_upper", cols(0, 1), (2, 3), "tab0")
-
-        def pairs_of(j):
-            return [lower[:, :, cols(j)], upper[:, :, cols(j)]]
-
-        def limit(j, pairs):
-            rows = tile(f"z1_rows{j}", [P, PACK * (1 + j), PIECE], BF16)[:, 0:PACK, :]
-            for u in range(2):
-                slots = slice(2 * u, 2 * u + 2)
-                nc.vector.tensor_tensor(rows[:, slots, :], pairs[u], cap1[:, slots, cols(j)], ALU.min)
-            grouped = tile(f"z1_{j}", [P, PIECE, PACK], BF16)
-            nc.scalar.copy(word_order(grouped[:]), row_order(rows))
-            return grouped
-
-        def limit_grouped(n, picked, after=None):
-            span = spans[n]
-            grouped = tile(f"z1_{n}", [P, span.stop - span.start, PACK], BF16, after)
-            nc.vector.tensor_tensor(word_order(grouped[:]), row_order(picked[:]), row_order(cap1[:, :, span]), ALU.min)
-            return grouped
-
-        every = (0, 1, 2, 3)
-        first = limit(0, pairs_of(0))
-        grouped = limit(1, pairs_of(1))
-        finish(0, first[:])
-        store(0)
-        picked = fetch("x1_2", spans[2], every, "v0_256")
-        finish(1, grouped[:])
-        store(1)
-        opened[PIECES] = open_scores(PIECES)
-        finish(2, limit_grouped(2, picked)[:])
-        store(2)
-        opened[last] = open_scores(last)
-        first_half = fetch("x1_3", spans[3], every, "z1_1")
-        finish(3, limit_grouped(3, first_half)[:])
-        second_half = fetch("x1_4", spans[4], every, "v0_256")
-        finish(4, limit_grouped(4, second_half)[:])
-        store(3)
+        first = group(0)
+        limit_row(cols(1, 3))
+        second = group(1)
+        third = tile("z_2", [P, 2, PIECE, PACK], BF16)
+        weave(third[:, 0, :, :], spans[2])
+        z0_last = tile("z0_last", [P, PIECE, PACK], BF16)
+        weave(z0_last[:], cols(3))
+        finish(0, first)
+        limit(third[:, 1, :, :], spans[2])
+        finish(1, second)
+        last_codes = tile("last_codes", [P, 2, PIECE], U32)
+        last_plane = tile("last_plane", [P, 2, PIECE], U8)
+        z_3 = tile("z_3", [P, HALF, PACK], BF16)
+        limit(z_3[:], spans[3])
+        finish(2, third)
+        quantize(last_codes[:, 0, :], last_plane[:, 0, :], z0_last[:].rearrange("p n t -> p (n t)"))
+        banks3 = [bank(6 + pair, [P, 2, HALF]) for pair in range(2)]
+        banks4 = [bank(c, [P, HALF]) for c in range(4)]
+        for c in range(4):
+            score(banks3[c // 2][:, c % 2, :], c, 0, last_codes[:, 0, halves[0]], last_plane[:, 0, halves[0]], c % 2 == 0, False)
+        for c in range(4):
+            score(banks4[c][:], c, 0, last_codes[:, 0, halves[1]], last_plane[:, 0, halves[1]], True, False)
+        z_4 = tile("z_4", [P, HALF, PACK], BF16)
+        limit(z_4[:], spans[4])
+        quantize(last_codes[:, 1, halves[0]], last_plane[:, 1, halves[0]], z_3[:].rearrange("p n t -> p (n t)"))
+        for c in range(4):
+            score(banks3[c // 2][:, c % 2, :], c, 1, last_codes[:, 1, halves[0]], last_plane[:, 1, halves[0]], False, c % 2 == 1)
+        quantize(last_codes[:, 1, halves[1]], last_plane[:, 1, halves[1]], z_4[:].rearrange("p n t -> p (n t)"))
+        for c in range(4):
+            score(banks4[c][:], c, 1, last_codes[:, 1, halves[1]], last_plane[:, 1, halves[1]], False, True)
+        for pair in range(2):
+            store(3, pair, banks3[pair])
         for pair in range(2):
             staged = tile(f"staged4{pair}", [P, 2, HALF], F32)
-            nc.vector.tensor_copy(staged[:, 0, :], opened[PIECES][2 * pair][:, 0, :])
-            nc.scalar.copy(staged[:, 1, :], opened[PIECES][2 * pair + 1][:, 0, :])
-            nc.sync.dma_start(out_rows[:, 2 * pair : 2 * pair + 2, spans[PIECES]], staged[:])
+            nc.vector.tensor_copy(staged[:, 0, :], banks4[2 * pair][:])
+            nc.scalar.copy(staged[:, 1, :], banks4[2 * pair + 1][:])
+            nc.sync.dma_start(out_rows[:, 2 * pair : 2 * pair + 2, spans[4]], staged[:])

@@ -1,6 +1,7 @@
 from contextlib import ExitStack
 
 import concourse.mybir as mybir
+from concourse.masks import make_identity
 
 K, M, H, N, T, S, T2, PICKS = 1024, 512, 1024, 512, 2048, 1024, 2048, 1024
 FLOPS = 2 * (K * M * S + M * H * S + H * N * PICKS)
@@ -34,10 +35,8 @@ PLACES = {
     "w2_early": 24576,
     "w1_raw": 24576,
     "page2": 32768,
-    "tab1": 40960,
-    "w2_codes1": 40960,
-    "w1_plane_raw": 116736,
-    "page3": 116736,
+    "w1_plane_raw": 40960,
+    "page3": 40960,
     "page4": 49152,
     "w2_front1": 56320,
     "w2_back": 57344,
@@ -46,28 +45,29 @@ PLACES = {
     "page5": 57344,
     "page6": 73728,
     "page7": 65536,
-    "cap1": 81920,
-    "x0": 16384,
-    "gap2": 20480,
-    "z_0": 20480,
-    "z_3": 20480,
-    "x2": 24576,
-    "z_1": 24576,
-    "z_4": 24576,
-    "take0": 28672,
+    "e_grouped2": 16384,
+    "both2": 16384,
+    "cost13": 24576,
+    "both1": 24576,
+    "both0": 81920,
+    "cost15": 90112,
+    "both3": 90112,
+    "rest1": 98304,
+    "weighted2": 98304,
+    "cap1": 98304,
     "x_upper": 32768,
-    "cost12": 98304,
-    "cap0_0": 98304,
-    "cost13": 102400,
-    "cap0_1": 102400,
-    "cost15": 106496,
-    "cap0_2": 106496,
-    "x3": 106496,
-    "z_2": 106496,
-    "cost14": 110592,
-    "e_codes2": 110592,
-    "cap0_3": 112640,
-    "cost05": 112640,
+    "z0_0": 61440,
+    "z1_0": 73728,
+    "z1_1": 75776,
+    "z1_2": 77824,
+    "z1_3": 79872,
+    "z1_4": 80896,
+    "staged00": 49152,
+    "staged01": 51200,
+    "staged10": 53248,
+    "staged11": 55296,
+    "staged20": 57344,
+    "staged21": 59392,
 }
 
 
@@ -86,8 +86,8 @@ def tile_list_spill_slot_advisor_kernel(
                 return placed.tile(shape, dtype, name=name, align_bytes=64, offset=PLACES[name])
             return sb.tile(shape, dtype, name=name, tag=after or name, align_bytes=64)
 
-        def bank(n, shape):
-            return psum.tile(shape, F32, name=f"bank{n}", tag=f"bank{n}")
+        def bank(n, shape, dtype=F32):
+            return psum.tile(shape, dtype, name=f"bank{n}", tag=f"bank{n}")
 
         def cols(first, last=None):
             return slice(first * PIECE, ((first if last is None else last) + 1) * PIECE)
@@ -341,180 +341,178 @@ def tile_list_spill_slot_advisor_kernel(
         th = tile("th2", [P, PACK, 2 * PIECE], F32)
         squash(2, th, (0, 1, 0, 1), 1)
         features(2, th, "cost10", "cost14")
-        h = tile("cost16", [P, 3 * PIECE], F32, "cost10")
-        fill(h[:, cols(0)], 1, [(2, 1)], 3)
-        fill(h[:, cols(1, 2)], 1, [(3, 0), (3, 1)], 2)
-        put(1, 2, parts[1], h[:, cols(0)])
-        put(1, 3, cols(0, 1), h[:, cols(1, 2)])
+        put(1, 2, parts[1], costs("cost16", 1, [(2, 1)], 3, "cost10")[:])
 
         late = parts[2]
-        rest = [costs(f"rest{k}", k // PACK, [(k % PACK, 2)], (4 + k) % 8) for k in range(2 * PACK)]
         cap_rows = cap.rearrange("(a p t) m -> a p t m", a=2, t=PACK)
-        cap0 = [tile(f"cap0_{t}", [P, PICKS], F32) for t in range(PACK)]
+        both = [tile(f"both{t}", [P, 2, PICKS], F32) for t in range(PACK)]
         for t in range(PACK):
-            nc.sync.dma_start(cap0[t][:], cap_rows[0][:, t, :])
-        cap1 = tile("cap1", [P, PACK, PICKS], F32)
-        nc.sync.dma_start(cap1[:], cap_rows[1])
+            nc.sync.dma_start(both[t][:, 1, :], cap_rows[0][:, t, :])
+
+        def negate(t):
+            nc.scalar.activation(both[t][:, 1, :], both[t][:, 1, :], ACT.Copy, scale=-1.0)
+
+        runs = [[0], [1], [2], [3], [4, 5, 6]]
+        rest = [tile(f"rest{n}", [P, len(run), 2 * PIECE], F32) for n, run in enumerate(runs)]
+        for n, run in enumerate(runs):
+            for u, k in enumerate(run):
+                fill(rest[n][:, u, :], k // PACK, [(k % PACK, 2)], (4 + k) % 8)
+            if n == 1:
+                negate(0)
+        early = costs("early", 1, [(3, 0), (3, 1)], 2)
+        ident = tile("ident", [P, P], F32, "cost10")
+        make_identity(nc, ident[:])
+        ident_bf = tile("ident_bf", [P, P], BF16)
+        nc.scalar.copy(ident_bf[:], ident[:])
         z0_rows = tile("z0_rows", [P, PACK, PICKS], BF16)
         weighted = {}
+        shares = {}
 
-        def weigh(k):
-            weighted[k] = tile(f"weighted{k}", [P, 2 * PIECE], F32, f"rest{k - 1}")
-            nc.gpsimd.tensor_tensor(weighted[k][:], rest[k][:], wgs_sb[:, k % PACK, late], ALU.mult)
+        def weigh(n):
+            run = runs[n]
+            products = tile(f"weighted{n}", [P, len(run), 2 * PIECE], F32, f"rest{n - 1}")
+            nc.gpsimd.tensor_tensor(products[:], rest[n][:], wgs_sb[:, run[0] % PACK : run[-1] % PACK + 1, late], ALU.mult)
+            for u, k in enumerate(run):
+                weighted[k] = products[:, u, :]
 
         def place(k):
-            nc.vector.tensor_copy(pages[k][:].indirect(idx2[:, entries(late)]), weighted[k][:])
+            span = late if k < 2 * PACK - 1 else cols(0, 1)
+            nc.vector.tensor_copy(pages[k][:].indirect(idx2[:, entries(span)]), weighted[k])
 
-        def pick(k, dst):
-            nc.vector.tensor_copy(dst, pages[k][:].indirect(idx3[:]))
+        def add_turned(t, half, number):
+            acc = bank(number, [P, 4, P])
+            for j in range(4):
+                block = slice(P * (4 * half + j), P * (4 * half + j + 1))
+                for side in (1, 0):
+                    nc.tensor.matmul(acc[:, j, :], both[t][:, side, block], ident[:], start=side == 1, stop=side == 0, is_transpose=True)
+            return acc
 
-        def compare(t, x, gap, take):
-            nc.gpsimd.tensor_tensor(gap, x, cap0[t][:], ALU.subtract)
-            nc.scalar.activation(gap, gap, ACT.Sign)
-            nc.scalar.activation(take, gap, ACT.Copy, scale=-0.5, bias=0.5)
-            nc.scalar.activation(gap, gap, ACT.Copy, scale=0.5, bias=0.5)
+        def compare(t):
+            nc.vector.tensor_copy(both[t][:, 0, :], pages[t][:].indirect(idx3[:]))
+            signs = tile(f"signs{t}", [P, 8, P], BF16, f"signs{t % 2}")
+            shares[t] = tile(f"shares{t}", [P, 2, PICKS], F32, f"page{t % 2}")
+            for half in range(2):
+                nc.scalar.activation(signs[:, 4 * half : 4 * half + 4, :], add_turned(t, half, (2 * t + half) % 3)[:], ACT.Sign)
+            for half in range(2):
+                back = bank(3 if half else (2 * t + 2) % 3, [P, 4 * P], BF16)
+                for j in range(4):
+                    nc.tensor.transpose(back[:, P * j : P * (j + 1)], signs[:, 4 * half + j, :], ident_bf[:])
+                span = cols(2 * half, 2 * half + 1)
+                nc.scalar.activation(shares[t][:, 0, span], back[:], ACT.Copy, scale=-0.5, bias=0.5)
+                nc.scalar.activation(shares[t][:, 1, span], back[:], ACT.Copy, scale=-0.5, bias=-0.5)
 
-        def keep_x(x, take):
-            nc.gpsimd.tensor_tensor(x, x, take, ALU.mult)
+        def choose(t):
+            nc.gpsimd.tensor_tensor(both[t][:], both[t][:], shares[t][:], ALU.mult)
 
-        def keep_cap(t, gap):
-            nc.gpsimd.tensor_tensor(gap, gap, cap0[t][:], ALU.mult)
+        def join(t, span):
+            nc.gpsimd.tensor_tensor(z0_rows[:, t, span], both[t][:, 0, span], both[t][:, 1, span], ALU.add)
 
-        def join(t, x, gap):
-            nc.gpsimd.tensor_tensor(z0_rows[:, t, :], x, gap, ALU.add)
+        def join_turned(t):
+            turned = tile(f"turned{t}", [P, 8, P], BF16)
+            for half in range(2):
+                nc.scalar.copy(turned[:, 4 * half : 4 * half + 4, :], add_turned(t, half, 2 * (t - 1) + half)[:])
+            back = bank(3 + t, [P, PICKS], BF16)
+            for j in range(8):
+                nc.tensor.transpose(back[:, P * j : P * (j + 1)], turned[:, j, :], ident_bf[:])
+            nc.scalar.copy(z0_rows[:, t, :], back[:])
 
-        put(0, 0, late, rest[0][:])
-        weigh(1)
-        x0 = tile("x0", [P, PICKS], F32)[:]
-        pick(0, x0)
-        weigh(2)
-        place(1)
-        on_page0 = tile("on_page0", [P, 2, PICKS], F32, "page0")
-        x1, gap0 = on_page0[:, 0, :], on_page0[:, 1, :]
-        take0 = tile("take0", [P, PICKS], F32)[:]
-        compare(0, x0, gap0, take0)
-        weigh(3)
-        pick(1, x1)
-        weigh(4)
-        place(2)
-        on_page1 = tile("on_page1", [P, 2, PICKS], F32, "page1")
-        gap1, take1 = on_page1[:, 0, :], on_page1[:, 1, :]
-        compare(1, x1, gap1, take1)
-        x2 = tile("x2", [P, PICKS], F32)[:]
-        pick(2, x2)
-        keep_x(x0, take0)
-        keep_cap(0, gap0)
-        place(3)
-        place(4)
-        gap2 = tile("gap2", [P, PICKS], F32)[:]
-        take2 = tile("take2", [P, PICKS], F32, "v0_256")[:]
-        compare(2, x2, gap2, take2)
-        weigh(5)
-        join(0, x0, gap0)
+        put(0, 0, late, rest[0][:, 0, :])
+        for n in range(1, len(runs)):
+            weigh(n)
+        weighted[2 * PACK - 1] = tile("weighted_early", [P, 2 * PIECE], F32, "rest4")[:]
+        nc.gpsimd.tensor_tensor(weighted[2 * PACK - 1], early[:], wgs_sb[:, PACK - 1, cols(0, 1)], ALU.mult)
+        compare(0)
+        for t in range(1, PACK):
+            negate(t)
+            place(t)
+            compare(t)
+            choose(t - 1)
+            if t == 2:
+                join(0, cols(0, 3))
+        cap1 = tile("cap1", [P, PACK, PICKS], F32)
+        nc.sync.dma_start(cap1[:], cap_rows[1])
         x_upper = tile("x_upper", [P, PACK, PICKS], F32)
-        pick(4, x_upper[:, 0, :])
-        keep_x(x1, take1)
-        place(5)
-        weigh(6)
-        keep_cap(1, gap1)
-        pick(5, x_upper[:, 1, :])
-        place(6)
-        weigh(7)
-        join(1, x1, gap1)
-        pick(6, x_upper[:, 2, :])
-        place(7)
-        keep_x(x2, take2)
-        pick(7, x_upper[:, 3, :])
-        keep_cap(2, gap2)
-        x3 = tile("x3", [P, PICKS], F32)[:]
-        pick(3, x3)
-        join(2, x2, gap2)
+        for k in range(PACK, 2 * PACK - 1):
+            place(k)
+            nc.vector.tensor_copy(x_upper[:, k - PACK, :], pages[k][:].indirect(idx3[:]))
+        place(2 * PACK - 1)
+        join_turned(1)
+        join_turned(2)
+        choose(3)
+        join(3, cols(0, 1))
+        join(3, cols(2, 3))
 
-        def limit_row(span):
-            nc.vector.tensor_tensor(z0_rows[:, 3, span], x3[:, span], cap0[3][:, span], ALU.min)
-
-        limit_row(cols(0))
-
+        z0 = [tile(f"z0_{half}", [P, 2 * PIECE, PACK], BF16) for half in range(2)]
+        for n in range(PIECES):
+            nc.scalar.copy(word_order(z0[n // 2][:, cols(n % 2), :]), row_order(z0_rows[:, :, cols(n)]))
         out_rows = out.rearrange("(c p) m -> p c m", p=P)
-        spans = [cols(0), cols(1), cols(2), slice(768, 896), slice(896, 1024)]
+        last = PIECES - 1
+        spans = [cols(j) for j in range(last)] + [slice(768, 896), slice(896, 1024)]
+        score_banks = [(0, 1), (2, 3), (4, 5), (6, 7), (0, 1)]
+        z_plane = [tile(f"z_plane{a}", [P, PICKS], U8) for a in range(2)]
+        z_codes = {}
+        opened = {}
 
-        def weave(grouped, span):
-            nc.scalar.copy(word_order(grouped), row_order(z0_rows[:, :, span]))
+        def quantize_z(a, pieces, grouped, after=None):
+            span = slice(spans[pieces[0]].start, spans[pieces[-1]].stop)
+            codes = tile(f"z_codes{a}{pieces[0]}", [P, span.stop - span.start], U32, after)
+            quantize(codes[:], z_plane[a][:, span], grouped.rearrange("p n t -> p (n t)"))
+            for n in pieces:
+                z_codes[a, n] = codes[:, spans[n].start - span.start : spans[n].stop - span.start]
 
-        def limit(grouped, span):
-            nc.vector.tensor_tensor(word_order(grouped), row_order(x_upper[:, :, span]), row_order(cap1[:, :, span]), ALU.min)
-
-        def score(dst, c, a, codes, plane, start, stop):
-            nc.tensor.matmul_mx(
-                out=dst,
-                lhsT=w3_codes[:, a, 128 * c : 128 * c + 128].bitcast(FP8X4),
-                lhsT_scale=w3_plane[:, a, 128 * c : 128 * c + 128],
-                rhs=codes.bitcast(FP8X4),
-                rhs_scale=plane,
-                start=start,
-                stop=stop,
-            )
-
-        def store(n, pair, acc):
+        def score_pass(a, n):
             span = spans[n]
-            staged = tile(f"staged{n}{pair}", [P, 2, span.stop - span.start], F32)
-            if n >= 2 and pair == 1:
-                nc.vector.tensor_copy(staged[:], acc[:])
-            else:
-                nc.scalar.copy(staged[:], acc[:])
-            nc.sync.dma_start(out_rows[:, 2 * pair : 2 * pair + 2, span], staged[:])
-
-        def group(n):
-            grouped = tile(f"z_{n}", [P, 2, PIECE, PACK], BF16)
-            weave(grouped[:, 0, :, :], spans[n])
-            limit(grouped[:, 1, :, :], spans[n])
-            return grouped
+            share = 4 // len(score_banks[n])
+            if a == 0:
+                opened[n] = [bank(number, [P, share, span.stop - span.start]) for number in score_banks[n]]
+            for c in range(4):
+                nc.tensor.matmul_mx(
+                    out=opened[n][c // share][:, c % share, :],
+                    lhsT=w3_codes[:, a, 128 * c : 128 * c + 128].bitcast(FP8X4),
+                    lhsT_scale=w3_plane[:, a, 128 * c : 128 * c + 128],
+                    rhs=z_codes[a, n].bitcast(FP8X4),
+                    rhs_scale=z_plane[a][:, span],
+                    start=(a == 0 and c % share == 0),
+                    stop=(a == 1 and c % share == share - 1),
+                )
 
         def finish(n, grouped):
-            codes = tile(f"z_codes{n}", [P, 2 * PIECE], U32)
-            plane = tile(f"z_plane{n}", [P, 2 * PIECE], U8)
-            quantize(codes[:], plane[:], grouped[:].rearrange("p a n t -> p (a n t)"))
-            for pair in range(2):
-                acc = bank(2 * n + pair, [P, 2, PIECE])
-                for u in range(2):
-                    for a in range(2):
-                        score(acc[:, u, :], 2 * pair + u, a, codes[:, cols(a)], plane[:, cols(a)], a == 0, a == 1)
-                store(n, pair, acc)
+            quantize_z(1, [n], grouped[:])
+            score_pass(1, n)
 
-        first = group(0)
-        limit_row(cols(1, 3))
-        second = group(1)
-        third = tile("z_2", [P, 2, PIECE, PACK], BF16)
-        weave(third[:, 0, :, :], spans[2])
-        z0_last = tile("z0_last", [P, PIECE, PACK], BF16)
-        weave(z0_last[:], cols(3))
-        finish(0, first)
-        limit(third[:, 1, :, :], spans[2])
-        finish(1, second)
-        last_codes = tile("last_codes", [P, 2, PIECE], U32)
-        last_plane = tile("last_plane", [P, 2, PIECE], U8)
-        z_3 = tile("z_3", [P, HALF, PACK], BF16)
-        limit(z_3[:], spans[3])
-        finish(2, third)
-        quantize(last_codes[:, 0, :], last_plane[:, 0, :], z0_last[:].rearrange("p n t -> p (n t)"))
-        banks3 = [bank(6 + pair, [P, 2, HALF]) for pair in range(2)]
-        banks4 = [bank(c, [P, HALF]) for c in range(4)]
-        for c in range(4):
-            score(banks3[c // 2][:, c % 2, :], c, 0, last_codes[:, 0, halves[0]], last_plane[:, 0, halves[0]], c % 2 == 0, False)
-        for c in range(4):
-            score(banks4[c][:], c, 0, last_codes[:, 0, halves[1]], last_plane[:, 0, halves[1]], True, False)
-        z_4 = tile("z_4", [P, HALF, PACK], BF16)
-        limit(z_4[:], spans[4])
-        quantize(last_codes[:, 1, halves[0]], last_plane[:, 1, halves[0]], z_3[:].rearrange("p n t -> p (n t)"))
-        for c in range(4):
-            score(banks3[c // 2][:, c % 2, :], c, 1, last_codes[:, 1, halves[0]], last_plane[:, 1, halves[0]], False, c % 2 == 1)
-        quantize(last_codes[:, 1, halves[1]], last_plane[:, 1, halves[1]], z_4[:].rearrange("p n t -> p (n t)"))
-        for c in range(4):
-            score(banks4[c][:], c, 1, last_codes[:, 1, halves[1]], last_plane[:, 1, halves[1]], False, True)
-        for pair in range(2):
-            store(3, pair, banks3[pair])
-        for pair in range(2):
-            staged = tile(f"staged4{pair}", [P, 2, HALF], F32)
-            nc.vector.tensor_copy(staged[:, 0, :], banks4[2 * pair][:])
-            nc.scalar.copy(staged[:, 1, :], banks4[2 * pair + 1][:])
-            nc.sync.dma_start(out_rows[:, 2 * pair : 2 * pair + 2, spans[4]], staged[:])
+        def store(n, move):
+            span = spans[n]
+            for pair in range(2):
+                staged = tile(f"staged{n}{pair}", [P, 2, span.stop - span.start], F32)
+                move(staged[:], opened[n][pair][:])
+                nc.sync.dma_start(out_rows[:, 2 * pair : 2 * pair + 2, span], staged[:])
+
+        def limit(n):
+            span = spans[n]
+            grouped = tile(f"z1_{n}", [P, span.stop - span.start, PACK], BF16)
+            nc.vector.tensor_tensor(word_order(grouped[:]), row_order(x_upper[:, :, span]), row_order(cap1[:, :, span]), ALU.min)
+            return grouped
+
+        def fetch(n):
+            nc.vector.tensor_copy(x_upper[:, PACK - 1, cols(n)], pages[2 * PACK - 1][:].indirect(idx3[:, entries(cols(n))]))
+
+        quantize_z(0, [0, 1], z0[0][:])
+        put(1, 3, late, costs("closing", 1, [(3, 2)], 7, "z0_rows")[:])
+        score_pass(0, 0)
+        score_pass(0, 1)
+        fetch(0)
+        quantize_z(0, [2, 3, 4], z0[1][:], "z0_rows")
+        score_pass(0, 2)
+        score_pass(0, 3)
+        for n in range(last):
+            grouped = limit(n)
+            fetch(n + 1)
+            finish(n, grouped)
+            store(n, nc.scalar.copy)
+            if n == 0:
+                score_pass(0, 4)
+        halves_grouped = [limit(3), limit(4)]
+        finish(3, halves_grouped[0])
+        finish(4, halves_grouped[1])
+        store(3, nc.scalar.copy)
+        store(4, nc.vector.tensor_copy)

@@ -1,7 +1,6 @@
 from contextlib import ExitStack
 
 import concourse.mybir as mybir
-from concourse.masks import make_identity
 
 K, M, H, N, T, S, T2, PICKS = 1024, 512, 1024, 512, 2048, 1024, 2048, 1024
 FLOPS = 2 * (K * M * S + M * H * S + H * N * PICKS)
@@ -343,6 +342,14 @@ def tile_list_spill_slot_advisor_kernel(
         features(2, th, "cost10", "cost14")
         put(1, 2, parts[1], costs("cost16", 1, [(2, 1)], 3, "cost10")[:])
 
+        distance = tile("distance", [P, P], F32, "cost12")
+        nc.gpsimd.iota(distance[:], [[1, P]], base=0, channel_multiplier=-1, allow_small_or_imprecise_dtypes=True)
+        nc.scalar.activation(distance[:], distance[:], ACT.Abs)
+        ident = tile("ident", [P, P], F32)
+        ident_bf = tile("ident_bf", [P, P], BF16)
+        for unit in (ident, ident_bf):
+            nc.scalar.activation(unit[:], distance[:], ACT.Relu, scale=-1.0, bias=1.0)
+
         late = parts[2]
         cap_rows = cap.rearrange("(a p t) m -> a p t m", a=2, t=PACK)
         both = [tile(f"both{t}", [P, 2, PICKS], F32) for t in range(PACK)]
@@ -360,11 +367,7 @@ def tile_list_spill_slot_advisor_kernel(
             if n == 1:
                 negate(0)
         early = costs("early", 1, [(3, 0), (3, 1)], 2)
-        ident = tile("ident", [P, P], F32, "cost10")
-        make_identity(nc, ident[:])
-        ident_bf = tile("ident_bf", [P, P], BF16)
-        nc.scalar.copy(ident_bf[:], ident[:])
-        z0_rows = tile("z0_rows", [P, PACK, PICKS], BF16)
+        z0_rows = [tile(f"z0_rows{half}", [P, PACK, 2 * PIECE], BF16) for half in range(2)]
         weighted = {}
         shares = {}
 
@@ -404,8 +407,10 @@ def tile_list_spill_slot_advisor_kernel(
         def choose(t):
             nc.gpsimd.tensor_tensor(both[t][:], both[t][:], shares[t][:], ALU.mult)
 
-        def join(t, span):
-            nc.gpsimd.tensor_tensor(z0_rows[:, t, span], both[t][:, 0, span], both[t][:, 1, span], ALU.add)
+        def join(t):
+            for half in range(2):
+                span = cols(2 * half, 2 * half + 1)
+                nc.gpsimd.tensor_tensor(z0_rows[half][:, t, :], both[t][:, 0, span], both[t][:, 1, span], ALU.add)
 
         def join_turned(t):
             turned = tile(f"turned{t}", [P, 8, P], BF16)
@@ -414,7 +419,8 @@ def tile_list_spill_slot_advisor_kernel(
             back = bank(3 + t, [P, PICKS], BF16)
             for j in range(8):
                 nc.tensor.transpose(back[:, P * j : P * (j + 1)], turned[:, j, :], ident_bf[:])
-            nc.scalar.copy(z0_rows[:, t, :], back[:])
+            for half in range(2):
+                nc.scalar.copy(z0_rows[half][:, t, :], back[:, cols(2 * half, 2 * half + 1)])
 
         put(0, 0, late, rest[0][:, 0, :])
         for n in range(1, len(runs)):
@@ -428,7 +434,7 @@ def tile_list_spill_slot_advisor_kernel(
             compare(t)
             choose(t - 1)
             if t == 2:
-                join(0, cols(0, 3))
+                join(0)
         cap1 = tile("cap1", [P, PACK, PICKS], F32)
         nc.sync.dma_start(cap1[:], cap_rows[1])
         x_upper = tile("x_upper", [P, PACK, PICKS], F32)
@@ -439,12 +445,11 @@ def tile_list_spill_slot_advisor_kernel(
         join_turned(1)
         join_turned(2)
         choose(3)
-        join(3, cols(0, 1))
-        join(3, cols(2, 3))
+        join(3)
 
         z0 = [tile(f"z0_{half}", [P, 2 * PIECE, PACK], BF16) for half in range(2)]
         for n in range(PIECES):
-            nc.scalar.copy(word_order(z0[n // 2][:, cols(n % 2), :]), row_order(z0_rows[:, :, cols(n)]))
+            nc.scalar.copy(word_order(z0[n // 2][:, cols(n % 2), :]), row_order(z0_rows[n // 2][:, :, cols(n % 2)]))
         out_rows = out.rearrange("(c p) m -> p c m", p=P)
         last = PIECES - 1
         spans = [cols(j) for j in range(last)] + [slice(768, 896), slice(896, 1024)]
@@ -497,11 +502,11 @@ def tile_list_spill_slot_advisor_kernel(
             nc.vector.tensor_copy(x_upper[:, PACK - 1, cols(n)], pages[2 * PACK - 1][:].indirect(idx3[:, entries(cols(n))]))
 
         quantize_z(0, [0, 1], z0[0][:])
-        put(1, 3, late, costs("closing", 1, [(3, 2)], 7, "z0_rows")[:])
+        put(1, 3, late, costs("closing", 1, [(3, 2)], 7, "z0_rows0")[:])
         score_pass(0, 0)
         score_pass(0, 1)
         fetch(0)
-        quantize_z(0, [2, 3, 4], z0[1][:], "z0_rows")
+        quantize_z(0, [2, 3, 4], z0[1][:], "z0_rows0")
         score_pass(0, 2)
         score_pass(0, 3)
         for n in range(last):

@@ -453,7 +453,7 @@ def tile_list_spill_slot_advisor_kernel(
         out_rows = out.rearrange("(c p) m -> p c m", p=P)
         last = PIECES - 1
         spans = [cols(j) for j in range(last)] + [slice(768, 896), slice(896, 1024)]
-        score_banks = [(0, 1), (2, 3), (4, 5), (6, 7), (0, 1)]
+        score_banks = [(0, 1), (2, 3), (4, 5), (6, 7), (0, 1, 2, 3)]
         z_plane = [tile(f"z_plane{a}", [P, PICKS], U8) for a in range(2)]
         z_codes = {}
         opened = {}
@@ -485,11 +485,11 @@ def tile_list_spill_slot_advisor_kernel(
             quantize_z(1, [n], grouped[:])
             score_pass(1, n)
 
-        def store(n, move):
+        def store(n):
             span = spans[n]
             for pair in range(2):
                 staged = tile(f"staged{n}{pair}", [P, 2, span.stop - span.start], F32)
-                move(staged[:], opened[n][pair][:])
+                nc.scalar.copy(staged[:], opened[n][pair][:])
                 nc.sync.dma_start(out_rows[:, 2 * pair : 2 * pair + 2, span], staged[:])
 
         def limit(n):
@@ -499,7 +499,7 @@ def tile_list_spill_slot_advisor_kernel(
             return grouped
 
         def fetch(n):
-            nc.vector.tensor_copy(x_upper[:, PACK - 1, cols(n)], pages[2 * PACK - 1][:].indirect(idx3[:, entries(cols(n))]))
+            nc.vector.tensor_copy(x_upper[:, PACK - 1, spans[n]], pages[2 * PACK - 1][:].indirect(idx3[:, entries(spans[n])]))
 
         quantize_z(0, [0, 1], z0[0][:])
         put(1, 3, late, costs("closing", 1, [(3, 2)], 7, "z0_rows0")[:])
@@ -509,15 +509,16 @@ def tile_list_spill_slot_advisor_kernel(
         quantize_z(0, [2, 3, 4], z0[1][:], "z0_rows0")
         score_pass(0, 2)
         score_pass(0, 3)
-        for n in range(last):
+        for n in range(PIECES):
             grouped = limit(n)
             fetch(n + 1)
             finish(n, grouped)
-            store(n, nc.scalar.copy)
-            if n == 0:
-                score_pass(0, 4)
-        halves_grouped = [limit(3), limit(4)]
-        finish(3, halves_grouped[0])
-        finish(4, halves_grouped[1])
-        store(3, nc.scalar.copy)
-        store(4, nc.vector.tensor_copy)
+            store(n)
+            if n == 1:
+                score_pass(0, PIECES)
+        finish(PIECES, limit(PIECES))
+        for pair in range(2):
+            staged = tile(f"staged4{pair}", [P, 2, HALF], F32)
+            nc.vector.tensor_copy(staged[:, 0, :], opened[PIECES][2 * pair][:, 0, :])
+            nc.scalar.copy(staged[:, 1, :], opened[PIECES][2 * pair + 1][:, 0, :])
+            nc.sync.dma_start(out_rows[:, 2 * pair : 2 * pair + 2, spans[PIECES]], staged[:])

@@ -450,6 +450,8 @@ def tile_list_spill_slot_advisor_kernel(
         z0 = [tile(f"z0_{half}", [P, 2 * PIECE, PACK], BF16) for half in range(2)]
         for n in range(PIECES):
             nc.scalar.copy(word_order(z0[n // 2][:, cols(n % 2), :]), row_order(z0_rows[n // 2][:, :, cols(n % 2)]))
+            if n == 1:
+                closing = costs("closing", 1, [(3, 2)], 7, "z0_rows0")
         out_rows = out.rearrange("(c p) m -> p c m", p=P)
         last = PIECES - 1
         spans = [cols(j) for j in range(last)] + [slice(768, 896), slice(896, 1024)]
@@ -502,7 +504,7 @@ def tile_list_spill_slot_advisor_kernel(
             nc.vector.tensor_copy(x_upper[:, PACK - 1, spans[n]], pages[2 * PACK - 1][:].indirect(idx3[:, entries(spans[n])]))
 
         quantize_z(0, [0, 1], z0[0][:])
-        put(1, 3, late, costs("closing", 1, [(3, 2)], 7, "z0_rows0")[:])
+        put(1, 3, late, closing[:])
         score_pass(0, 0)
         score_pass(0, 1)
         fetch(0)

from contextlib import ExitStack

import concourse.mybir as mybir

K, M, H, N, T, S, T2, PICKS = 1024, 512, 1024, 512, 2048, 1024, 2048, 1024
FLOPS = 2 * (K * M * S + M * H * S + H * N * PICKS)

F32 = mybir.dt.float32
BF16 = mybir.dt.bfloat16
I32 = mybir.dt.int32
U32 = mybir.dt.uint32
U16 = mybir.dt.uint16
U8 = mybir.dt.uint8
FP8X4 = mybir.dt.float8_e4m3fn_x4
FP4X4 = mybir.dt.float4_e2m1fn_x4
ACT = mybir.ActivationFunctionType
ALU = mybir.AluOpType

P = 128
PACK = 4
PIECE = 256
PIECES = S // PIECE
LIST_COLS = PIECE // 16
HALF = 128

PLACES = {
    "wgs_sb": 0,
    "tab_plane": 15360,
    "tab0": 73728,
    "w2_late": 74752,
    "cost02": 74752,
    "th1": 81920,
    "th2": 81920,
    "w2_early": 24576,
    "w1_raw": 24576,
    "page2": 32768,
    "w1_plane_raw": 40960,
    "page3": 40960,
    "page4": 49152,
    "w2_front1": 56320,
    "w2_back": 57344,
    "e_grouped1": 65536,
    "cost03": 75776,
    "page5": 57344,
    "page6": 73728,
    "page7": 65536,
    "e_grouped2": 16384,
    "both2": 16384,
    "cost13": 24576,
    "both1": 24576,
    "both0": 81920,
    "cost15": 90112,
    "both3": 90112,
    "rest1": 98304,
    "weighted2": 98304,
    "cap1": 98304,
    "x_upper": 32768,
    "z0_0": 61440,
    "z1_0": 73728,
    "z1_1": 75776,
    "z1_2": 77824,
    "z1_3": 79872,
    "z1_4": 80896,
    "staged00": 49152,
    "staged01": 51200,
    "staged10": 53248,
    "staged11": 55296,
    "staged20": 57344,
    "staged21": 59392,
}


def tile_list_spill_slot_advisor_kernel(
    tc, tab_words, tab_scales, offs, w1_words, w1_scales, b1, gain, w2, wgs, offs2, offs3, cap, w3_words, w3_scales, out
):
    nc = tc.nc
    with ExitStack() as ctx:
        lists = ctx.enter_context(tc.tile_pool(name="lists", bufs=1))
        sb = ctx.enter_context(tc.tile_pool(name="sb", bufs=1))
        placed = ctx.enter_context(tc.tile_pool(name="placed", bufs=1))
        psum = ctx.enter_context(tc.psum_pool(name="psum", bufs=1))

        def tile(name, shape, dtype, after=None):
            if name in PLACES:
                return placed.tile(shape, dtype, name=name, align_bytes=64, offset=PLACES[name])
            return sb.tile(shape, dtype, name=name, tag=after or name, align_bytes=64)

        def bank(n, shape, dtype=F32):
            return psum.tile(shape, dtype, name=f"bank{n}", tag=f"bank{n}")

        def cols(first, last=None):
            return slice(first * PIECE, ((first if last is None else last) + 1) * PIECE)

        def entries(span):
            return slice(span.start // 16, span.stop // 16)

        def word_order(grouped):
            return grouped.rearrange("p (c i) t -> p c t i", i=4)

        def row_order(rows):
            return rows.rearrange("p t (c i) -> p c t i", i=4)

        def quantize(codes, plane, grouped):
            nc.vector.quantize_mx(out=codes.bitcast(FP8X4), scales=plane, in_=grouped)

        pages = []

        def new_page():
            page = tile(f"page{len(pages)}", [P, T2], F32)
            nc.gpsimd.memset(page[:], 0.0)
            pages.append(page)

        def zero_on_vector(words, zero):
            last = words.shape[1] - 1
            nc.vector.memset(words[:, 0:last], zero)
            nc.vector.memset(words[:, last : last + 1], zero)

        def load_scale_rows(plane, scales):
            for q in range(4):
                nc.sync.dma_start(
                    plane[32 * q : 32 * q + 4, :, :].bitcast(I32),
                    scales[:, 4 * q : 4 * q + 4, :].rearrange("a r c -> r a c").bitcast(I32),
                )

        tab_plane = tile("tab_plane", [P, T], U8)
        w1_plane_raw = tile("w1_plane_raw", [P, 2, M], U8)
        shifted = [tile("shifted_first", [P, PIECE], U8), tile("shifted_rest", [P, S - PIECE], U8)]
        nc.gpsimd.memset(tab_plane[:].bitcast(I32), 0)
        pages.append(tile("page0", [P, T2], F32))
        zero_on_vector(pages[0][:], 0.0)
        nc.gpsimd.memset(w1_plane_raw[:].rearrange("p a c -> p (a c)").bitcast(I32), 0)
        for plane in shifted:
            nc.gpsimd.memset(plane[96:128, :].bitcast(I32), 0)
        new_page()
        new_page()

        idx = lists.tile([P, S // 16], U16, name="idx")
        idx2 = lists.tile([P, S // 16], U16, name="idx2")
        idx3 = lists.tile([P, PICKS // 16], U16, name="idx3")
        b1_sb = tile("b1_sb", [P, PACK], F32)
        gain_sb = tile("gain_sb", [P, PACK], F32)
        tab = [tile(f"tab{a}", [P, T], I32) for a in range(2)]
        w1_raw = tile("w1_raw", [P, 2, M // 2], I32)
        w2_rows = w2.rearrange("(p j) r -> p j r", j=PACK)

        nc.sync.dma_start(idx[:], offs)
        scale_rows = tab_scales.rearrange("a (q r) c -> r q a c", r=4)
        for r in range(4):
            nc.sync.dma_start(tab_plane[r:P:16, :].bitcast(I32), scale_rows[r].bitcast(I32))
        nc.sync.dma_start(w1_raw[:], w1_words.rearrange("a p b -> p a b").bitcast(I32))
        nc.sync.dma_start(tab[0][:], tab_words[0].rearrange("p t i -> p (t i)").bitcast(I32))
        load_scale_rows(w1_plane_raw, w1_scales)
        nc.sync.dma_start(tab[1][:], tab_words[1].rearrange("p t i -> p (t i)").bitcast(I32))
        nc.sync.dma_start(b1_sb[:], b1.rearrange("(p t) -> p t", t=PACK))
        nc.sync.dma_start(gain_sb[:], gain.rearrange("(p t) -> p t", t=PACK))
        nc.sync.dma_start(idx2[:], offs2)
        nc.sync.dma_start(idx3[:], offs3)

        def pick_scales(name, span):
            picked = tile(name, [P, span.stop - span.start], U8)
            nc.vector.tensor_copy(picked[:], tab_plane[:].indirect(idx[:, entries(span)]))
            return picked

        def shift(picked, plane):
            nc.sync.dma_start(plane[0:112, :].bitcast(I32), picked[16:P, :].bitcast(I32))

        def pick_words(a, span, after=None):
            codes = tile(f"v{a}_{span.start}", [P, span.stop - span.start], U32, after)
            nc.vector.tensor_copy(codes[:], tab[a][:].bitcast(U32).indirect(idx[:, entries(span)]))
            return codes

        picked_first = pick_scales("picked_first", cols(0))
        shift(picked_first, shifted[0])
        picked_rest = pick_scales("picked_rest", cols(1, PIECES - 1))
        parts = [cols(0), cols(1), cols(2, 3)]
        later = [slice(0, PIECE), slice(PIECE, S - PIECE)]
        v_plane = [
            [picked_first[:]] + [picked_rest[:, span] for span in later],
            [shifted[0][:]] + [shifted[1][:, span] for span in later],
        ]
        w2_early = tile("w2_early", [P, PACK, 512], F32)
        nc.sync.dma_start(w2_early[:], w2_rows[:, :, 0:512])
        shift(picked_rest, shifted[1])
        wgs_rows = wgs.rearrange("(p t) s -> p t s", t=PACK)
        wgs_sb = tile("wgs_sb", [P, PACK, S], F32, "tab_plane")

        def load_weights(slots, span):
            for q in (0, 2, 1, 3):
                nc.sync.dma_start(wgs_sb[32 * q : 32 * q + 32, slots, span], wgs_rows[:, slots, span])

        load_weights(slice(0, 2), cols(0))
        w2_late = tile("w2_late", [P, PACK, 512], F32)
        nc.sync.dma_start(w2_late[:], w2_rows[:, :, 512:1024])
        load_weights(slice(2, PACK), cols(0))
        load_weights(slice(0, PACK), cols(1))
        load_weights(slice(0, PACK), cols(2, PIECES - 1))

        w1_codes = tile("w1_codes", [P, 2, M // 2], I32)
        nc.scalar.copy(
            w1_codes[:].bitcast(U16).rearrange("p a (t m) -> p a t m", t=PACK),
            w1_raw[:].bitcast(U16).rearrange("p a (m t) -> p a t m", t=PACK),
        )
        w1_plane = tile("w1_plane", [P, 2, M], U8)
        for a in range(2):
            nc.gpsimd.tensor_copy(
                w1_plane[:, a, :].rearrange("p (t m) -> p t m", t=PACK),
                w1_plane_raw[:, a, :].rearrange("p (m t) -> p t m", t=PACK),
            )
        new_page()
        v_codes = [[pick_words(a, cols(0))[:]] for a in range(2)]
        for a in range(2):
            rest = pick_words(a, cols(1, PIECES - 1))
            v_codes[a].extend(rest[:, span] for span in later)

        def first_pass(dst, a, j, t, span, start, stop):
            nc.tensor.matmul_mx(
                out=dst,
                lhsT=w1_codes[:, a, 64 * t : 64 * t + 64].bitcast(FP4X4),
                lhsT_scale=w1_plane[:, a, 128 * t : 128 * t + 128],
                rhs=v_codes[a][j][:, span].bitcast(FP8X4),
                rhs_scale=v_plane[a][j][:, span],
                start=start,
                stop=stop,
            )

        def round_w2(raw, grouped, t0):
            nc.scalar.copy(
                grouped.rearrange("p t m j -> p m j t"),
                raw.rearrange("p j (m t) -> p m j t", t=PACK)[:, :, :, t0 : t0 + 2],
            )

        e_codes = [tile("e_codes0", [P, PIECE], U32)]
        e_plane = tile("e_plane", [P, S], U8)
        w2_codes = [tile("w2_codes0", [P, 256], U32)]
        w2_plane = [tile(f"w2_plane{a}", [P, 512], U8) for a in range(2)]
        halves = [slice(0, HALF), slice(HALF, PIECE)]
        sums = [(half, t, bank(PACK * half + t, [P, HALF])) for half in range(2) for t in range(PACK)]
        for half, t, pre in sums:
            first_pass(pre[:], 0, 0, t, halves[half], True, False)
        th0 = [tile(f"th0{half}", [P, HALF // 4, PACK, 4], F32) for half in range(2)]
        for half, t, pre in sums:
            first_pass(pre[:], 1, 0, t, halves[half], False, True)
            nc.scalar.activation(th0[half][:, :, t, :], pre[:].rearrange("p (c i) -> p c i", i=4), ACT.Tanh, bias=b1_sb[:, t : t + 1])
        w2_front = [tile(f"w2_front{u}", [P, 2, 128, PACK], BF16) for u in range(2)]
        for u in range(2):
            round_w2(w2_early[:], w2_front[u][:], 2 * u)
        e_first = [tile(f"e_first{half}", [P, HALF, PACK], BF16) for half in range(2)]
        for half in range(2):
            nc.vector.tensor_tensor(
                word_order(e_first[half][:]),
                th0[half][:],
                gain_sb[:].unsqueeze(1).unsqueeze(3).to_broadcast([P, HALF // 4, PACK, 4]),
                ALU.mult,
            )
        for half in range(2):
            span = slice(HALF * half, HALF * half + HALF)
            quantize(e_codes[0][:, span], e_plane[:, span], e_first[half][:].rearrange("p n t -> p (n t)"))
        quantize(w2_codes[0][:], w2_plane[0][:, 0:256], w2_front[0][:].rearrange("p t m j -> p (t m j)"))

        def squash(j, th, banks, share):
            width = parts[j].stop - parts[j].start
            for n, number in enumerate(banks):
                pre = bank(number, [P, share, width])
                for a in range(2):
                    for u in range(share):
                        first_pass(pre[:, u, :], a, j, share * n + u, slice(0, width), (a, u) == (0, 0), (a, u) == (1, share - 1))
                for u in range(share):
                    t = share * n + u
                    nc.scalar.activation(th[:, t, :], pre[:, u, :], ACT.Tanh, bias=b1_sb[:, t : t + 1])

        def features(j, th, rows_after, codes_after):
            width = parts[j].stop - parts[j].start
            e_rows = tile(f"e_rows{j}", [P, PACK, width], BF16, rows_after)
            for t in range(PACK):
                nc.scalar.activation(e_rows[:, t, :], th[:, t, :], ACT.Copy, scale=gain_sb[:, t : t + 1])
            e_grouped = tile(f"e_grouped{j}", [P, width, PACK], BF16)
            nc.scalar.copy(word_order(e_grouped[:]), row_order(e_rows[:]))
            e_codes.append(tile(f"e_codes{j}", [P, width], U32, codes_after))
            quantize(e_codes[j][:], e_plane[:, parts[j]], e_grouped[:].rearrange("p n t -> p (n t)"))

        def w2_slot(a, t):
            if a == 0:
                return w2_codes[t // 2][:, 128 * (t % 2) : 128 * (t % 2) + 128]
            return w2_codes[2][:, 128 * t : 128 * t + 128]

        def costs(name, a, terms, number, after=None):
            widths = [parts[j].stop - parts[j].start for t, j in terms]
            h = tile(name, [P, sum(widths)], F32, after)
            fill(h[:], a, terms, number)
            return h

        def fill(h, a, terms, number):
            widths = [parts[j].stop - parts[j].start for t, j in terms]
            acc = bank(number, [P, sum(widths)])
            for u, (t, j) in enumerate(terms):
                nc.tensor.matmul_mx(
                    out=acc[:, sum(widths[:u]) : sum(widths[: u + 1])],
                    lhsT=w2_slot(a, t).bitcast(FP8X4),
                    lhsT_scale=w2_plane[a][:, 128 * t : 128 * t + 128],
                    rhs=e_codes[j][:].bitcast(FP8X4),
                    rhs_scale=e_plane[:, parts[j]],
                    start=True,
                    stop=True,
                )
            nc.scalar.copy(h, acc[:])

        def put(a, t, span, values):
            page = pages[PACK * a + t]
            nc.vector.tensor_tensor(page[:].indirect(idx2[:, entries(span)]), values, wgs_sb[:, t, span], ALU.mult)

        h = costs("cost00", 0, [(0, 0)], 4)
        w2_codes.append(tile("w2_codes1", [P, 256], U32, "tab1"))
        quantize(w2_codes[1][:], w2_plane[0][:, 256:512], w2_front[1][:].rearrange("p t m j -> p (t m j)"))
        new_page()
        put(0, 0, parts[0], h[:])
        put(0, 1, parts[0], costs("cost01", 0, [(1, 0)], 5)[:])
        w2_back = tile("w2_back", [P, PACK, 128, PACK], BF16)
        for u in range(2):
            round_w2(w2_late[:], w2_back[:, 2 * u : 2 * u + 2, :, :], 2 * u)
        w2_codes.append(tile("w2_codes2", [P, 512], U32))
        quantize(w2_codes[2][:], w2_plane[1][:], w2_back[:].rearrange("p t m j -> p (t m j)"))
        new_page()
        for n in range(2, 2 * PACK - 2):
            put(n // PACK, n % PACK, parts[0], costs(f"cost0{n}", n // PACK, [(n % PACK, 0)], (4 + n) % 8)[:])
            if n == 3:
                new_page()
        th = tile("th1", [P, PACK, PIECE], F32)
        squash(1, th, (4, 5), 2)
        features(1, th, None, "cost04")
        new_page()
        put(1, 2, parts[0], costs("cost06", 1, [(2, 0)], 7, "e_rows1")[:])

        for n in range(2 * PACK - 2):
            put(n // PACK, n % PACK, parts[1], costs(f"cost1{n}", n // PACK, [(n % PACK, 1)], 2 + n % 6)[:])
        w3_plane = tile("w3_plane", [P, 2, N], U8, "cost11")
        nc.gpsimd.memset(w3_plane[:].rearrange("p a c -> p (a c)").bitcast(I32), 0)
        load_scale_rows(w3_plane, w3_scales)
        w3_codes = tile("w3_codes", [P, 2, N], I32, "shifted_rest")
        nc.sync.dma_start(w3_codes[:], w3_words.rearrange("a p c i -> p a (c i)").bitcast(I32))
        th = tile("th2", [P, PACK, 2 * PIECE], F32)
        squash(2, th, (0, 1, 0, 1), 1)
        features(2, th, "cost10", "cost14")
        put(1, 2, parts[1], costs("cost16", 1, [(2, 1)], 3, "cost10")[:])

        distance = tile("distance", [P, P], F32, "cost12")
        nc.gpsimd.iota(distance[:], [[1, P]], base=0, channel_multiplier=-1, allow_small_or_imprecise_dtypes=True)
        nc.scalar.activation(distance[:], distance[:], ACT.Abs)
        ident = tile("ident", [P, P], F32)
        ident_bf = tile("ident_bf", [P, P], BF16)
        for unit in (ident, ident_bf):
            nc.scalar.activation(unit[:], distance[:], ACT.Relu, scale=-1.0, bias=1.0)

        late = parts[2]
        cap_rows = cap.rearrange("(a p t) m -> a p t m", a=2, t=PACK)
        both = [tile(f"both{t}", [P, 2, PICKS], F32) for t in range(PACK)]
        for t in range(PACK):
            nc.sync.dma_start(both[t][:, 1, :], cap_rows[0][:, t, :])

        def negate(t):
            nc.scalar.activation(both[t][:, 1, :], both[t][:, 1, :], ACT.Copy, scale=-1.0)

        runs = [[0], [1], [2], [3], [4, 5, 6]]
        rest = [tile(f"rest{n}", [P, len(run), 2 * PIECE], F32) for n, run in enumerate(runs)]
        for n, run in enumerate(runs):
            for u, k in enumerate(run):
                fill(rest[n][:, u, :], k // PACK, [(k % PACK, 2)], (4 + k) % 8)
            if n == 1:
                negate(0)
        early = costs("early", 1, [(3, 0), (3, 1)], 2)
        z0_rows = [tile(f"z0_rows{half}", [P, PACK, 2 * PIECE], BF16) for half in range(2)]
        weighted = {}
        shares = {}

        def weigh(n):
            run = runs[n]
            products = tile(f"weighted{n}", [P, len(run), 2 * PIECE], F32, f"rest{n - 1}")
            nc.gpsimd.tensor_tensor(products[:], rest[n][:], wgs_sb[:, run[0] % PACK : run[-1] % PACK + 1, late], ALU.mult)
            for u, k in enumerate(run):
                weighted[k] = products[:, u, :]

        def place(k):
            span = late if k < 2 * PACK - 1 else cols(0, 1)
            nc.vector.tensor_copy(pages[k][:].indirect(idx2[:, entries(span)]), weighted[k])

        def add_turned(t, half, number):
            acc = bank(number, [P, 4, P])
            for j in range(4):
                block = slice(P * (4 * half + j), P * (4 * half + j + 1))
                for side in (1, 0):
                    nc.tensor.matmul(acc[:, j, :], both[t][:, side, block], ident[:], start=side == 1, stop=side == 0, is_transpose=True)
            return acc

        def compare(t):
            nc.vector.tensor_copy(both[t][:, 0, :], pages[t][:].indirect(idx3[:]))
            signs = tile(f"signs{t}", [P, 8, P], BF16, f"signs{t % 2}")
            shares[t] = tile(f"shares{t}", [P, 2, PICKS], F32, f"page{t % 2}")
            for half in range(2):
                nc.scalar.activation(signs[:, 4 * half : 4 * half + 4, :], add_turned(t, half, (2 * t + half) % 3)[:], ACT.Sign)
            for half in range(2):
                back = bank(3 if half else (2 * t + 2) % 3, [P, 4 * P], BF16)
                for j in range(4):
                    nc.tensor.transpose(back[:, P * j : P * (j + 1)], signs[:, 4 * half + j, :], ident_bf[:])
                span = cols(2 * half, 2 * half + 1)
                nc.scalar.activation(shares[t][:, 0, span], back[:], ACT.Copy, scale=-0.5, bias=0.5)
                nc.scalar.activation(shares[t][:, 1, span], back[:], ACT.Copy, scale=-0.5, bias=-0.5)

        def choose(t):
            nc.gpsimd.tensor_tensor(both[t][:], both[t][:], shares[t][:], ALU.mult)

        def join(t):
            for half in range(2):
                span = cols(2 * half, 2 * half + 1)
                nc.gpsimd.tensor_tensor(z0_rows[half][:, t, :], both[t][:, 0, span], both[t][:, 1, span], ALU.add)

        def join_turned(t):
            turned = tile(f"turned{t}", [P, 8, P], BF16)
            for half in range(2):
                nc.scalar.copy(turned[:, 4 * half : 4 * half + 4, :], add_turned(t, half, 2 * (t - 1) + half)[:])
            back = bank(3 + t, [P, PICKS], BF16)
            for j in range(8):
                nc.tensor.transpose(back[:, P * j : P * (j + 1)], turned[:, j, :], ident_bf[:])
            for half in range(2):
                nc.scalar.copy(z0_rows[half][:, t, :], back[:, cols(2 * half, 2 * half + 1)])

        put(0, 0, late, rest[0][:, 0, :])
        for n in range(1, len(runs)):
            weigh(n)
        weighted[2 * PACK - 1] = tile("weighted_early", [P, 2 * PIECE], F32, "rest4")[:]
        nc.gpsimd.tensor_tensor(weighted[2 * PACK - 1], early[:], wgs_sb[:, PACK - 1, cols(0, 1)], ALU.mult)
        compare(0)
        for t in range(1, PACK):
            negate(t)
            place(t)
            compare(t)
            choose(t - 1)
            if t == 2:
                join(0)
        cap1 = tile("cap1", [P, PACK, PICKS], F32)
        nc.sync.dma_start(cap1[:], cap_rows[1])
        x_upper = tile("x_upper", [P, PACK, PICKS], F32)
        for k in range(PACK, 2 * PACK - 1):
            place(k)
            nc.vector.tensor_copy(x_upper[:, k - PACK, :], pages[k][:].indirect(idx3[:]))
        place(2 * PACK - 1)
        join_turned(1)
        join_turned(2)
        choose(3)
        join(3)

        z0 = [tile(f"z0_{half}", [P, 2 * PIECE, PACK], BF16) for half in range(2)]
        for n in range(PIECES):
            nc.scalar.copy(word_order(z0[n // 2][:, cols(n % 2), :]), row_order(z0_rows[n // 2][:, :, cols(n % 2)]))
            if n == 1:
                closing = costs("closing", 1, [(3, 2)], 7, "z0_rows0")
        out_rows = out.rearrange("(c p) m -> p c m", p=P)
        last = PIECES - 1
        spans = [cols(j) for j in range(last)] + [slice(768, 896), slice(896, 1024)]
        score_banks = [(0, 1), (2, 3), (4, 5), (6, 7), (0, 1, 2, 3)]
        z_plane = [tile(f"z_plane{a}", [P, PICKS], U8) for a in range(2)]
        z_codes = {}
        opened = {}

        def quantize_z(a, pieces, grouped, after=None):
            span = slice(spans[pieces[0]].start, spans[pieces[-1]].stop)
            codes = tile(f"z_codes{a}{pieces[0]}", [P, span.stop - span.start], U32, after)
            quantize(codes[:], z_plane[a][:, span], grouped.rearrange("p n t -> p (n t)"))
            for n in pieces:
                z_codes[a, n] = codes[:, spans[n].start - span.start : spans[n].stop - span.start]

        def score_pass(a, n):
            span = spans[n]
            share = 4 // len(score_banks[n])
            if a == 0:
                opened[n] = [bank(number, [P, share, span.stop - span.start]) for number in score_banks[n]]
            for c in range(4):
                nc.tensor.matmul_mx(
                    out=opened[n][c // share][:, c % share, :],
                    lhsT=w3_codes[:, a, 128 * c : 128 * c + 128].bitcast(FP8X4),
                    lhsT_scale=w3_plane[:, a, 128 * c : 128 * c + 128],
                    rhs=z_codes[a, n].bitcast(FP8X4),
                    rhs_scale=z_plane[a][:, span],
                    start=(a == 0 and c % share == 0),
                    stop=(a == 1 and c % share == share - 1),
                )

        def finish(n, grouped):
            quantize_z(1, [n], grouped[:])
            score_pass(1, n)

        def store(n):
            span = spans[n]
            for pair in range(2):
                staged = tile(f"staged{n}{pair}", [P, 2, span.stop - span.start], F32)
                nc.scalar.copy(staged[:], opened[n][pair][:])
                nc.sync.dma_start(out_rows[:, 2 * pair : 2 * pair + 2, span], staged[:])

        def limit(n):
            span = spans[n]
            grouped = tile(f"z1_{n}", [P, span.stop - span.start, PACK], BF16)
            nc.vector.tensor_tensor(word_order(grouped[:]), row_order(x_upper[:, :, span]), row_order(cap1[:, :, span]), ALU.min)
            return grouped

        def fetch(n):
            nc.vector.tensor_copy(x_upper[:, PACK - 1, spans[n]], pages[2 * PACK - 1][:].indirect(idx3[:, entries(spans[n])]))

        quantize_z(0, [0, 1], z0[0][:])
        put(1, 3, late, closing[:])
        score_pass(0, 0)
        score_pass(0, 1)
        fetch(0)
        quantize_z(0, [2, 3, 4], z0[1][:], "z0_rows0")
        score_pass(0, 2)
        score_pass(0, 3)
        for n in range(PIECES):
            grouped = limit(n)
            fetch(n + 1)
            finish(n, grouped)
            store(n)
            if n == 1:
                score_pass(0, PIECES)
        finish(PIECES, limit(PIECES))
        for pair in range(2):
            staged = tile(f"staged4{pair}", [P, 2, HALF], F32)
            nc.vector.tensor_copy(staged[:, 0, :], opened[PIECES][2 * pair][:, 0, :])
            nc.scalar.copy(staged[:, 1, :], opened[PIECES][2 * pair + 1][:, 0, :])
            nc.sync.dma_start(out_rows[:, 2 * pair : 2 * pair + 2, spans[PIECES]], staged[:])
